import numpy as np, ml_dtypes
CORES = [23,119,17,113]
N = 4
BF = ml_dtypes.bfloat16
def gentries(a):
    return np.ascontiguousarray(a.reshape(8, 16, -1).transpose(0, 2, 1)).reshape(8, -1)
def gtable(e):
    e = np.asarray(e); return np.ascontiguousarray(e.reshape(8, -1, 16).transpose(0, 2, 1)).reshape(128, -1).astype(np.int32)
W0, P, S, R, A, W = 2560, 256, 2, 6, 512, 4096
WT = [1, 64, 5, 83, 17, 131, 29, 211, 43, 157, 61, 239, 71, 113, 97, 199]
def parts(rng):
    x = rng.integers(0, 64, (N, 8, 16, W0)); rich = rng.permutation(8)[:3]; x[:, rich] = 48 + (x[:, rich] >> 2)
    fr = rng.integers(0, A, (N, 8, W0))
    hot = np.argsort(rng.random((N, 8, W0)), axis=-1)[..., :256]
    often = np.take_along_axis(hot, rng.integers(0, 256, (N, 8, A * 16)), 2).reshape(N, 8, A, 16)
    C = np.where(rng.random((N, 8, A, 16)) < 0.4, often, rng.integers(0, W0, (N, 8, A, 16)))
    return x, fr, C, rng.integers(0, 64, (N, 8, P, 16)), rng.integers(0, A, (N, 8, P))
def pack(x, fr, C, z, b):
    return {"x0": np.ascontiguousarray(x.reshape(N, 128, W0)).astype(np.float32).astype(BF), "fr0": np.ascontiguousarray(fr).astype(np.int32),
            "pl": np.ascontiguousarray(C.transpose(0, 1, 3, 2).reshape(N, 128, A)).astype(np.int32),
            "z0": np.ascontiguousarray(z.transpose(0, 1, 3, 2).reshape(N, 128, P)).astype(np.float32).astype(BF), "b0": np.stack([gtable(a) for a in b])}
def setup_inputs(rng):
    return pack(*parts(rng))
def setup_inputs_spread(rng):
    x, fr, C, z, b = parts(rng)
    x = (np.exp2(6 * rng.random((N, 8, 1, W0))) * rng.random((N, 8, 16, W0))).astype(np.int64)
    z = (np.exp2(6 * rng.random((N, 8, P, 1))) * rng.random((N, 8, P, 16))).astype(np.int64)
    fr[:, ::2] = (A * rng.random((N, 4, W0)) ** 3).astype(np.int64)
    C = (W0 * rng.random((N, 8, A, 16)) ** 2).astype(np.int64); b = (A * rng.random((N, 8, P)) ** 2).astype(np.int64)
    return pack(x, fr, C, z, b)
def setup_inputs_ends(rng):
    x, fr, C, z, b = parts(rng)
    sd = rng.integers(0, 2, (N, 8, W0)); sd[..., 0] = 0; sd[..., W0 - 1] = 1; sd[:, 7, 1] = 1; fr = sd * (A - 1)
    kd = rng.random((N, 8, 1, W0)); mix = 63 * rng.integers(0, 2, (N, 8, 16, W0))
    less = 63 - (np.arange(16)[:, None] == rng.integers(0, 16, (N, 8, 1, W0)))
    x = np.where(kd < 0.45, 63, np.where(kd < 0.6, less, np.where(kd < 0.75, 0, mix)))
    x[:, 0::2, :, 0] = 0; x[:, 0::2, :, W0 - 1] = 0; x[:, 1::2, :, 0] = 63; x[:, 1::2, :, W0 - 1] = 63
    x[:, 7, :, 1] = 63; x[:, 7, 5, 1] = 62
    ps = rng.integers(0, 2, (N, 8, A)); ps[..., 0] = 0; ps[..., A - 1] = 1; ps = ps[..., None]
    by = np.argsort(sd + 0.5 * rng.random((N, 8, W0)), axis=-1); c1 = np.sum(sd, axis=-1)[:, :, None, None]; u = rng.random((N, 8, A, 16))
    ix = np.where(ps == 1, W0 - c1 + (u * c1).astype(np.int64), (u * (W0 - c1)).astype(np.int64))
    some = np.take_along_axis(by, ix.reshape(N, 8, A * 16), 2).reshape(N, 8, A, 16)
    C = np.where(rng.random((N, 8, A, 16)) < 0.68, ps * (W0 - 1), some)
    kz = rng.random((N, 8, P, 1))
    z = np.where(kz < 0.3, 63, np.where(kz < 0.4, 0, 63 * rng.integers(0, 2, (N, 8, P, 16))))
    b = np.where(rng.random((N, 8, P)) < 0.7, (A - 1) * rng.integers(0, 2, (N, 8, P)), b)
    for a in (A - S, A - 1):
        C[:, 7, a, :15] = 1; C[:, 7, a, 15] = W0 - 1
    z[:, 7, P - 1] = 63; b[:, 7, P - 1] = A - 1
    return pack(x, fr, C, z, b)
def setup_inputs_corners(rng):
    x, fr, C, z, b = parts(rng); o = [int(v) for v in rng.permutation(8)]
    fr[:, o[0]] = (fr[:, o[0]] // N) * N + np.arange(N)[:, None]
    fr[:, o[1]] = int(rng.integers(0, A))
    g = o[2]; zz = rng.integers(0, 64, (N, P, 16)); zz[..., :2] = 0; want = S * np.arange(P)
    need = (want[None, :] - np.sum(zz * np.array(WT), axis=-1)) & (A - 1); zz[..., 0] = need & 63; zz[..., 1] = need >> 6
    x[:, g] = 0; fr[:, g, :A] = np.arange(A); C[:, g, :, 0] = np.arange(A); z[:, g] = zz; b[:, g] = want
    g = o[3]; few = np.argsort(rng.random((N, W0)), axis=-1)[:, :320]; few[:, 0] = 0; few[:, 319] = W0 - 1
    x[:, g] = 63; C[:, g] = np.take_along_axis(few, rng.integers(0, 320, (N, A * 16)), 1).reshape(N, A, 16)
    g = o[4]; C[:, g] = rng.integers(0, W0, (N, A, 1)); C[:, g, ::7] = 0; C[:, g, A - 1] = W0 - 1
    fr[:, g] = rng.integers(0, 8, (N, W0))
    g = o[5]; own = np.arange(A)[:, None] + np.zeros((1, 16), np.int64); kd = rng.integers(0, 4, (N, A, 16))
    C[:, g] = np.where(kd == 0, 0, np.where(kd == 1, W0 - 1, np.where(kd == 2, own, C[:, g])))
    x[:, g] = 63 * rng.integers(0, 2, (N, 1, W0)); b[:, g] = np.where(rng.random((N, P)) < 0.5, np.arange(P) * S, b[:, g])
    g = o[6]; z[:, g, ::2] = 0; z[:, g, 1::2] = 63; x[::2, g] = 0
    g = o[7]; bl = np.arange(P // 4); ev = (bl & 1) == 0; od = ~ev; e8 = np.arange(8); amt = 8 * rng.integers(1, 4, P // 4)
    pt = S * (4 * bl[:, None] + (e8 >> 1)[None, :]) + (e8 & 1)[None, :]
    kind = np.zeros((P // 4, 8, 4), np.int64) + np.array([1, 2, 2, 7, 5, 7, 7, 7])[None, :, None]
    kind[:, 0, 0] = 6; kind[:, 3, 0] = 6; kind[ev, 3, 1] = 3; kind[ev, 4, 0] = 6; kind[ev, 4, 1] = 3; kind[ev, 7, :3] = 3; kind[od, 6, 0] = 3
    nme = np.zeros((A, 4), np.int64); nme[pt] = pt[bl[:, None, None], kind]
    bal = np.zeros((A, 4), np.int64); bal[pt[od, 0], 0] = 2 * amt[od]; bal[pt[od, 3], 0] = amt[od]; bal[pt[od, 6], 0] = amt[od]
    pm = np.argsort(rng.random((N, W0)), axis=-1)[:, :4 * A]; rk = np.arange(N)[:, None]
    fr[rk, g, pm] = nme.reshape(-1)[None, :]; x[:, g] = 0; x[rk, g, 1, pm] = bal.reshape(-1)[None, :]
    C[:, g] = pm[:, 4 * np.arange(A)[:, None] + np.minimum(np.arange(16), 3)[None, :]]
    want = pt[:, [3, 4, 2, 0]].reshape(P); zz = rng.integers(0, 64, (N, P, 16)); zz[..., 0] = 0; zz[..., 10] = 0; zz[..., 1] = np.repeat(amt, 4)
    need = (want[None, :] - np.sum(zz * np.array(WT), axis=-1)) & (A - 1); zz[..., 10] = need // WT[10]; zz[..., 0] = need - WT[10] * zz[..., 10]
    z[:, g] = zz; b[:, g] = want
    return pack(x, fr, C, z, b)
def setup_inputs_crowd(rng):
    x, fr, C, z, b = parts(rng); o = [int(v) for v in rng.permutation(8)]
    for j in (0, 1):
        g = o[j]; one = np.argsort(rng.random((N, W0)), axis=-1)[:, :16]
        fr[:, g] = int(rng.integers(0, A)); x[:, g] = rng.integers(0, 41, (N, 16, W0)); z[:, g] = rng.integers(41, 64, (N, P, 16))
        for r in range(N):
            other = C[r, g, 0].copy(); C[r, g] = one[r]; x[r, g, :, int(one[r, int(rng.integers(0, 16))])] = 63
            if j == 1: C[r, g, S * int(rng.integers(0, P))] = other
    for j in (2, 3):
        g = o[j]; B = int(rng.integers(0, A))
        fr[:, g] = int(rng.integers(0, A)); x[:, g] = rng.integers(0, 41, (N, 16, W0)); z[:, g] = rng.integers(41, 64, (N, P, 16))
        C[:, g] = np.arange(A)[:, None] + A * (np.arange(16)[None, :] % (W0 // A)); x[:, g, :, B] = 63; b[:, g] = B
        if j == 3:
            for r in range(N): b[r, g, int(rng.integers(0, P))] = (B + 1) % A
    g = o[4]; fr[:, g] = (A - 1) * rng.integers(0, 2, (N, W0))
    pay = np.arange(A) // S; pn = np.arange(P); rk = np.arange(N)[:, None]
    for j in (5, 6):
        g = o[j]; bal = np.zeros((A, 4), np.int64)
        if j == 5:
            am = 8 * rng.integers(1, 4, P); nxt = S * ((pn + 1) % P); nme = (S * pay)[:, None] + np.zeros((1, 4), np.int64)
            nme[S * pn, 0] = nxt; nme[S * pn, 1:] = (S * pn + 1)[:, None]; bal[S * pn, 0] = am; bal[S * pn, 1:] = 2 * am[:, None]
            bal[S * pn + 1, 1:] = np.roll(am, 1)[:, None]; want = nxt + 1; z1 = 2 * am
        else:
            bl = np.arange(P // 4); ev = (bl & 1) == 0; am = 8 * rng.integers(1, 3, P // 4); p0, p1, p2, p3 = [S * (4 * bl + v) for v in range(4)]
            nme = np.repeat(np.stack([p0 + 1, p1 + 1, p2, p2 + 1], axis=1).reshape(P), S)[:, None] + np.zeros((1, 4), np.int64)
            up = np.where(ev, p2 + 2 % S, p2 + 1)
            nme[p0, 0] = p1; nme[p1 + 1, 0] = p3 + 1; nme[up, 0] = p3 + 1; nme[p3 + 1] = p1[:, None]
            bal[p0, 0] = 3 * am; bal[p1 + 1, 0] = am; bal[up, 0] = am; bal[p3 + 1, 1:] = 3 * am[:, None]
            want = np.stack([p3 + 1, p0, p0, p1 + 1], axis=1).reshape(P)
            z1 = np.stack([3 * am + np.where(ev, 0, 8), am, am * np.where(ev, 1, 2), am], axis=1).reshape(P)
        pm = np.argsort(rng.random((N, W0)), axis=-1)[:, :4 * A]
        fr[rk, g, pm] = nme.reshape(-1)[None, :]; x[:, g] = 0; x[rk, g, 1, pm] = bal.reshape(-1)[None, :]
        C[:, g] = pm[:, 4 * np.arange(A)[:, None] + np.minimum(np.arange(16), 3)[None, :]]
        zz = rng.integers(0, 64, (N, P, 16)); zz[..., 0] = 0; zz[..., 10] = 0; zz[..., 1] = z1
        need = (want[None, :] - np.sum(zz * np.array(WT), axis=-1)) & (A - 1); zz[..., 10] = need // WT[10]; zz[..., 0] = need - WT[10] * zz[..., 10]
        z[:, g] = zz; b[:, g] = want
    g = o[7]; pm = np.argsort(rng.random((N, W0)), axis=-1)[:, :2 * A]
    nme = np.zeros((A, 2), np.int64); nme[:, 0] = 1; nme[S * pn, 0] = 0; nme[:, 1] = A - 1
    fr[rk, g, pm] = nme.reshape(-1)[None, :]
    for r in range(N):
        x[r, g] = 63 * rng.integers(0, 2, (1, W0)); x[r, g][:, pm[r, 0::2]] = 63; x[r, g][:, pm[r, 1::2]] = 0
    C[:, g] = pm[:, 2 * np.arange(A)[:, None] + (np.arange(16) == 15).astype(np.int64)[None, :]]
    z[:, g] = 63; b[:, g] = S * pn + 1
    return pack(x, fr, C, z, b)
def setup_inputs_ties(rng):
    x, fr, C, z, b = parts(rng)
    x = rng.integers(2, 5, (N, 8, 1, W0)) + np.zeros((1, 1, 16, 1), np.int64); z = rng.integers(2, 4, (N, 8, P, 16)); z[:, :, ::3] = 3
    fr[:, ::2] = rng.integers(0, 24, (N, 4, W0))
    return pack(x, fr, C, z, b)
def check_inputs(d):
    bad = []
    for k, lo, hi in (("x0", 0, 63), ("fr0", 0, A - 1), ("pl", 0, W0 - 1), ("z0", 0, 63), ("b0", 0, A - 1)):
        a = np.asarray(d[k]).astype(np.float64)
        if not (np.min(a) >= lo and np.max(a) <= hi): bad.append("range of " + k)
        elif not np.all(a == np.floor(a)): bad.append("whole numbers in " + k)
    return bad
def first(key):
    ok = np.zeros(len(key), bool); ok[np.unique(key, return_index=True)[1]] = True
    return ok
def reference(x0, fr0, pl, z0, b0):
    X = np.zeros((N, 8, W, 16), np.int32); X[:, :, :W0] = x0.astype(np.float32).astype(np.int32).reshape(N, 8, 16, W0).transpose(0, 1, 3, 2)
    nm = np.zeros((N, 8, W), np.int64); nm[:, :, :W0] = fr0
    sup = np.zeros((N, 8, 2, R * P), np.int64)
    C = np.ascontiguousarray(pl.astype(np.int64).reshape(N, 8, 16, A).transpose(0, 1, 3, 2))
    z = np.ascontiguousarray(z0.astype(np.float32).astype(np.int32).reshape(N, 8, 16, P).transpose(0, 1, 3, 2))
    b = np.stack([gentries(a) for a in b0]).astype(np.int64)
    g2 = np.arange(8)[:, None]; g3 = g2[:, :, None]; pi = np.arange(P)[None, :]; wt = np.array(WT)
    for t in range(R):
        s = t % S; base = X.copy(); took = np.zeros_like(X); back = np.zeros_like(X); D = C.copy(); made = []
        for r in range(N):
            q = (r + 1 + s) % N
            La = C[r][:, s::S]; Ma = C[q][g2, b[r]]
            y = X[r][g3, La]; h = X[q][g3, Ma]
            fk = np.add.reduce(np.minimum(y, z[r][:, :, None, :]), axis=3); hl = np.add.reduce(np.minimum(h, z[r][:, :, None, :]), axis=3)
            fits = nm[r][g3, La][:, :, :, None] == nm[q][g3, Ma][:, :, None, :]
            score = np.where(fits, fk[:, :, :, None] + hl[:, :, None, :], -1).reshape(8, P, 256)
            best = np.argmax(score, axis=2); found = np.max(score, axis=2) >= 0
            k = np.where(found, best >> 4, np.argmin(fk, axis=2)); l = best & 15
            c = La[g2, pi, k]; m = Ma[g2, pi, l]; yk = y[g2, pi, k]
            v = np.minimum(np.minimum(yk, z[r]), h[g2, pi, l])
            gb, ib = np.nonzero(found)
            ok = first(gb * W + c[gb, ib]); gb, ib = gb[ok], ib[ok]
            ok = first(gb * W + m[gb, ib]); gb, ib = gb[ok], ib[ok]
            j = P * t + ib; cb, mb, vb = c[gb, ib], m[gb, ib], v[gb, ib]
            took[r, gb, cb] += vb; took[q, gb, mb] += vb
            made.append((r, gb, W0 + j, vb)); nm[r, gb, W0 + j] = b[r][gb, ib]
            sup[r, gb, 0, j] = cb; sup[r, gb, 1, j] = mb; D[r, gb, S * ib + s, k[gb, ib]] = W0 + j
            gc, ic = np.nonzero(~found & (c >= W0)); n = c[gc, ic] - W0; w = yk[gc, ic]
            base[r, gc, W0 + n] = 0
            np.add.at(back[r], (gc, sup[r, gc, 0, n]), w); np.add.at(back[q], (gc, sup[r, gc, 1, n]), w)
            D[r, gc, S * ic + s, k[gc, ic]] = sup[r, gc, 0, n]
            if t < R - 1:
                z[r] = np.abs(z[r] - yk); b[r] = np.add.reduce(z[r] * wt, axis=2) & (A - 1)
        X = np.minimum(63, np.maximum(base - took, 0) + back); C = D
        for r, gb, n, vb in made: X[r, gb, n] = vb
    rec = np.concatenate([nm[:, :, W0:], sup[:, :, 0], sup[:, :, 1]], axis=1)
    return {"xo": np.ascontiguousarray(X.transpose(0, 1, 3, 2)).reshape(N, 128, W).astype(np.float32).astype(BF),
            "co": np.ascontiguousarray(C.transpose(0, 1, 3, 2)).reshape(N, 128, A).astype(np.float32), "rec": rec.astype(np.float32)}

@@ -1,0 +1,684 @@
+from concourse.bass import DstId, RemoteDMATransfer
+from concourse.mybir import AluOpType, ActivationFunctionType, AxisListType
+
+ALU, ACT = AluOpType, ActivationFunctionType
+
+N = 4
+W0, P, R, A = 2560, 256, 6, 512
+WT = [1, 64, 5, 83, 17, 131, 29, 211, 43, 157, 61, 239, 71, 113, 97, 199]
+KR = 8
+ORDER = "y0 d0 n0 r0 h0 p0 y1 m0 s0 P0 h1 d1 e0 E0 o0 r1 m1 p1 g0 b0 s1 B0 t0 P1 e1 o1 E1 l0 g1 f0 b1 B1"
+NA = 7
+MAGIC = 1.5 * 2 ** 23
+XO = 256
+NCH = 2
+CW = 4096 // NCH
+
+F, B, I32, U16 = "float32", "bfloat16", "int32", "uint16"
+SCRATCH = {
+    "sti": ("dram", [N, 128, 172], I32), "lni": ("dram", [N, 128, 172], I32),
+    "stb": ("dram", [N, 128, 704], B), "lnb": ("dram", [N, 128, 704], B),
+    "stf": ("dram", [N, 128, 200], F), "lnf": ("dram", [N, 128, 200], F),
+    "X": ("sbuf", [128, XO + 4096], B), "y": ("sbuf", [128, 4096], B), "mh": ("sbuf", [128, 4096], B),
+    "my": ("sbuf", [128, 4096], B), "zrep": ("sbuf", [128, 4096], B), "zf": ("sbuf", [128, 256], B),
+    "crs": ("sbuf", [128, 256], F), "mrs": ("sbuf", [128, 256], F), "ad": ("sbuf", [128, 2048], B), "eqa": ("sbuf", [128, 2048], B),
+    "od16": ("sbuf", [128, 256], B), "in32": ("sbuf", [128, 128], F),
+    "Eb": ("sbuf", [128, 4352], F), "d0": ("sbuf", [128, 1280], F), "am": ("sbuf", [128, 64], F), "So": ("sbuf", [128, 4352], F),
+    "selm": ("sbuf", [128, 4096], B), "nil": ("sbuf", [128, 512], B), "eq": ("sbuf", [128, 16, 256], B),
+    "nm": ("sbuf", [128, W0], I32), "nmb": ("sbuf", [128, W0], B), "pli": ("sbuf", [128, A], I32), "plu": ("sbuf", [128, A], U16),
+    "CN": ("sbuf", [128, A], F), "Cf": ("sbuf", [128, A], F), "Nb": ("sbuf", [128, A], B),
+    "Lu": ("sbuf", [128, 2, 256], U16), "Mu": ("sbuf", [128, 256], U16), "Mf": ("sbuf", [128, 256], F), "NM": ("sbuf", [128, 256], B),
+    "Ls": ("sbuf", [128, 2, 256], F), "Us": ("sbuf", [128, 2, 256], F), "recb": ("sbuf", [128, 1536], F), "nod": ("sbuf", [128, 256], B),
+    "z": ("sbuf", [128, 2, 256], B), "bexp": ("sbuf", [128, 2, 256], B), "Gs": ("sbuf", [128, 256], F),
+    "bi": ("sbuf", [128, 16], I32), "ki": ("sbuf", [128, 16], I32), "li": ("sbuf", [128, 16], I32), "lf": ("sbuf", [128, 16], F),
+    "t1": ("sbuf", [128, 16], I32), "t2": ("sbuf", [128, 16], I32), "t3": ("sbuf", [128, 16], I32), "bl": ("sbuf", [128, 16], I32),
+    "bc": ("sbuf", [128, 16], F), "bu": ("sbuf", [128, 16], U16), "cu": ("sbuf", [128, 16], U16), "mu": ("sbuf", [128, 16], U16),
+    "cs": ("sbuf", [128, R, 16], U16), "ms": ("sbuf", [128, R, 16], U16), "ex": ("sbuf", [128, 3, 16], U16), "exi": ("sbuf", [128, 3, 16], I32),
+    "iw": ("sbuf", [128, 256], B), "inw": ("sbuf", [128, 256], B), "i8w": ("sbuf", [128, 256], B), "i4": ("sbuf", [128, 128], B),
+    "i32": ("sbuf", [128, 128], F), "bo": ("sbuf", [128, 256], B), "bo8": ("sbuf", [128, 256], B), "bo32": ("sbuf", [128, 128], F),
+    "bop": ("sbuf", [128, 256], B), "bon": ("sbuf", [128, 256], B), "bof": ("sbuf", [128, 256], B), "bow": ("sbuf", [128, 256], B),
+    "zw": ("sbuf", [128, 272], B), "zw32": ("sbuf", [128, 272], F), "od": ("sbuf", [128, 256], B), "od8": ("sbuf", [128, 256], B),
+    "dm": ("sbuf", [128, 256], B), "rs": ("sbuf", [128, 256], F), "rm": ("sbuf", [128, 256], F), "i16": ("sbuf", [128, 256], F),
+    "i256": ("sbuf", [128, 256], B), "c256": ("sbuf", [128, 256], B), "ones": ("sbuf", [128, 256], B),
+    "w1": ("sbuf", [128, 272], F), "w2": ("sbuf", [128, 272], F), "w3": ("sbuf", [128, 272], F), "col": ("sbuf", [128, 16], F),
+    "coli": ("sbuf", [128, 4], I32), "wrow": ("sbuf", [128, 32], F),
+}
+for _n in ["nek", "nel", "nfT", "foT", "yk", "hm", "v0", "nv0", "vf", "nvf", "c1s", "nbs", "sga", "sgb", "tg",
+           "wh0", "wh1", "wf0", "wf1", "uh0", "uh1", "uf0", "uf1"]:
+    SCRATCH[_n] = ("sbuf", [128, 256], B)
+for _n in ["pc", "pm", "scl", "sml", "sm2"]:
+    SCRATCH[_n] = ("sbuf", [128, 256], F)
+for _c in range(NCH):
+    SCRATCH["sto%d" % _c] = ("dram", [N, 128, CW // 4], B)
+    SCRATCH["lno%d" % _c] = ("dram", [N, 128, CW // 4], B)
+for _b in range(8):
+    SCRATCH["pb%d" % _b] = ("psum", [128, 512], F)
+SEMAPHORES = ["sV", "sA", "sT", "sG"] + ["d%d" % _i for _i in range(48)] + ["ar%d" % _i for _i in range(3 + NCH)] + ["ls%d" % _i for _i in range(3 + NCH)]
+
+
+def engine_split(core, peers, topo):
+    far = [p for p in peers if topo.chip(p) != topo.chip(core)]
+    near = [p for p in peers if p not in far]
+    out, used = {}, []
+    for grp in (far, near):
+        if not grp:
+            continue
+        free = [e for e in topo.engines(core, grp[0]) if e not in used]
+        n = 1
+        while 2 * n * len(grp) <= len(free):
+            n *= 2
+        for i, p in enumerate(grp):
+            out[p] = free[i * n:(i + 1) * n]
+            used += out[p]
+    return out
+
+
+def apart(k):
+    return (len(k) == 2 and k[0] == "b" and k[1].isdigit()) or k.rstrip("01") in (
+        "K", "KA", "So", "zrep", "zrepV", "ad", "mym", "myr", "wrow", "selm", "recb")
+
+
+def emit(g, T, ops):
+    Q = {"V": g.vector, "A": g.scalar, "T": g.tensor, "G": g, "S": g.sync}
+    lastw, readers, clock, pos, need, waits = {}, {}, {k: {} for k in Q}, {k: 0 for k in Q}, set(), []
+    done = []
+    for i, (e, fn, rd, wr, sig) in enumerate(ops):
+        deps = set()
+        for k in rd:
+            if k in lastw:
+                deps.add(lastw[k])
+        for k in wr:
+            j = lastw.get(k)
+            if j is not None and (ops[j][0] != e or ops[j][4] is not None or sig is not None or not apart(k)):
+                deps.add(j)
+            deps.update(readers.get(k, []))
+        mine = []
+        if e is not None:
+            ck = clock[e]
+            for j in sorted(deps, reverse=True):
+                src, val, know = done[j]
+                if ck.get(src, -1) >= val:
+                    continue
+                mine.append(j)
+                need.add(j)
+                for a, b in know.items():
+                    ck[a] = max(ck.get(a, -1), b)
+                ck[src] = val
+            pos[e] += 1
+        waits.append(mine)
+        done.append((e if sig is None else sig[0], pos[e] if sig is None else 0, dict(clock[e]) if e is not None else {}))
+        for k in rd:
+            readers.setdefault(k, []).append(i)
+        for k in wr:
+            lastw[k] = i
+            readers[k] = []
+    last = {}
+    for i, o in enumerate(ops):
+        if o[0] is not None and o[4] is None:
+            last[o[0]] = i
+    need |= set(last.values())
+    cnt, at = {k: 0 for k in Q}, {}
+    for i, (e, fn, rd, wr, sig) in enumerate(ops):
+        if sig is not None:
+            at[i] = sig
+        elif i in need:
+            cnt[e] += 1
+            at[i] = ("s" + e, cnt[e])
+    for i, (e, fn, rd, wr, sig) in enumerate(ops):
+        if e is None:
+            continue
+        for j in waits[i]:
+            Q[e].wait_ge(T.sem[at[j][0]], at[j][1])
+        ins = fn(Q[e])
+        if sig is not None:
+            if sig[0][0] == "d":
+                ins.then_inc(T.sem[sig[0]], 16)
+        elif i in need:
+            ins.then_inc(T.sem[at[i][0]], 1)
+    for i, o in enumerate(ops):
+        if o[4] is not None:
+            g.wait_ge(T.sem[o[4][0]], o[4][1])
+    for k in cnt:
+        if cnt[k]:
+            g.wait_ge(T.sem["s" + k], cnt[k])
+
+
+def rank_program(g, core, T, topo):
+    me = T.rank_of(core)
+    if me is None:
+        return
+    cores = list(T.cores)
+    peers = [c for c in cores if c != core]
+    mine = engine_split(core, peers, topo)
+    arrive = sum(len(engine_split(c, [x for x in cores if x != c], topo)[core]) for c in peers)
+    ops, nd, stops = [], [0], set()
+
+    def op(e, fn, rd, wr):
+        ops.append((e, fn, list(rd), list(wr), None))
+
+    def dma(e, out, in_, rd, wr):
+        ops.append((e, lambda q: q.dma_start(out, in_), list(rd), list(wr), ("d%d" % nd[0], 16)))
+        nd[0] += 1
+
+    def exchange(n, st, ln, rd, wr):
+        def fn(q):
+            tr = []
+            for c in peers:
+                rid, pid, _ = topo.addr(c)
+                tr.append(RemoteDMATransfer(dst_ids=[DstId(rid=rid, pnc=pid)], dma_engine_mask=sum(1 << e for e in mine[c]),
+                                            remote_sem=T.sem["ar%d" % n], src=st[T.rank_of(c)], dst=ln[me]))
+            return q.remote_dma_fused(tr, local_sem=T.sem["ls%d" % n])
+        ops.append(("G", fn, list(rd), [], ("ls%d" % n, sum(len(v) for v in mine.values()))))
+        ops.append((None, None, [], list(wr), ("ar%d" % n, arrive)))
+
+    def ts(out, in0, s1, o0, s2=None, o1=None, rd=(), wr=()):
+        if o1 is None:
+            op("V", lambda q: q.tensor_scalar(out, in0, s1, None, o0), rd, wr)
+        else:
+            op("V", lambda q: q.tensor_scalar(out, in0, s1, s2, o0, o1), rd, wr)
+
+    def tt(out, in0, in1, o, rd=(), wr=()):
+        op("V", lambda q: q.tensor_tensor(out, in0, in1, o), rd, wr)
+
+    def cp(out, in_, rd=(), wr=()):
+        op("V", lambda q: q.tensor_copy(out, in_), rd, wr)
+
+    def ms(ap, v, wr):
+        op("V", lambda q: q.memset(ap, v), [], wr)
+
+    def scan(out, a, b, init, o0, o1, rd=(), wr=()):
+        op("V", lambda q: q.tensor_tensor_scan(out, a, b, init, o0, o1), rd, wr)
+
+    def act(out, in_, func, bias=0.0, scale=1.0, rd=(), wr=()):
+        if func == ACT.Copy:
+            op("A", lambda q: q.activation(out, in_, func), rd, wr)
+        else:
+            op("A", lambda q: q.activation(out, in_, func, bias=bias, scale=scale), rd, wr)
+
+    def mm(out, lhsT, rhs, st, sp, rd, bank):
+        def fn(q):
+            return q.matmul(out, lhsT, rhs, st, sp or fn in stops)
+        op("T", fn, rd, [bank])
+
+    def iota(out, pat, base, cm, wr, flt=True):
+        if flt:
+            op("G", lambda q: q.iota(out, pat, base, cm, allow_small_or_imprecise_dtypes=True), [], wr)
+        else:
+            op("G", lambda q: q.iota(out, pat, base, cm), [], wr)
+
+    def sh(w, d):
+        c = 128 - 16 * (d % 8)
+        return w[:, c:c + 128]
+
+    bk = [T["pb%d" % i] for i in range(8)]
+    X, I, In, I8, I4 = T.X, T.iw[:, 128:256], T.inw[:, 128:256], T.i8w[:, 128:256], T.i4[:]
+    lo, hi = slice(0, 256), slice(256, 512)
+    H = [slice(0, 128), slice(128, 256)]
+    r32 = slice(32 * me, 32 * me + 32)
+
+    dma("S", T.sti[:, :, 0:128], T.pl[:], [], ["sti0"])
+    dma("A", T.sti[:, :, 128:168], T.fr0[:], [], ["sti1"])
+    dma("S", T.sti[:, :, 168:172], T.b0[:], [], ["sti2"])
+    dma("A", T.stb[:, :, 0:640], T.x0[:], [], ["stb0"])
+    dma("S", T.stb[:, :, 640:704], T.z0[:], [], ["stb1"])
+    dma("A", T.lni[me, :, 0:128], T.pl[r32, :], [], ["lni0"])
+    dma("S", T.lni[me, :, 128:168], T.fr0[2 * me:2 * me + 2, :], [], ["lni1"])
+    dma("A", T.lni[me, :, 168:172], T.b0[r32, :], [], ["lni2"])
+    dma("S", T.lnb[me, :, 640:704], T.z0[r32, :], [], ["lnb1"])
+    dma("A", X[r32, XO:XO + W0], T.x0[r32, :], [], ["Xown"])
+
+    iota(T.coli[:, 0:1], [[0, 1]], 0, 1, ["coli0"], False)
+    iota(T.w1[:, 0:256], [[0, 2], [1, 128]], 0, 0, ["w1"])
+    iota(T.w2[:, 0:256], [[0, 2], [1, 8], [0, 16]], 0, 0, ["w2"])
+    iota(T.i16[:], [[0, 16], [1, 16]], 0, 0, ["i16"])
+    exchange(0, T.sti, T.lni, ["sti0", "sti1", "sti2"], ["lni"])
+    exchange(1, T.stb, T.lnb, ["stb0", "stb1"], ["lnb"])
+    iota(T.w3[:], [[1, 272]], -16, 0, ["w3"])
+    iota(T.i256[:], [[1, 256]], 0, 0, ["i256"])
+    iota(T.exi[:, 0, :], [[1, 16]], 0, 0, ["exi"], False)
+    iota(T.lf[:], [[-16, 16]], 255, 0, ["lf"])
+    ms(T.nm[:], 0, ["nm0"])
+    cp(T.col[:, 0:1], T.coli[:, 0:1], ["coli0"], ["colp"])
+    ts(T.coli[:, 1:2], T.coli[:, 0:1], 4, ALU.arith_shift_right, rd=["coli0"], wr=["coli1"])
+    ts(T.coli[:, 2:3], T.coli[:, 0:1], 15, ALU.bitwise_and, rd=["coli0"], wr=["coli2"])
+    cp(T.col[:, 1:3], T.coli[:, 1:3], ["coli1", "coli2"], ["colg"])
+    cp_, cg, ce = T.col[:, 0:1], T.col[:, 1:2], T.col[:, 2:3]
+    ts(T.iw[:], T.w1[:, 0:256], cp_, ALU.is_equal, rd=["w1", "colp"], wr=["iw"])
+    ts(T.bo[:], T.w2[:, 0:256], cg, ALU.is_equal, rd=["w2", "colg"], wr=["bo"])
+    ts(T.wrow[:, 16:32], T.i16[:, 0:16], ce, ALU.is_equal, 2.0 ** 32, ALU.mult, rd=["i16", "colg"], wr=["rowm"])
+    for out, v, n in ((T.inw, -1.0, 256), (T.i8w, -8192.0, 256), (T.i4, 4096.0, 128), (T.i32, 1.0, 128), (T.in32, -1.0, 128)):
+        act(out[:, 0:n], T.iw[:, 0:n], ACT.Identity, 0.0, v, rd=["iw"], wr=["KA"])
+    for j in range(4):
+        act(T.nil[:, j:512:4], T.iw[:, 0:128], ACT.Identity, 0.0, -2.0 ** 32, rd=["iw"], wr=["KA"])
+    for out, v, n in ((T.bo8, -8192.0, 256), (T.bo32, 1.0, 128), (T.bop, 512.0, 256), (T.bon, -512.0, 256), (T.bof, 1.0 / 1024, 256)):
+        act(out[:, 0:n], T.bo[:, 0:n], ACT.Identity, 0.0, v, rd=["bo"], wr=["KA"])
+
+
+    def make_selm(s):
+        for l in range(16):
+            c = 2048 * s + 512 * (l // 4)
+            act(T.selm[:, c + l % 4:c + 512:4], sh(T.bo, -2 * (1 + s)), ACT.Identity, 0.0, T.wrow[:, 16 + l:17 + l], rd=["rowm", "bo"], wr=["selm%d" % s])
+    make_selm(0)
+    ts(T.dm[:], T.i16[:], ce, ALU.is_equal, rd=["i16", "colg"], wr=["dm"])
+    ts(T.od[:], T.i16[:], ce, ALU.not_equal, 32768.0, ALU.mult, rd=["i16", "colg"], wr=["od"])
+    ts(T.col[:, 3:4], ce, 0.0, ALU.is_equal, 1.0 / 1024, ALU.mult, rd=["colg"], wr=["col3"])
+    ts(T.col[:, 4:5], ce, 0.0, ALU.is_equal, 512.0, ALU.mult, rd=["colg"], wr=["col4"])
+    ts(T.col[:, 5:6], cg, 16.0, ALU.mult, rd=["colg"], wr=["col5"])
+    for j in range(16):
+        ms(T.wrow[:, j:j + 1], float(WT[j]), ["wrow"])
+    act(T.od8[:], T.od[:], ACT.Identity, -8192.0, rd=["od"], wr=["KA"])
+    act(T.od16[:], T.od[:], ACT.Identity, -16384.0, rd=["od"], wr=["KA"])
+    act(T.nod[:], T.od[:], ACT.Identity, 0.0, -1.0, rd=["od"], wr=["KA"])
+    act(T.c256[:], T.od[:], ACT.Identity, 256.0, 0.0, rd=["od"], wr=["KA"])
+    act(T.ones[:], T.od[:], ACT.Identity, 1.0, 0.0, rd=["od"], wr=["KA"])
+    act(X[:, 0:XO], T.od[:], ACT.Identity, 0.0, 0.0, rd=["od"], wr=["X"])
+    act(T.rs[:], T.od[:], ACT.Identity, 0.0, 0.0, rd=["od"], wr=["rs"])
+    act(T.rs[:, 0:256:16], T.od[:, 0:16], ACT.Identity, 131072.0, 0.0, rd=["od", "rs"], wr=["rs", "KA"])
+    ts(T.col[:, 6:7], T.col[:, 4:5], -256.0, ALU.add, rd=["col4"], wr=["K"])
+    tt(T.wrow[:, 0:16], T.wrow[:, 0:16], T.dm[:, 0:16], ALU.mult, ["wrow", "dm"], ["wrow"])
+    ts(T.w1[:], T.w3[:], T.col[:, 5:6], ALU.subtract, rd=["w3", "col5"], wr=["w1"])
+    op("V", lambda q: q.tensor_reduce(T.col[:, 9:10], T.wrow[:, 0:16], AxisListType.X, ALU.add), ["wrow"], ["col9"])
+    ts(T.w2[:], T.w1[:], 0.0, ALU.is_equal, rd=["w1"], wr=["w2"])
+    ts(T.w3[:], T.w1[:], 128.0, ALU.is_equal, rd=["w1"], wr=["w3"])
+    act(T.bow[:], T.bo[:], ACT.Identity, 0.0, T.col[:, 9:10], rd=["col9", "bo"], wr=["KA"])
+    tt(T.zw32[:], T.w2[:], T.w3[:], ALU.add, ["w2", "w3"], ["zw32"])
+    ms(T.rm[:], 131072.0, ["rm"])
+    act(T.zw[:], T.zw32[:], ACT.Copy, rd=["zw32"], wr=["KA"])
+    ts(T.rm[:, 0:256:16], T.lf[:], ce, ALU.subtract, rd=["rm", "lf", "colg"], wr=["rm"])
+    for s in range(2):
+        ts(T.t1[:], T.exi[:, 0, :], 8 - 2 * (1 + s), ALU.add, rd=["exi"], wr=["t1"])
+        ts(T.t2[:], T.t1[:], 7, ALU.bitwise_and, rd=["t1"], wr=["t2"])
+        ts(T.t3[:], T.exi[:, 0, :], 8, ALU.bitwise_and, rd=["exi"], wr=["t3"])
+        tt(T.exi[:, 1 + s, :], T.t2[:], T.t3[:], ALU.add, ["t2", "t3"], ["exi1"])
+    cp(T.ex[:], T.exi[:], ["exi", "exi1"], ["K"])
+    iota(T.d0[:, 0:1024], [[0, 1024]], -1, 0, ["d00", "d01"])
+    iota(T.d0[:, 1024:1280], [[0, 256]], -32, 0, ["d00", "d01"])
+    op("G", lambda q: q.iota(T.d0[:, 0:1024:512], [[0, 2]], 2 ** 23, 0, allow_small_or_imprecise_dtypes=True), ["d00"], ["d00", "d01"])
+    op("G", lambda q: q.iota(T.d0[:, 1024:1280:16], [[0, 16]], 2 ** 23, 0, allow_small_or_imprecise_dtypes=True), ["d00"], ["d00", "d01"])
+    ts(T.col[:, 7:8], T.col[:, 0:1], 1.0, ALU.mult, rd=["colp", "rm", "od", "dm", "zw32", "i256", "i16", "K"], wr=["K"])
+    K = ["K", "KA"]
+
+    dma("S", T.pli[:], T.lni[:, :, 0:128], ["lni", "lni0"], ["pli"])
+    dma("S", T.nm[0:128:16, :], T.lni[:, :, 128:168], ["lni", "lni1", "nm0"], ["nm"])
+    dma("S", T.bl[32:128, :], T.lni[0:3, :, 168:172], ["lni", "lni2"], ["bl0"])
+    dma("S", T.bl[0:32, :], T.lni[3, :, 168:172], ["lni", "lni2"], ["bl1"])
+    dma("S", T.z[:, 0, :], T.lnb[:, :, 640:704], ["lnb", "lnb1"], ["z0"])
+    dma("S", T.zf[32:128, :], T.lnb[0:3, :, 640:704], ["lnb", "lnb1"], ["zf1"])
+    dma("S", T.zf[0:32, :], T.lnb[3, :, 640:704], ["lnb", "lnb1", "zf1"], ["zf"])
+    for n, (a, b) in enumerate(((0, me), (me + 1, N))):
+        if b > a:
+            dma("S", X[32 * a:32 * b, XO:XO + W0], T.lnb[a:b, :, 0:640], ["lnb"], ["Xin%d" % n])
+
+    cp(T.plu[:], T.pli[:], ["pli"], ["plu"])
+    ts(T.nmb[:], T.nm[:], -256.0, ALU.add, T.col[:, 3:4], ALU.mult, rd=["nm", "col3"], wr=["nmb"])
+    act(T.mh[:], T.nmb[:].indirect(T.plu[:, hi]), ACT.Copy, rd=["nmb", "plu"], wr=["mh0", "mh1"])
+    MY = ["myr0", "myr1", "mym0", "mym1"]
+    ts(T.Lu[:, 0, :], T.pli[:, 0:A:2], 256.0, ALU.add, rd=["pli"], wr=["Lu0"])
+    cp(T.my[:], T.nmb[:].indirect(T.plu[:, lo]), ["nmb", "plu"], MY)
+    ts(T.Cf[:], T.pli[:], 256.0, ALU.add, rd=["pli"], wr=["Cf"])
+    for c, buf, keys in ((1, T.mh, ["mh0", "mh1"]), (0, T.my, MY)):
+        for k in range(16):
+            mm(bk[c][:, lo], T.zw[:, 16 - k:144 - k], buf[:, k:4096:16], k == 0, k == 15, keys + K, "b%d" % c)
+
+    def payee(par, keys, lst=True):
+        if lst:
+            cp(T.bu[:], T.bl[:], keys, ["bu"])
+        ts(T.bc[:], T.bl[:], -256.0, ALU.add, rd=keys, wr=["bc"])
+        tt(T.bexp[:, par, :], T.bc[:].indirect(T.ex[:, 0, :]), T.dm[:], ALU.mult, ["bc"] + K, ["bexp%d" % par])
+
+    def spread(js):
+        for j in js:
+            op("G", lambda q, j=j: q.affine_select(T.zrep[:, j:4096:16], T.zf[:], [[0, 256]], ALU.is_ge, 0.0, 0, 0), ["zf"], ["zrep"])
+
+    cp(T.bu[:], T.bl[:], ["bl0", "bl1"], ["bu"])
+    cp(T.Mu[:], T.Cf[:].indirect(T.bu[:]), ["Cf", "bu"], ["Mu"])
+    spread(range(8))
+    for j in range(8, 16):
+        cp(T.zrep[:, j:4096:16], T.zf[:], ["zf"], ["zrepV"])
+    mm(bk[7][:, lo], I, T.z[:, 0, :], True, True, ["z0"] + K, "b7")
+
+    def first_names():
+        for c in (1, 0):
+            act(T.Nb[:, 256 * c:256 * c + 256], bk[c][:, lo], ACT.Copy, wr=["b%d" % c, "Nb"])
+
+    def first_lists():
+        ts(T.bc[:], T.bl[:], -256.0, ALU.add, rd=["bl0", "bl1"], wr=["bc"])
+        ts(T.Lu[:, 1, :], T.pli[:, 1:A:2], 256.0, ALU.add, rd=["pli"], wr=["Lu1"])
+        tt(T.bexp[:, 0, :], T.bc[:].indirect(T.ex[:, 0, :]), T.dm[:], ALU.mult, ["bc"] + K, ["bexp0"])
+        for c in (1, 0):
+            sl = slice(256 * c, 256 * c + 256)
+            tt(T.CN[:, sl], T.Nb[:, sl], T.Cf[:, sl], ALU.add, ["Cf", "Nb"], ["CN"])
+
+    late, nbs_ = [first_lists], [first_names]
+    for t in range(R):
+        s, par = t % 2, t % 2
+        d = 2 * (1 + s)
+        dn = 2 * (1 + (1 - s))
+        zk, z = "z%d" % par, T.z[:, par, :]
+        wt = XO + W0 + P * t
+        win = X[:, 0:wt]
+        XK = ["X", "Xnew", "Xown", "Xin0", "Xin1"]
+        gens = [u for u in (t - 2, t - 4) if u >= 0]
+
+        def ygather(h):
+            act(T.y[:, 2048 * h:2048 * h + 2048], win.indirect(T.Lu[:, s, H[h]]), ACT.Copy, rd=XK + ["Lu%d" % s], wr=["y%d" % h])
+
+        def hgather(h):
+            tt(T.mh[:, 2048 * h:2048 * h + 2048], win.indirect(T.Mu[:, H[h]]), T.zrep[:, 2048 * h:2048 * h + 2048], ALU.min,
+               XK + ["Mu", "zrep", "zrepV"], ["mh%d" % h])
+
+        def ycol(h, k):
+            return T.y[:, 2048 * h + k:2048 * h + 2048:16]
+
+        def myk(h, k, n=1):
+            c = (16 * h + k) * 128
+            return T.my[:, c:c + 128 * n]
+
+        quads = [(k0, min(4, 16 - k0)) for k0 in range(16 - KR, 16, 4)]
+
+        def differ(h, ns=(0, 1)):
+            for n in ns:
+                if n < len(quads):
+                    b = 4 + n % 2
+                    for j in range(quads[n][1]):
+                        o = bk[b][:, 128 * j:128 * j + 128]
+                        mm(o, I, T.z[:, par, H[h]], True, False, [zk] + K, "b%d" % b)
+                        mm(o, In, ycol(h, quads[n][0] + j), False, True, ["y%d" % h] + K, "b%d" % b)
+
+        def relu_part(h):
+            for n, (k0, w) in enumerate(quads):
+                act(myk(h, k0, w), bk[4 + n % 2][:, 0:128 * w], ACT.Relu, wr=["b%d" % (4 + n % 2), "myr%d" % h])
+                differ(h, (n + 2,))
+
+        def min_part(h):
+            for k in range(16 - KR):
+                tt(myk(h, k), bk[7][:, H[h]], ycol(h, k), ALU.min, ["y%d" % h], ["b7", "mym%d" % h])
+
+        def fsum(h):
+            for k in list(range(16 - KR, 16)) + list(range(16 - KR)):
+                o = bk[6][:, 128 * h + k:128 * h + 128:16]
+                if k >= 16 - KR:
+                    mm(o, T.z[:, par, H[h]], T.bop[:, 128:256:16], True, False, [zk] + K, "b6")
+                    mm(o, myk(h, k), T.bon[:, 128:256:16], False, True, ["myr%d" % h] + K, "b6")
+                else:
+                    mm(o, myk(h, k), T.bop[:, 128:256:16], True, True, ["mym%d" % h] + K, "b6")
+
+        def fout(h):
+            act(T.Gs[:, H[h]], bk[6][:, H[h]], ACT.Identity, -29.0, wr=["b6", "Gs%d" % h])
+            if h:
+                act(T.Eb[:, 4096:4352], bk[6][:, lo], ACT.Identity, 2.0 ** 20 + 496, wr=["b6", "Ef"])
+            act(T.Gs[:, 128 * h:128 * h + 128:16], bk[6][:, 128 * h:128 * h + 128:16], ACT.Identity, 2.0 ** 23, rd=["Gs%d" % h], wr=["b6", "Gs%d" % h])
+
+        def pairs(h, b0):
+            for b in (b0, b0 + 1):
+                c0 = 2048 * s + 512 * b
+                mm(bk[b][:], T.NM[:, H[h]], T.selm[:, c0:c0 + 512], True, False, ["NM", "selm%d" % s] + K, "b%d" % b)
+                mm(bk[b][:], T.Nb[:, 256 * h + s:256 * h + 256:2], T.nil[:], False, False, ["Nb"] + K, "b%d" % b)
+                for j in range(4):
+                    mm(bk[b][:, j:512:4], T.mh[:, 2048 * h + 4 * b + j:2048 * h + 2048:16], sh(T.bon, -d), False, j == 3, ["mh%d" % h] + K, "b%d" % b)
+
+        def fold(h, b0):
+            for b in (b0, b0 + 1):
+                c = 1024 * b + 512 * h
+                act(T.Eb[:, c:c + 512], bk[b][:], ACT.Abs, 512.0 * 2016 + 454 + 4 * b, wr=["b%d" % b, "Ep%d%d" % (h, b)])
+
+        def step(h):
+            a = 128 * h
+            tt(T.d0[:, 4 * a + 4:4 * a + 512:4], T.Gs[:, a + 1:a + 128], bk[6][:, a:a + 127], ALU.subtract, ["Gs%d" % h], ["b6", "d0%d" % h])
+
+        def best(h, b0):
+            for b in (b0, b0 + 1):
+                c = 1024 * b + 512 * h
+                scan(T.So[:, c:c + 512], T.d0[:, 512 * h:512 * h + 512], T.Eb[:, c:c + 512], 0.0, ALU.add, ALU.min,
+                     ["d0%d" % h, "Ep%d%d" % (h, b)], ["So"])
+
+        def least(h):
+            scan(T.So[:, 4096:4352], T.d0[:, 1024:1280], T.Eb[:, 4096:4352], 0.0, ALU.add, ALU.min, ["Ef"], ["So"])
+
+        def names():
+            for fn in nbs_:
+                fn()
+            act(T.NM[:], T.Nb[:].indirect(T.bu[:]), ACT.Copy, rd=["Nb", "bu"], wr=["NM"])
+
+        def farlist():
+            act(T.Mf[:], T.Cf[:].indirect(T.bu[:]), ACT.Copy, rd=["Cf", "bu"], wr=["Mf"])
+
+        def tidy():
+            for fn in late:
+                fn()
+
+        steps = {"y": ygather, "h": hgather, "r": relu_part, "m": min_part, "s": fsum, "o": fout, "d": differ,
+                 "g": step, "f": least, "b": lambda h: best(h, 0), "B": lambda h: best(h, 2),
+                 "p": lambda h: pairs(h, 0), "P": lambda h: pairs(h, 2), "e": lambda h: fold(h, 0), "E": lambda h: fold(h, 2),
+                 "n": lambda h: names(), "l": lambda h: farlist(), "t": lambda h: tidy()}
+        for w in ORDER.split():
+            steps[w[0]](int(w[1]))
+
+        mm(bk[0][:, lo], T.i32[:], T.Cf[:, s:A:2], True, False, ["Cf"] + K, "b0")
+        mm(bk[1][:, lo], T.i32[:], T.Mf[:], True, False, ["Mf"] + K, "b1")
+        mm(bk[2][:, lo], In, T.od16[:], True, False, K, "b2")
+        mm(bk[3][:, lo], T.ones[0:64, 0:128], T.c256[0:64, :], True, False, K, "b3")
+        mm(bk[5][:, lo], In, T.od8[:], True, False, K, "b5")
+        tt(T.am[:, 0:32], T.So[:, 63:2048:64], T.So[:, 2111:4096:64], ALU.min, ["So"], ["am0"])
+        tt(T.am[:, 32:48], T.am[:, 0:16], T.am[:, 16:32], ALU.min, ["am0"], ["am1"])
+        tt(T.am[:, 48:64], T.am[:, 32:48], T.Gs[:, 15:256:16], ALU.subtract, ["am1", "Gs0", "Gs1"], ["am2"])
+        tt(T.bi[:], T.am[:, 48:64], T.So[:, 4111:4352:16], ALU.min, ["am2"], ["bi"])
+        ts(T.li[:], T.bi[:], 31, ALU.bitwise_and, rd=["bi"], wr=["li"])
+        ts(T.ki[:], T.bi[:], 5, ALU.arith_shift_right, 15, ALU.bitwise_and, rd=["bi"], wr=["ki"])
+        cp(T.lf[:], T.li[:], ["li"], ["lf"])
+        tt(T.nek[:], T.ki[:].indirect(T.ex[:, 0, :]), T.i16[:], ALU.not_equal, ["ki"] + K, ["nek"])
+        act(T.nfT[:], T.lf[:].indirect(T.ex[:, 0, :]), ACT.Relu, -30.0, 2.0, rd=["lf"] + K, wr=["nfT"])
+        tt(T.nel[:], T.li[:].indirect(T.ex[:, 1 + s, :]), T.i16[:], ALU.not_equal, ["li"] + K, ["nel"])
+
+        def turned(bank, c0, src, key, w, stop):
+            for h in range(2):
+                mm(bk[bank][:, c0 + 128 * h:c0 + 128 * h + 128], src[:, H[h]], w, False, stop and h == 1, [key] + K, "b%d" % bank)
+
+        turned(0, 0, T.nek, "nek", I8, True)
+        act(T.pc[:], bk[0][:, lo], ACT.Relu, wr=["b0", "pc"])
+        if gens:
+            act(T.foT[:], T.lf[:].indirect(T.ex[:, 0, :]), ACT.Relu, 16.0, -1.0, rd=["lf"] + K, wr=["foT"])
+        turned(1, 0, T.nel, "nel", I8, True)
+        ts(T.pm[:], bk[1][:, lo], 0.0, ALU.max, wr=["b1", "pm"])
+        mm(bk[2][:, lo], T.bo32[:], T.pc[:], False, False, ["pc"] + K, "b2")
+        turned(2, 0, T.nfT, "nfT", I8, True)
+        mm(bk[3][:, lo], T.bo32[:], T.pc[:], False, False, ["pc"] + K, "b3")
+        turned(3, 0, T.nfT, "nfT", I8, True)
+        mm(bk[5][:, lo], T.bo32[:], T.pm[:], False, True, ["pm"] + K, "b5")
+        mm(bk[1][:, lo], In, T.od8[:], True, False, K, "b1")
+        mm(bk[1][:, lo], T.bo32[:], T.pm[:], False, False, ["pm"] + K, "b1")
+        scan(T.scl[:], T.rm[:], bk[2][:, lo], 131072.0, ALU.min, ALU.max, K, ["b2", "scl"])
+        cp(T.t1[:], T.scl[:, 15:256:16], ["scl"], ["t1"])
+        ts(T.t2[:], T.t1[:], 8191, ALU.bitwise_and, rd=["t1"], wr=["t2"])
+        tt(T.eq[:, 15, :], bk[3][:, lo], T.scl[:], ALU.is_equal, ["scl"], ["b3", "eq15"])
+        act(T.crs[:], bk[3][:, lo], ACT.Copy, wr=["b3", "crs"])
+        cp(T.cu[:], T.t2[:], ["t2"], ["cu"])
+        act(T.yk[:], win.indirect(T.cu[:]), ACT.Copy, rd=XK + ["cu"], wr=["yk"])
+        scan(T.sml[:], T.rm[:], bk[5][:, lo], 131072.0, ALU.min, ALU.max, K, ["b5", "sml"])
+
+        def equal_rows(bank, rep, lst, outs, extra):
+            segs, o = [], 0
+            for j in range(15 - NA, 15):
+                c = 16 * j + 16
+                act(T.ad[:, o:o + 256 - c], T[rep][:, c:256], ACT.Abs, T[lst][:, c - 1:c], -1.0, rd=[rep, lst], wr=["ad"])
+                segs.append((c, o))
+                o += 256 - c
+            if NA:
+                act(T.eqa[:, 0:o], T.ad[:, 0:o], ACT.Relu, 1.0, -1.0, rd=["ad"], wr=["eqa"])
+            for j in range(15 - NA):
+                c = 16 * j + 16
+                ts(T.eq[:, j, c:256], bk[bank][:, c:256], T[lst][:, c - 1:c], ALU.is_equal, rd=[lst], wr=["b%d" % bank, "eq%d" % j])
+                for b, c0, w in outs:
+                    mm(bk[b][:, c0 + c:c0 + 256], w, T.eq[:, j, c:256], False, False, ["eq%d" % j] + K, "b%d" % b)
+                if j == 12 - NA:
+                    for b, c0, w in outs:
+                        for c, o in segs:
+                            mm(bk[b][:, c0 + c:c0 + 256], w, T.eqa[:, o:o + 256 - c], False, False, ["eqa"] + K, "b%d" % b)
+                if j in extra:
+                    extra[j]()
+            for b, c0, w in outs:
+                last = ops[max(i for i, x in enumerate(ops) if x[0] == "T" and x[3] == ["b%d" % b])]
+                stops.add(last[1])
+
+        zn, znk = T.z[:, 1 - par, :], "z%d" % (1 - par)
+
+        def amounts():
+            ts(T.mu[:], T.sml[:, 15:256:16], -8192.0, ALU.add, rd=["sml"], wr=["mu"])
+            act(T.hm[:], win.indirect(T.mu[:]), ACT.Copy, rd=XK + ["mu"], wr=["hm"])
+            mm(bk[4][:, lo], T.bo32[:], T.pm[:], True, True, ["pm"] + K, "b4")
+            act(T.mrs[:], bk[4][:, lo], ACT.Copy, wr=["b4", "mrs"])
+
+        def relist():
+            mm(bk[2][:, hi], In, T.od8[:], True, False, K, "b2")
+            turned(2, 256, T.nfT, "nfT", I8, False)
+            mm(bk[2][:, hi], T.bo32[:], T.pc[:], False, False, ["pc"] + K, "b2")
+
+        def relist2():
+            mm(bk[5][:, hi], In, T.od[:], True, False, K, "b5")
+            mm(bk[5][:, hi], T.bo32[:], T.pm[:], False, False, ["pm"] + K, "b5")
+
+        def newz():
+            if t < R - 1:
+                mm(bk[7][:, hi], sh(T.iw, dn), z, True, False, [zk] + K, "b7")
+                mm(bk[7][:, hi], sh(T.inw, dn), T.yk[:], False, True, ["yk"] + K, "b7")
+                mm(bk[6][:, lo], I, z, True, False, [zk] + K, "b6")
+                mm(bk[6][:, lo], In, T.yk[:], False, True, ["yk"] + K, "b6")
+                act(T.zf[:], bk[7][:, hi], ACT.Abs, wr=["b7", "zf"])
+                spread(range(16))
+                act(zn, bk[6][:, lo], ACT.Abs, wr=["b6", znk])
+
+        mm(bk[1][:, lo], sh(T.bo8, d), T.eq[:, 15, :], False, False, ["eq15"] + K, "b1")
+        equal_rows(3, "crs", "scl", [(1, 0, sh(T.bo8, d))], {0: amounts, 1: newz})
+        mm(bk[0][:, hi], sh(T.iw, -d), T.hm[:], True, True, ["hm"] + K, "b0")
+        relist()
+        tt(T.tg[:], win.indirect(T.cu[:]), z, ALU.min, XK + ["cu", zk], ["tg"])
+        scan(T.sm2[:], T.rm[:], bk[1][:, lo], 131072.0, ALU.min, ALU.max, K, ["b1", "sm2"])
+        tt(T.c1s[:], bk[1][:, lo], T.nod[:], ALU.is_lt, K, ["b1", "c1s"])
+        tt(T.eq[:, 15, :], bk[4][:, lo], T.sm2[:], ALU.is_equal, ["sm2"], ["b4", "eq15"])
+        tt(T.v0[:], bk[0][:, hi], T.tg[:], ALU.min, ["tg"], ["b0", "v0"])
+        if t < R - 1:
+            mm(bk[6][:, hi], I4, T.od[:], True, False, K, "b6")
+            mm(bk[6][:, hi], sh(T.bow, dn), zn, False, True, [znk] + K, "b6")
+            mm(bk[7][:, lo], I, zn, True, True, [znk] + K, "b7")
+        for _ in range(2):
+            mm(bk[2][:, hi], sh(T.i8w, -d), T.c1s[:], False, False, ["c1s"] + K, "b2")
+        mm(bk[2][:, hi], sh(T.bo8, -d), T.eq[:, 15, :], False, False, ["eq15"] + K, "b2")
+        mm(bk[0][:, lo], sh(T.iw, d), T.v0[:], True, True, ["v0"] + K, "b0")
+        thr = XO + W0 - 0.5
+        equal_rows(4, "mrs", "sm2", [(2, 256, sh(T.bo8, -d))], {})
+        relist2()
+        act(T.nv0[:], T.v0[:], ACT.Identity, 0.0, -1.0, rd=["v0"], wr=["nv0"])
+        if t < R - 1:
+            scan(T.sm2[:], T.rs[:], bk[6][:, hi], 0.0, ALU.add, ALU.min, K, ["b6", "sm2"])
+        if gens:
+            act(T.sgb[:], T.crs[:], ACT.Sign, thr + P * gens[0] * (len(gens) - 1), -1.0, rd=["crs"], wr=["sgb"])
+            mm(bk[3][:, hi], I, T.yk[:], True, False, ["yk"] + K, "b3")
+            turned(3, 256, T.foT, "foT", I8, False)
+            mm(bk[3][:, hi], I8, T.sgb[:], False, True, ["sgb"] + K, "b3")
+        if len(gens) > 1:
+            act(T.sga[:], T.crs[:], ACT.Sign, -thr, 1.0, rd=["crs"], wr=["sga"])
+            mm(bk[1][:, hi], I, T.yk[:], True, False, ["yk"] + K, "b1")
+            mm(bk[1][:, hi], I4, T.sgb[:], False, False, ["sgb"] + K, "b1")
+            mm(bk[1][:, hi], I4, T.sga[:], False, True, ["sga"] + K, "b1")
+        if gens:
+            act(T.wh0[:], bk[3][:, hi], ACT.Relu, -8192.0, wr=["b3", "wh0"])
+        act(T.vf[:], bk[0][:, lo], ACT.Copy, wr=["b0", "vf"])
+        if len(gens) > 1:
+            act(T.wh1[:], bk[1][:, hi], ACT.Relu, -8192.0, wr=["b1", "wh1"])
+        act(T.nvf[:], bk[0][:, lo], ACT.Identity, 0.0, -1.0, wr=["b0", "nvf"])
+        scan(T.scl[:], T.rm[:], bk[2][:, hi], 131072.0, ALU.min, ALU.max, K, ["b2", "scl"])
+        tt(T.nbs[:], bk[2][:, hi], T.nod[:], ALU.is_lt, K, ["b2", "nbs"])
+        cp(T.cs[:, t, :], T.scl[:, 15:256:16], ["scl"], ["cs%d" % t])
+        mm(bk[5][:, hi], sh(T.i8w, d), T.nbs[:], False, True, ["nbs"] + K, "b5")
+        mm(bk[4][:, hi], I, T.v0[:], True, False, ["v0"] + K, "b4")
+        mm(bk[4][:, hi], I8, T.nbs[:], False, True, ["nbs"] + K, "b4")
+        for n in range(len(gens)):
+            b = (2, 3)[n]
+            mm(bk[b][:, lo], sh(T.iw, d), T["wh%d" % n][:], True, True, ["wh%d" % n] + K, "b%d" % b)
+            act(T["uh%d" % n][:], T["wh%d" % n][:], ACT.Identity, 63.0, -1.0, rd=["wh%d" % n], wr=["uh%d" % n])
+            act(T["wf%d" % n][:], bk[b][:, lo], ACT.Copy, wr=["b%d" % b, "wf%d" % n])
+            act(T["uf%d" % n][:], bk[b][:, lo], ACT.Identity, 63.0, -1.0, wr=["b%d" % b, "uf%d" % n])
+
+        tt(win.indirect(T.cs[:, t, :]), T.yk[:], T.nv0[:], ALU.add, ["X", "cs%d" % t, "yk", "nv0"], ["X"])
+        act(X[:, wt:wt + P], bk[4][:, hi], ACT.Relu, wr=["b4", "Xnew"])
+        scan(T.sml[:], T.rm[:], bk[5][:, hi], 131072.0, ALU.min, ALU.max, K, ["b5", "sml"])
+        for n, u in enumerate(gens):
+            blk = X[:, XO + W0 + P * u:XO + W0 + P * u + P]
+            tt(blk, blk, T["wh%d" % n][:], ALU.subtract, ["X", "wh%d" % n], ["X"])
+        cp(T.ms[:, t, :], T.sml[:, 15:256:16], ["sml"], ["ms%d" % t])
+        tt(T.tg[:], win.indirect(T.ms[:, t, :]), T.vf[:], ALU.max, ["X", "ms%d" % t, "vf"], ["tg"])
+        tt(win.indirect(T.ms[:, t, :]), T.tg[:], T.nvf[:], ALU.add, ["X", "tg", "nvf"], ["X"])
+        for n, u in enumerate(gens):
+            for lst, w_, u_ in ((T.cs, "wh%d" % n, "uh%d" % n), (T.ms, "wf%d" % n, "uf%d" % n)):
+                tt(T.tg[:], win.indirect(lst[:, u, :]), T[u_][:], ALU.min, ["X", u_], ["tg"])
+                tt(win.indirect(lst[:, u, :]), T.tg[:], T[w_][:], ALU.add, ["X", "tg", w_], ["X"])
+
+        be, bek = T.bexp[:, par, :], "bexp%d" % par
+        cn = T.CN[:, s:A:2]
+        if t < 2:
+            act(T.Ls[:, s, :], cn, ACT.Copy, rd=["CN"], wr=["Ls%d" % s])
+        mm(bk[0][:, hi], I, T.i256[:], True, False, K, "b0")
+        mm(bk[0][:, hi], T.ones[0:11 + t, 0:128], T.c256[0:11 + t, :], False, False, K, "b0")
+        mm(bk[0][:, hi], sh(T.bof, -d), be, False, False, [bek] + K, "b0")
+        turned(0, 256, T.nek, "nek", I8, False)
+        mm(bk[0][:, hi], I8, T.nbs[:], False, True, ["nbs"] + K, "b0")
+        if gens:
+            src, key = (T.Ls, "Ls%d" % s) if len(gens) == 1 else (T.Us, "Us%d" % s)
+            mm(bk[1][:, hi], T.i32[:], src[:, s, :], True, False, [key] + K, "b1")
+            turned(1, 256, T.nek, "nek", I4, False)
+            turned(1, 256, T.foT, "foT", I4, True)
+        if len(gens) == 1:
+            mm(bk[7][:, hi], T.i32[:], cn, True, False, ["CN"] + K, "b7")
+            turned(7, 256, T.nek, "nek", I8, False)
+            mm(bk[7][:, hi], I8, T.nbs[:], False, True, ["nbs"] + K, "b7")
+        c1 = 128 - 16 * ((-d) % 8)
+        mm(bk[4][:, lo], T.zw[:, 16 + c1:144 + c1], be, True, False, [bek] + K, "b4")
+        mm(bk[4][:, lo], T.zw32[:, 15:143], T.pc[:], False, False, ["pc"] + K, "b4")
+        mm(bk[4][:, lo], T.zw32[:, 14 + c1:142 + c1], T.pm[:], False, False, ["pm"] + K, "b4")
+        mm(bk[4][:, lo], I8, T.nbs[:], False, True, ["nbs"] + K, "b4")
+        act(T.recb[:, P * t:P * t + P], bk[4][:, lo], ACT.Relu, T.col[:, 6:7], rd=K, wr=["b4", "recb"])
+        if t == R - 1:
+            for c in range(NCH):
+                xs = slice(XO + CW * c, XO + CW * c + CW)
+                dma("S", T["sto%d" % c][:], X[:, xs], XK, ["sto%d" % c])
+            for c in range(NCH):
+                xs = slice(XO + CW * c, XO + CW * c + CW)
+                exchange(3 + c, T["sto%d" % c], T["lno%d" % c], ["sto%d" % c], ["lno%d" % c])
+            dma("S", T.xo[r32, :], X[r32, XO:XO + 4096], XK, [])
+        if t == 0:
+            make_selm(1)
+        if gens:
+            tt(cn, bk[1][:, hi], cn, ALU.min, ["CN"], ["b1", "CN"])
+        if t < R - 1:
+            cp(T.t3[:], T.sm2[:, 15:256:16], ["sm2"], ["t3"])
+        tt(cn, bk[0][:, hi], cn, ALU.max, ["CN"], ["b0", "CN"])
+        if t < R - 1:
+            ts(T.bl[:], T.t3[:], 511, ALU.bitwise_and, rd=["t3"], wr=["bl0", "bl1"])
+        ts(T.Cf[:, s:A:2], cn, MAGIC, ALU.add, -MAGIC, ALU.add, rd=["CN"], wr=["Cf"])
+        if t < R - 1:
+            cp(T.bu[:], T.bl[:], ["bl0"], ["bu"])
+            mm(bk[2][:, hi], T.i32[:], cn, True, False, ["CN"] + K, "b2")
+            mm(bk[2][:, hi], T.in32[:], T.Cf[:, s:A:2], False, True, ["Cf"] + K, "b2")
+            nbs_ = [lambda s=s: act(T.Nb[:, s:A:2], bk[2][:, hi], ACT.Copy, wr=["b2", "Nb"])]
+            cp(T.Mu[:], T.Cf[:].indirect(T.bu[:]), ["Cf", "bu"], ["Mu"])
+            late = [lambda par=par: payee(1 - par, ["bl0", "bl1"], False)]
+            if len(gens) == 1:
+                tt(T.Us[:, s, :], bk[7][:, hi], T.Ls[:, s, :], ALU.max, ["Ls%d" % s], ["b7", "Us%d" % s])
+            if t < R - 2:
+                late.append(lambda s=s: cp(T.Lu[:, s, :], T.Cf[:, s:A:2], ["Cf"], ["Lu%d" % s]))
+
+    ts(T.CN[:], T.Cf[:], -256.0, ALU.add, rd=["Cf"], wr=["CN"])
+    dma("A", T.stf[:, :, 0:128], T.CN[:], ["CN"], ["stf3"])
+    for e in range(3):
+        dma("A", T.stf[:, :, 128 + 24 * e:152 + 24 * e], T.recb[e:128:16, :], ["recb"], ["stf%d" % e])
+    SF = ["stf0", "stf1", "stf2", "stf3"]
+    exchange(2, T.stf, T.lnf, SF, ["lnf"])
+    dma("A", T.lnf[me], T.stf[me], SF, ["lnfo"])
+    for c in range(NCH):
+        for a, b in ((0, me), (me + 1, N)):
+            if b > a:
+                dma("S", T.xo[32 * a:32 * b, CW * c:CW * c + CW], T["lno%d" % c][a:b], ["lno%d" % c], [])
+    dma("A", T.co[:], T.lnf[:, :, 0:128], ["lnf", "lnfo"], [])
+    for e in range(3):
+        dma("A", T.rec[8 * e:8 * e + 8, :], T.lnf[:, :, 128 + 24 * e:152 + 24 * e], ["lnf", "lnfo"], [])
+    emit(g, T, ops)

@@ -6,41 +6,50 @@ ALU, ACT = AluOpType, ActivationFunctionType
 N = 4
 W0, P, R, A = 2560, 256, 6, 512
 WT = [1, 64, 5, 83, 17, 131, 29, 211, 43, 157, 61, 239, 71, 113, 97, 199]
-KR = 8
+ZA = [8, 8, 4, 4, 0, 0]
+KRS = [7, 7, 7, 8, 8, 6]
 ORDER = "y0 d0 n0 r0 h0 p0 y1 m0 s0 P0 h1 d1 e0 E0 o0 r1 m1 p1 g0 b0 s1 B0 t0 P1 e1 o1 E1 l0 g1 f0 b1 B1"
-NA = 7
+ORDER0 = "y0 d0 r0 h0 y1 m0 s0 h1 d1 n0 o0 r1 p0 m1 P0 s1 e0 t0 E0 p1 o1 g0 P1 b0 g1 f0 B0 e1 E1 l0 b1 B1 c0"
+JZ, JF, JV, JE = 0, 1, 3, 4
+GE = True
+NP = 3
+SL = 6
+NA = 6
 MAGIC = 1.5 * 2 ** 23
 XO = 256
-NCH = 2
-CW = 4096 // NCH
+CH = [(2816, 4096), (0, 1408), (1408, 2816)]
+NCH = len(CH)
+XH = W0 // 2
 
 F, B, I32, U16 = "float32", "bfloat16", "int32", "uint16"
 SCRATCH = {
-    "sti": ("dram", [N, 128, 172], I32), "lni": ("dram", [N, 128, 172], I32),
-    "stb": ("dram", [N, 128, 704], B), "lnb": ("dram", [N, 128, 704], B),
+    "sti": ("dram", [N, 128, 132], I32), "lni": ("dram", [N, 128, 132], I32),
+    "stn": ("dram", [N, 128, 128], B), "lnn": ("dram", [N, 128, 128], B), "plh": ("sbuf", [128, A + 160], I32),
+    "stb": ("dram", [N, 128, 384], B), "lnb": ("dram", [N, 128, 384], B),
+    "stc": ("dram", [N, 128, 320], B), "lnc": ("dram", [N, 128, 320], B),
     "stf": ("dram", [N, 128, 200], F), "lnf": ("dram", [N, 128, 200], F),
     "X": ("sbuf", [128, XO + 4096], B), "y": ("sbuf", [128, 4096], B), "mh": ("sbuf", [128, 4096], B),
     "my": ("sbuf", [128, 4096], B), "zrep": ("sbuf", [128, 4096], B), "zf": ("sbuf", [128, 256], B),
     "crs": ("sbuf", [128, 256], F), "mrs": ("sbuf", [128, 256], F), "ad": ("sbuf", [128, 2048], B), "eqa": ("sbuf", [128, 2048], B),
-    "od16": ("sbuf", [128, 256], B), "in32": ("sbuf", [128, 128], F),
-    "Eb": ("sbuf", [128, 4352], F), "d0": ("sbuf", [128, 1280], F), "am": ("sbuf", [128, 64], F), "So": ("sbuf", [128, 4352], F),
+    "i18": ("sbuf", [128, 128], B), "in32": ("sbuf", [128, 128], F),
+    "Eb": ("sbuf", [128, 4352], F), "d0": ("sbuf", [128, 1280], F), "So": ("sbuf", [128, 4416], F),
     "selm": ("sbuf", [128, 4096], B), "nil": ("sbuf", [128, 512], B), "eq": ("sbuf", [128, 16, 256], B),
-    "nm": ("sbuf", [128, W0], I32), "nmb": ("sbuf", [128, W0], B), "pli": ("sbuf", [128, A], I32), "plu": ("sbuf", [128, A], U16),
+    "nmb": ("sbuf", [128, W0], B), "pli": ("sbuf", [128, A], I32), "plu": ("sbuf", [128, A], U16),
     "CN": ("sbuf", [128, A], F), "Cf": ("sbuf", [128, A], F), "Nb": ("sbuf", [128, A], B),
     "Lu": ("sbuf", [128, 2, 256], U16), "Mu": ("sbuf", [128, 256], U16), "Mf": ("sbuf", [128, 256], F), "NM": ("sbuf", [128, 256], B),
     "Ls": ("sbuf", [128, 2, 256], F), "Us": ("sbuf", [128, 2, 256], F), "recb": ("sbuf", [128, 1536], F), "nod": ("sbuf", [128, 256], B),
     "z": ("sbuf", [128, 2, 256], B), "bexp": ("sbuf", [128, 2, 256], B), "Gs": ("sbuf", [128, 256], F),
     "bi": ("sbuf", [128, 16], I32), "ki": ("sbuf", [128, 16], I32), "li": ("sbuf", [128, 16], I32), "lf": ("sbuf", [128, 16], F),
-    "t1": ("sbuf", [128, 16], I32), "t2": ("sbuf", [128, 16], I32), "t3": ("sbuf", [128, 16], I32), "bl": ("sbuf", [128, 16], I32),
+    "t3": ("sbuf", [128, 16], I32), "bl": ("sbuf", [128, 16], I32),
     "bc": ("sbuf", [128, 16], F), "bu": ("sbuf", [128, 16], U16), "cu": ("sbuf", [128, 16], U16), "mu": ("sbuf", [128, 16], U16),
     "cs": ("sbuf", [128, R, 16], U16), "ms": ("sbuf", [128, R, 16], U16), "ex": ("sbuf", [128, 3, 16], U16), "exi": ("sbuf", [128, 3, 16], I32),
     "iw": ("sbuf", [128, 256], B), "inw": ("sbuf", [128, 256], B), "i8w": ("sbuf", [128, 256], B), "i4": ("sbuf", [128, 128], B),
     "i32": ("sbuf", [128, 128], F), "bo": ("sbuf", [128, 256], B), "bo8": ("sbuf", [128, 256], B), "bo32": ("sbuf", [128, 128], F),
-    "bop": ("sbuf", [128, 256], B), "bon": ("sbuf", [128, 256], B), "bof": ("sbuf", [128, 256], B), "bow": ("sbuf", [128, 256], B),
+    "bop": ("sbuf", [128, 256], B), "bon": ("sbuf", [128, 256], B), "bof": ("sbuf", [128, 256], B), "bow": ("sbuf", [128, 272], B),
     "zw": ("sbuf", [128, 272], B), "zw32": ("sbuf", [128, 272], F), "od": ("sbuf", [128, 256], B), "od8": ("sbuf", [128, 256], B),
-    "dm": ("sbuf", [128, 256], B), "rs": ("sbuf", [128, 256], F), "rm": ("sbuf", [128, 256], F), "i16": ("sbuf", [128, 256], F),
+    "dm": ("sbuf", [128, 256], B), "rm": ("sbuf", [128, 256], F), "i16": ("sbuf", [128, 256], F),
     "i256": ("sbuf", [128, 256], B), "c256": ("sbuf", [128, 256], B), "ones": ("sbuf", [128, 256], B),
-    "w1": ("sbuf", [128, 272], F), "w2": ("sbuf", [128, 272], F), "w3": ("sbuf", [128, 272], F), "col": ("sbuf", [128, 16], F),
+    "w1": ("sbuf", [128, 272], F), "col": ("sbuf", [128, 16], F),
     "coli": ("sbuf", [128, 4], I32), "wrow": ("sbuf", [128, 32], F),
 }
 for _n in ["nek", "nel", "nfT", "foT", "yk", "hm", "v0", "nv0", "vf", "nvf", "c1s", "nbs", "sga", "sgb", "tg",
@@ -49,11 +58,11 @@ for _n in ["nek", "nel", "nfT", "foT", "yk", "hm", "v0", "nv0", "vf", "nvf", "c1
 for _n in ["pc", "pm", "scl", "sml", "sm2"]:
     SCRATCH[_n] = ("sbuf", [128, 256], F)
 for _c in range(NCH):
-    SCRATCH["sto%d" % _c] = ("dram", [N, 128, CW // 4], B)
-    SCRATCH["lno%d" % _c] = ("dram", [N, 128, CW // 4], B)
+    SCRATCH["sto%d" % _c] = ("dram", [N, 128, (CH[_c][1] - CH[_c][0]) // 4], B)
+    SCRATCH["lno%d" % _c] = ("dram", [N, 128, (CH[_c][1] - CH[_c][0]) // 4], B)
 for _b in range(8):
     SCRATCH["pb%d" % _b] = ("psum", [128, 512], F)
-SEMAPHORES = ["sV", "sA", "sT", "sG"] + ["d%d" % _i for _i in range(48)] + ["ar%d" % _i for _i in range(3 + NCH)] + ["ls%d" % _i for _i in range(3 + NCH)]
+SEMAPHORES = ["sV", "sA", "sT", "sG"] + ["d%d" % _i for _i in range(56)] + ["ar%d" % _i for _i in range(5 + NCH)] + ["ls%d" % _i for _i in range(5 + NCH)]
 
 
 def engine_split(core, peers, topo):
@@ -75,7 +84,7 @@ def engine_split(core, peers, topo):
 
 def apart(k):
     return (len(k) == 2 and k[0] == "b" and k[1].isdigit()) or k.rstrip("01") in (
-        "K", "KA", "So", "zrep", "zrepV", "ad", "mym", "myr", "wrow", "selm", "recb")
+        "K", "KA", "KB", "So", "zrep", "zrepV", "ad", "mym", "myr", "wrow", "selm", "recb")
 
 
 def emit(g, T, ops):
@@ -216,109 +225,132 @@ def rank_program(g, core, T, topo):
     H = [slice(0, 128), slice(128, 256)]
     r32 = slice(32 * me, 32 * me + 32)
 
+    ms(T.nmb[:], 0.0, ["nm0"])
+    dma("S", T.plh[:, A:A + 160], T.fr0[:], [], ["nm"])
+    dma("A", T.stb[:, :, 0:320], T.x0[:, 0:XH], [], ["stb0"])
+    dma("S", T.stb[:, :, 320:384], T.z0[:], [], ["stb1"])
+    dma("A", T.plh[:, 0:A], T.pl[:], [], ["plh"])
     dma("S", T.sti[:, :, 0:128], T.pl[:], [], ["sti0"])
-    dma("A", T.sti[:, :, 128:168], T.fr0[:], [], ["sti1"])
-    dma("S", T.sti[:, :, 168:172], T.b0[:], [], ["sti2"])
-    dma("A", T.stb[:, :, 0:640], T.x0[:], [], ["stb0"])
-    dma("S", T.stb[:, :, 640:704], T.z0[:], [], ["stb1"])
+    dma("S", T.sti[:, :, 128:132], T.b0[:], [], ["sti2"])
+    dma("A", T.stc[:], T.x0[:, XH:W0], [], ["stc"])
     dma("A", T.lni[me, :, 0:128], T.pl[r32, :], [], ["lni0"])
-    dma("S", T.lni[me, :, 128:168], T.fr0[2 * me:2 * me + 2, :], [], ["lni1"])
-    dma("A", T.lni[me, :, 168:172], T.b0[r32, :], [], ["lni2"])
-    dma("S", T.lnb[me, :, 640:704], T.z0[r32, :], [], ["lnb1"])
-    dma("A", X[r32, XO:XO + W0], T.x0[r32, :], [], ["Xown"])
+    dma("A", T.lni[me, :, 128:132], T.b0[r32, :], [], ["lni2"])
+    dma("S", T.lnb[me, :, 320:384], T.z0[r32, :], [], ["lnb1"])
 
     iota(T.coli[:, 0:1], [[0, 1]], 0, 1, ["coli0"], False)
     iota(T.w1[:, 0:256], [[0, 2], [1, 128]], 0, 0, ["w1"])
-    iota(T.w2[:, 0:256], [[0, 2], [1, 8], [0, 16]], 0, 0, ["w2"])
+    iota(T.Eb[:, 0:256], [[0, 2], [1, 8], [0, 16]], 0, 0, ["w2"])
     iota(T.i16[:], [[0, 16], [1, 16]], 0, 0, ["i16"])
-    exchange(0, T.sti, T.lni, ["sti0", "sti1", "sti2"], ["lni"])
+    iota(T.So[:, 0:272], [[1, 272]], -16, 0, ["w3"])
     exchange(1, T.stb, T.lnb, ["stb0", "stb1"], ["lnb"])
-    iota(T.w3[:], [[1, 272]], -16, 0, ["w3"])
-    iota(T.i256[:], [[1, 256]], 0, 0, ["i256"])
+    exchange(0, T.sti, T.lni, ["sti0", "sti2"], ["lni"])
+    exchange(4 + NCH, T.stc, T.lnc, ["stc"], ["lnc"])
     iota(T.exi[:, 0, :], [[1, 16]], 0, 0, ["exi"], False)
+    for s in range(2):
+        d = 2 * (1 + s)
+        for h in range(2):
+            iota(T.exi[:, 1 + s, 8 * h:8 * h + d], [[1, d]], 8 * h + 8 - d, 0, ["exi"], False)
+            iota(T.exi[:, 1 + s, 8 * h + d:8 * h + 8], [[1, 8 - d]], 8 * h, 0, ["exi"], False)
     iota(T.lf[:], [[-16, 16]], 255, 0, ["lf"])
-    ms(T.nm[:], 0, ["nm0"])
+    iota(T.i256[:], [[1, 256]], 0, 0, ["i256"])
     cp(T.col[:, 0:1], T.coli[:, 0:1], ["coli0"], ["colp"])
     ts(T.coli[:, 1:2], T.coli[:, 0:1], 4, ALU.arith_shift_right, rd=["coli0"], wr=["coli1"])
     ts(T.coli[:, 2:3], T.coli[:, 0:1], 15, ALU.bitwise_and, rd=["coli0"], wr=["coli2"])
     cp(T.col[:, 1:3], T.coli[:, 1:3], ["coli1", "coli2"], ["colg"])
     cp_, cg, ce = T.col[:, 0:1], T.col[:, 1:2], T.col[:, 2:3]
     ts(T.iw[:], T.w1[:, 0:256], cp_, ALU.is_equal, rd=["w1", "colp"], wr=["iw"])
-    ts(T.bo[:], T.w2[:, 0:256], cg, ALU.is_equal, rd=["w2", "colg"], wr=["bo"])
+    ts(T.bo[:], T.Eb[:, 0:256], cg, ALU.is_equal, rd=["w2", "colg"], wr=["bo"])
+    ts(T.hm[:, 0:160], T.plh[:, A:A + 160], -256.0, ALU.add, 1.0 / 1024, ALU.mult, rd=["nm"], wr=["hm"])
+    dma("S", T.nmb[0:128:16, :], T.hm[:, 0:160], ["nm0", "hm"], ["nmb"])
+    dma("S", X[r32, XO:XO + W0], T.x0[r32, :], ["stc"], ["Xown"])
     ts(T.wrow[:, 16:32], T.i16[:, 0:16], ce, ALU.is_equal, 2.0 ** 32, ALU.mult, rd=["i16", "colg"], wr=["rowm"])
-    for out, v, n in ((T.inw, -1.0, 256), (T.i8w, -8192.0, 256), (T.i4, 4096.0, 128), (T.i32, 1.0, 128), (T.in32, -1.0, 128)):
-        act(out[:, 0:n], T.iw[:, 0:n], ACT.Identity, 0.0, v, rd=["iw"], wr=["KA"])
-    for j in range(4):
-        act(T.nil[:, j:512:4], T.iw[:, 0:128], ACT.Identity, 0.0, -2.0 ** 32, rd=["iw"], wr=["KA"])
-    for out, v, n in ((T.bo8, -8192.0, 256), (T.bo32, 1.0, 128), (T.bop, 512.0, 256), (T.bon, -512.0, 256), (T.bof, 1.0 / 1024, 256)):
-        act(out[:, 0:n], T.bo[:, 0:n], ACT.Identity, 0.0, v, rd=["bo"], wr=["KA"])
+    act(T.inw[:], T.iw[:], ACT.Identity, 0.0, -1.0, rd=["iw"], wr=["KA"])
+    act(X[:, 0:XO], T.iw[:], ACT.Identity, 0.0, 0.0, rd=["iw"], wr=["X"])
+
+    def scaled(part):
+        if part == 0:
+            for j in range(4):
+                act(T.nil[:, j:512:4], T.iw[:, 0:128], ACT.Identity, 0.0, -2.0 ** 32, rd=["iw"], wr=["KA"])
+            for out, v in ((T.bop, 512.0), (T.bon, -512.0)):
+                act(out[:], T.bo[:], ACT.Identity, 0.0, v, rd=["bo"], wr=["KA"])
+        elif part == 2:
+            for out, v in ((T.bo8, -8192.0), (T.bof, 1.0 / 1024)):
+                act(out[:], T.bo[:], ACT.Identity, 0.0, v, rd=["bo"], wr=["KB"])
+            for out, v, n in ((T.i8w, -8192.0, 256), (T.i4, 4096.0, 128), (T.i32, 1.0, 128), (T.in32, -1.0, 128)):
+                act(out[:, 0:n], T.iw[:, 0:n], ACT.Identity, 0.0, v, rd=["iw"], wr=["KB"])
+            act(T.bo32[:], T.bo[:, 0:128], ACT.Copy, rd=["bo"], wr=["KB"])
+        else:
+            ts(T.od8[:], T.od[:], -8192.0, ALU.add, rd=["od"], wr=["K"])
+            ts(T.i18[:], T.iw[:, 0:128], 0.125, ALU.mult, rd=["iw"], wr=["K"])
+            ts(T.nod[:], T.od[:], -1.0, ALU.mult, rd=["od"], wr=["K"])
 
 
-    def make_selm(s):
-        for l in range(16):
+    def make_selm(s, ls=range(16)):
+        for l in ls:
             c = 2048 * s + 512 * (l // 4)
             act(T.selm[:, c + l % 4:c + 512:4], sh(T.bo, -2 * (1 + s)), ACT.Identity, 0.0, T.wrow[:, 16 + l:17 + l], rd=["rowm", "bo"], wr=["selm%d" % s])
-    make_selm(0)
-    ts(T.dm[:], T.i16[:], ce, ALU.is_equal, rd=["i16", "colg"], wr=["dm"])
     ts(T.od[:], T.i16[:], ce, ALU.not_equal, 32768.0, ALU.mult, rd=["i16", "colg"], wr=["od"])
-    ts(T.col[:, 3:4], ce, 0.0, ALU.is_equal, 1.0 / 1024, ALU.mult, rd=["colg"], wr=["col3"])
-    ts(T.col[:, 4:5], ce, 0.0, ALU.is_equal, 512.0, ALU.mult, rd=["colg"], wr=["col4"])
-    ts(T.col[:, 5:6], cg, 16.0, ALU.mult, rd=["colg"], wr=["col5"])
-    for j in range(16):
-        ms(T.wrow[:, j:j + 1], float(WT[j]), ["wrow"])
-    act(T.od8[:], T.od[:], ACT.Identity, -8192.0, rd=["od"], wr=["KA"])
-    act(T.od16[:], T.od[:], ACT.Identity, -16384.0, rd=["od"], wr=["KA"])
-    act(T.nod[:], T.od[:], ACT.Identity, 0.0, -1.0, rd=["od"], wr=["KA"])
-    act(T.c256[:], T.od[:], ACT.Identity, 256.0, 0.0, rd=["od"], wr=["KA"])
-    act(T.ones[:], T.od[:], ACT.Identity, 1.0, 0.0, rd=["od"], wr=["KA"])
-    act(X[:, 0:XO], T.od[:], ACT.Identity, 0.0, 0.0, rd=["od"], wr=["X"])
-    act(T.rs[:], T.od[:], ACT.Identity, 0.0, 0.0, rd=["od"], wr=["rs"])
-    act(T.rs[:, 0:256:16], T.od[:, 0:16], ACT.Identity, 131072.0, 0.0, rd=["od", "rs"], wr=["rs", "KA"])
-    ts(T.col[:, 6:7], T.col[:, 4:5], -256.0, ALU.add, rd=["col4"], wr=["K"])
-    tt(T.wrow[:, 0:16], T.wrow[:, 0:16], T.dm[:, 0:16], ALU.mult, ["wrow", "dm"], ["wrow"])
-    ts(T.w1[:], T.w3[:], T.col[:, 5:6], ALU.subtract, rd=["w3", "col5"], wr=["w1"])
-    op("V", lambda q: q.tensor_reduce(T.col[:, 9:10], T.wrow[:, 0:16], AxisListType.X, ALU.add), ["wrow"], ["col9"])
-    ts(T.w2[:], T.w1[:], 0.0, ALU.is_equal, rd=["w1"], wr=["w2"])
-    ts(T.w3[:], T.w1[:], 128.0, ALU.is_equal, rd=["w1"], wr=["w3"])
-    act(T.bow[:], T.bo[:], ACT.Identity, 0.0, T.col[:, 9:10], rd=["col9", "bo"], wr=["KA"])
-    tt(T.zw32[:], T.w2[:], T.w3[:], ALU.add, ["w2", "w3"], ["zw32"])
-    ms(T.rm[:], 131072.0, ["rm"])
-    act(T.zw[:], T.zw32[:], ACT.Copy, rd=["zw32"], wr=["KA"])
-    ts(T.rm[:, 0:256:16], T.lf[:], ce, ALU.subtract, rd=["rm", "lf", "colg"], wr=["rm"])
-    for s in range(2):
-        ts(T.t1[:], T.exi[:, 0, :], 8 - 2 * (1 + s), ALU.add, rd=["exi"], wr=["t1"])
-        ts(T.t2[:], T.t1[:], 7, ALU.bitwise_and, rd=["t1"], wr=["t2"])
-        ts(T.t3[:], T.exi[:, 0, :], 8, ALU.bitwise_and, rd=["exi"], wr=["t3"])
-        tt(T.exi[:, 1 + s, :], T.t2[:], T.t3[:], ALU.add, ["t2", "t3"], ["exi1"])
-    cp(T.ex[:], T.exi[:], ["exi", "exi1"], ["K"])
-    iota(T.d0[:, 0:1024], [[0, 1024]], -1, 0, ["d00", "d01"])
-    iota(T.d0[:, 1024:1280], [[0, 256]], -32, 0, ["d00", "d01"])
-    op("G", lambda q: q.iota(T.d0[:, 0:1024:512], [[0, 2]], 2 ** 23, 0, allow_small_or_imprecise_dtypes=True), ["d00"], ["d00", "d01"])
-    op("G", lambda q: q.iota(T.d0[:, 1024:1280:16], [[0, 16]], 2 ** 23, 0, allow_small_or_imprecise_dtypes=True), ["d00"], ["d00", "d01"])
-    ts(T.col[:, 7:8], T.col[:, 0:1], 1.0, ALU.mult, rd=["colp", "rm", "od", "dm", "zw32", "i256", "i16", "K"], wr=["K"])
-    K = ["K", "KA"]
 
-    dma("S", T.pli[:], T.lni[:, :, 0:128], ["lni", "lni0"], ["pli"])
-    dma("S", T.nm[0:128:16, :], T.lni[:, :, 128:168], ["lni", "lni1", "nm0"], ["nm"])
-    dma("S", T.bl[32:128, :], T.lni[0:3, :, 168:172], ["lni", "lni2"], ["bl0"])
-    dma("S", T.bl[0:32, :], T.lni[3, :, 168:172], ["lni", "lni2"], ["bl1"])
-    dma("S", T.z[:, 0, :], T.lnb[:, :, 640:704], ["lnb", "lnb1"], ["z0"])
-    dma("S", T.zf[32:128, :], T.lnb[0:3, :, 640:704], ["lnb", "lnb1"], ["zf1"])
-    dma("S", T.zf[0:32, :], T.lnb[3, :, 640:704], ["lnb", "lnb1", "zf1"], ["zf"])
+    cp(T.plu[:], T.plh[:, 0:A], ["plh"], ["plu"])
+    scaled(0)
+    make_selm(0, range(6))
+    for h in range(2):
+        act(T.mh[:, 2048 * h:2048 * h + 2048], T.nmb[:].indirect(T.plu[:, 256 + 128 * h:384 + 128 * h]), ACT.Copy, rd=["nmb", "plu"], wr=["mh%d" % h])
+    ts(T.col[:, 5:6], cg, 16.0, ALU.mult, rd=["colg"], wr=["col5"])
+    ts(T.w1[:], T.So[:, 0:272], T.col[:, 5:6], ALU.subtract, rd=["w3", "col5"], wr=["w1"])
+    ts(T.Eb[:, 0:272], T.w1[:], 0.0, ALU.is_equal, rd=["w1"], wr=["w2"])
+    ts(T.So[:, 0:272], T.w1[:], 128.0, ALU.is_equal, rd=["w1"], wr=["w3"])
+    tt(T.zw32[:], T.Eb[:, 0:272], T.So[:, 0:272], ALU.add, ["w2", "w3"], ["zw32"])
+    cp(T.zw[:], T.zw32[:], ["zw32"], ["zw"])
+    for h in range(2):
+        cp(T.my[:, 2048 * h:2048 * h + 2048], T.nmb[:].indirect(T.plu[:, H[h]]), ["nmb", "plu"], ["myn%d" % h])
+    for h in range(2):
+        for c, buf, keys in ((1, T.mh, ["mh%d" % h]), (0, T.my, ["myn%d" % h, "myr0", "myr1", "mym0", "mym1"])):
+            b = 2 * h + c
+            for k in range(16):
+                mm(bk[b][:, 0:128], T.zw[:, 16 - k:144 - k], buf[:, 2048 * h + k:2048 * h + 2048:16], k == 0, k == 15, keys + ["zw"], "b%d" % b)
+    for b in (1, 0, 3, 2):
+        c = 256 * (b % 2) + 128 * (b // 2)
+        act(T.ad[:, c:c + 128], bk[b][:, 0:128], ACT.Copy, wr=["b%d" % b, "ad"])
+        if b == 0:
+            make_selm(0, range(6, 12))
+    dma("A", T.stn[:], T.ad[:, 0:512], ["ad"], ["stn"])
+    dma("A", T.Nb[r32, :], T.ad[r32, 0:512], ["ad"], ["Nbo"])
+    make_selm(0, range(12, 16))
+    scaled(2)
+    scaled(1)
+    ts(T.dm[:], T.i16[:], ce, ALU.is_equal, rd=["i16", "colg"], wr=["dm"])
+    ts(T.col[:, 4:5], ce, 0.0, ALU.is_equal, 512.0, ALU.mult, rd=["colg"], wr=["col4"])
+    ts(T.col[:, 6:7], T.col[:, 4:5], -256.0, ALU.add, rd=["col4"], wr=["K"])
+    iota(T.rm[:], [[0, 256]], 131072, 0, ["rm"])
+
+    def weights():
+        tt(T.wrow[:, 0:16], T.wrow[:, 0:16], T.dm[:, 0:16], ALU.mult, ["wrow", "dm"], ["wrow2"])
+        op("V", lambda q: q.tensor_reduce(T.col[:, 9:10], T.wrow[:, 0:16], AxisListType.X, ALU.add), ["wrow2"], ["col9"])
+        act(T.bow[:], T.zw[:], ACT.Identity, 0.0, T.col[:, 9:10], rd=["col9", "zw"], wr=["bow"])
+
+    ts(T.rm[:, 0:256:16], T.lf[:], ce, ALU.subtract, rd=["rm", "lf", "colg"], wr=["rm"])
+    cp(T.ex[:], T.exi[:], ["exi"], ["K"])
+    iota(T.c256[:], [[0, 256]], 256, 0, ["KG"])
+    iota(T.ones[:, 0:128], [[0, 128]], 1, 0, ["KG"])
+    ts(T.col[:, 7:8], T.col[:, 0:1], 1.0, ALU.mult, rd=["colp", "rm", "od", "dm", "zw32", "i256", "i16", "K"], wr=["K"])
+    K = ["K", "KA", "KG"]
+
+    dma("S", T.zf[32:128, :], T.lnb[0:3, :, 320:384], ["lnb", "lnb1"], ["zf1"])
+    dma("S", T.zf[0:32, :], T.lnb[3, :, 320:384], ["lnb", "lnb1"], ["zf"])
     for n, (a, b) in enumerate(((0, me), (me + 1, N))):
         if b > a:
-            dma("S", X[32 * a:32 * b, XO:XO + W0], T.lnb[a:b, :, 0:640], ["lnb"], ["Xin%d" % n])
+            dma("S", X[32 * a:32 * b, XO:XO + XH], T.lnb[a:b, :, 0:320], ["lnb"], ["Xin%d" % n])
+    dma("S", T.z[:, 0, :], T.lnb[:, :, 320:384], ["lnb", "lnb1"], ["z0"])
+    dma("S", T.pli[:], T.lni[:, :, 0:128], ["lni", "lni0"], ["pli"])
+    dma("S", T.bl[32:128, :], T.lni[0:3, :, 128:132], ["lni", "lni2"], ["bl0"])
+    dma("S", T.bl[0:32, :], T.lni[3, :, 128:132], ["lni", "lni2"], ["bl1"])
+    for n, (a, b) in enumerate(((0, me), (me + 1, N))):
+        if b > a:
+            dma("S", X[32 * a:32 * b, XO + XH:XO + W0], T.lnc[a:b], ["lnc"], ["Xin%d" % (2 + n)])
 
-    cp(T.plu[:], T.pli[:], ["pli"], ["plu"])
-    ts(T.nmb[:], T.nm[:], -256.0, ALU.add, T.col[:, 3:4], ALU.mult, rd=["nm", "col3"], wr=["nmb"])
-    act(T.mh[:], T.nmb[:].indirect(T.plu[:, hi]), ACT.Copy, rd=["nmb", "plu"], wr=["mh0", "mh1"])
-    MY = ["myr0", "myr1", "mym0", "mym1"]
     ts(T.Lu[:, 0, :], T.pli[:, 0:A:2], 256.0, ALU.add, rd=["pli"], wr=["Lu0"])
-    cp(T.my[:], T.nmb[:].indirect(T.plu[:, lo]), ["nmb", "plu"], MY)
     ts(T.Cf[:], T.pli[:], 256.0, ALU.add, rd=["pli"], wr=["Cf"])
-    for c, buf, keys in ((1, T.mh, ["mh0", "mh1"]), (0, T.my, MY)):
-        for k in range(16):
-            mm(bk[c][:, lo], T.zw[:, 16 - k:144 - k], buf[:, k:4096:16], k == 0, k == 15, keys + K, "b%d" % c)
 
     def payee(par, keys, lst=True):
         if lst:
@@ -328,28 +360,40 @@ def rank_program(g, core, T, topo):
 
     def spread(js):
         for j in js:
-            op("G", lambda q, j=j: q.affine_select(T.zrep[:, j:4096:16], T.zf[:], [[0, 256]], ALU.is_ge, 0.0, 0, 0), ["zf"], ["zrep"])
+            op("G", lambda q, j=j: q.affine_select(T.zrep[:, j:4096:16], T.zf[:], [[0, 256]], ALU.is_ge, 0.0, 0, 0), ["zf", "zf1"], ["zrep0", "zrep1"])
 
     cp(T.bu[:], T.bl[:], ["bl0", "bl1"], ["bu"])
     cp(T.Mu[:], T.Cf[:].indirect(T.bu[:]), ["Cf", "bu"], ["Mu"])
-    spread(range(8))
-    for j in range(8, 16):
-        cp(T.zrep[:, j:4096:16], T.zf[:], ["zf"], ["zrepV"])
+    spread(range(NP))
+    exchange(3 + NCH, T.stn, T.lnn, ["stn"], ["lnn"])
+    iota(T.d0[:, 0:1024], [[0, 1024]], -1, 0, ["d00", "d01"])
+    iota(T.d0[:, 1024:1280], [[0, 256]], -32, 0, ["d00", "d01"])
+    op("G", lambda q: q.iota(T.d0[:, 0:1024:512], [[0, 2]], 2 ** 23, 0, allow_small_or_imprecise_dtypes=True), ["d00"], ["d00", "d01"])
+    op("G", lambda q: q.iota(T.d0[:, 1024:1280:16], [[0, 16]], 2 ** 23, 0, allow_small_or_imprecise_dtypes=True), ["d00"], ["d00", "d01"])
+    for j in range(16):
+        op("G", lambda q, j=j: q.iota(T.wrow[:, j:j + 1], [[0, 1]], WT[j], 0, allow_small_or_imprecise_dtypes=True), [], ["wrow"])
+    for n, (a, b) in enumerate(((0, me), (me + 1, N))):
+        if b > a:
+            dma("S", T.Nb[32 * a:32 * b, :], T.lnn[a:b], ["lnn"], ["Nbi%d" % n])
+    for j in range(NP, 16):
+        cp(T.zrep[:, j:4096:16], T.zf[:], ["zf", "zf1"], ["zrepV"])
     mm(bk[7][:, lo], I, T.z[:, 0, :], True, True, ["z0"] + K, "b7")
 
     def first_names():
-        for c in (1, 0):
-            act(T.Nb[:, 256 * c:256 * c + 256], bk[c][:, lo], ACT.Copy, wr=["b%d" % c, "Nb"])
+        act(T.col[:, 10:11], T.col[:, 0:1], ACT.Copy, rd=["Nbo", "Nbi0", "Nbi1"], wr=["Nb"])
 
     def first_lists():
+        weights()
         ts(T.bc[:], T.bl[:], -256.0, ALU.add, rd=["bl0", "bl1"], wr=["bc"])
         ts(T.Lu[:, 1, :], T.pli[:, 1:A:2], 256.0, ALU.add, rd=["pli"], wr=["Lu1"])
         tt(T.bexp[:, 0, :], T.bc[:].indirect(T.ex[:, 0, :]), T.dm[:], ALU.mult, ["bc"] + K, ["bexp0"])
-        for c in (1, 0):
-            sl = slice(256 * c, 256 * c + 256)
-            tt(T.CN[:, sl], T.Nb[:, sl], T.Cf[:, sl], ALU.add, ["Cf", "Nb"], ["CN"])
 
-    late, nbs_ = [first_lists], [first_names]
+    def first_cn():
+        mm(bk[4][:], T.i32[:], T.Cf[:], True, False, ["Cf", "KB"], "b4")
+        mm(bk[4][:], I, T.Nb[:], False, True, ["Nb"] + K, "b4")
+        act(T.CN[:], bk[4][:], ACT.Copy, wr=["b4", "CN"])
+
+    late, nbs_, recs = [first_lists], [first_names], []
     for t in range(R):
         s, par = t % 2, t % 2
         d = 2 * (1 + s)
@@ -357,7 +401,7 @@ def rank_program(g, core, T, topo):
         zk, z = "z%d" % par, T.z[:, par, :]
         wt = XO + W0 + P * t
         win = X[:, 0:wt]
-        XK = ["X", "Xnew", "Xown", "Xin0", "Xin1"]
+        XK = ["X", "Xnew", "Xown", "Xin0", "Xin1", "Xin2", "Xin3"]
         gens = [u for u in (t - 2, t - 4) if u >= 0]
 
         def ygather(h):
@@ -365,18 +409,22 @@ def rank_program(g, core, T, topo):
 
         def hgather(h):
             tt(T.mh[:, 2048 * h:2048 * h + 2048], win.indirect(T.Mu[:, H[h]]), T.zrep[:, 2048 * h:2048 * h + 2048], ALU.min,
-               XK + ["Mu", "zrep", "zrepV"], ["mh%d" % h])
+               XK + ["Mu", "zrep%d" % h, "zrepV"], ["mh%d" % h])
 
         def ycol(h, k):
             return T.y[:, 2048 * h + k:2048 * h + 2048:16]
 
         def myk(h, k, n=1):
-            c = (16 * h + k) * 128
+            m = 16 - KRS[t]
+            c = (2 * k + h) * 128 if k < m else (2 * m + KRS[t] * h + k - m) * 128
             return T.my[:, c:c + 128 * n]
 
+        KR = KRS[t]
         quads = [(k0, min(4, 16 - k0)) for k0 in range(16 - KR, 16, 4)]
 
         def differ(h, ns=(0, 1)):
+            while recs:
+                recs.pop()()
             for n in ns:
                 if n < len(quads):
                     b = 4 + n % 2
@@ -393,6 +441,10 @@ def rank_program(g, core, T, topo):
         def min_part(h):
             for k in range(16 - KR):
                 tt(myk(h, k), bk[7][:, H[h]], ycol(h, k), ALU.min, ["y%d" % h], ["b7", "mym%d" % h])
+
+        def min_both(h):
+            for k in range(16 - KR):
+                tt(myk(0, k, 2), bk[7][:, lo], T.y[:, k:4096:16], ALU.min, ["y0", "y1"], ["b7", "mym0", "mym1"])
 
         def fsum(h):
             for k in list(range(16 - KR, 16)) + list(range(16 - KR)):
@@ -443,26 +495,29 @@ def rank_program(g, core, T, topo):
         def farlist():
             act(T.Mf[:], T.Cf[:].indirect(T.bu[:]), ACT.Copy, rd=["Cf", "bu"], wr=["Mf"])
 
+        def rest(h):
+            first_cn()
+            make_selm(1, range(SL))
+
         def tidy():
             for fn in late:
                 fn()
 
         steps = {"y": ygather, "h": hgather, "r": relu_part, "m": min_part, "s": fsum, "o": fout, "d": differ,
-                 "g": step, "f": least, "b": lambda h: best(h, 0), "B": lambda h: best(h, 2),
+                 "g": step, "M": min_both, "c": rest, "f": least, "b": lambda h: best(h, 0), "B": lambda h: best(h, 2),
                  "p": lambda h: pairs(h, 0), "P": lambda h: pairs(h, 2), "e": lambda h: fold(h, 0), "E": lambda h: fold(h, 2),
                  "n": lambda h: names(), "l": lambda h: farlist(), "t": lambda h: tidy()}
-        for w in ORDER.split():
+        for w in (ORDER if t else ORDER0).split():
             steps[w[0]](int(w[1]))
 
+        K = ["K", "KA", "KB", "KG"]
         mm(bk[0][:, lo], T.i32[:], T.Cf[:, s:A:2], True, False, ["Cf"] + K, "b0")
         mm(bk[1][:, lo], T.i32[:], T.Mf[:], True, False, ["Mf"] + K, "b1")
-        mm(bk[2][:, lo], In, T.od16[:], True, False, K, "b2")
-        mm(bk[3][:, lo], T.ones[0:64, 0:128], T.c256[0:64, :], True, False, K, "b3")
-        mm(bk[5][:, lo], In, T.od8[:], True, False, K, "b5")
-        tt(T.am[:, 0:32], T.So[:, 63:2048:64], T.So[:, 2111:4096:64], ALU.min, ["So"], ["am0"])
-        tt(T.am[:, 32:48], T.am[:, 0:16], T.am[:, 16:32], ALU.min, ["am0"], ["am1"])
-        tt(T.am[:, 48:64], T.am[:, 32:48], T.Gs[:, 15:256:16], ALU.subtract, ["am1", "Gs0", "Gs1"], ["am2"])
-        tt(T.bi[:], T.am[:, 48:64], T.So[:, 4111:4352:16], ALU.min, ["am2"], ["bi"])
+        mm(bk[2][:, lo], In, T.od[:], True, False, K, "b2")
+        tt(T.So[:, 4352:4384], T.So[:, 63:2048:64], T.So[:, 2111:4096:64], ALU.min, ["So"], ["am0"])
+        tt(T.So[:, 4384:4400], T.So[:, 4352:4368], T.So[:, 4368:4384], ALU.min, ["am0"], ["am1"])
+        tt(T.So[:, 4400:4416], T.So[:, 4384:4400], T.Gs[:, 15:256:16], ALU.subtract, ["am1", "Gs0", "Gs1"], ["am2"])
+        tt(T.bi[:], T.So[:, 4400:4416], T.So[:, 4111:4352:16], ALU.min, ["am2", "So"], ["bi"])
         ts(T.li[:], T.bi[:], 31, ALU.bitwise_and, rd=["bi"], wr=["li"])
         ts(T.ki[:], T.bi[:], 5, ALU.arith_shift_right, 15, ALU.bitwise_and, rd=["bi"], wr=["ki"])
         cp(T.lf[:], T.li[:], ["li"], ["lf"])
@@ -478,23 +533,23 @@ def rank_program(g, core, T, topo):
         act(T.pc[:], bk[0][:, lo], ACT.Relu, wr=["b0", "pc"])
         if gens:
             act(T.foT[:], T.lf[:].indirect(T.ex[:, 0, :]), ACT.Relu, 16.0, -1.0, rd=["lf"] + K, wr=["foT"])
+        else:
+            act(T.Ls[:, s, :], T.CN[:, s:A:2], ACT.Copy, rd=["CN"], wr=["Ls%d" % s])
         turned(1, 0, T.nel, "nel", I8, True)
         ts(T.pm[:], bk[1][:, lo], 0.0, ALU.max, wr=["b1", "pm"])
-        mm(bk[2][:, lo], T.bo32[:], T.pc[:], False, False, ["pc"] + K, "b2")
-        turned(2, 0, T.nfT, "nfT", I8, True)
-        mm(bk[3][:, lo], T.bo32[:], T.pc[:], False, False, ["pc"] + K, "b3")
-        turned(3, 0, T.nfT, "nfT", I8, True)
-        mm(bk[5][:, lo], T.bo32[:], T.pm[:], False, True, ["pm"] + K, "b5")
+        turned(2, 0, T.nfT, "nfT", T.i18[:], False)
+        mm(bk[2][:, lo], T.bo32[:], T.pc[:], False, True, ["pc"] + K, "b2")
+        mm(bk[3][:, lo], T.bo32[:], T.pc[:], True, False, ["pc"] + K, "b3")
+        turned(3, 0, T.nfT, "nfT", T.i18[:], True)
         mm(bk[1][:, lo], In, T.od8[:], True, False, K, "b1")
         mm(bk[1][:, lo], T.bo32[:], T.pm[:], False, False, ["pm"] + K, "b1")
+        mm(bk[4][:, lo], T.bo32[:], T.pm[:], True, True, ["pm"] + K, "b4")
         scan(T.scl[:], T.rm[:], bk[2][:, lo], 131072.0, ALU.min, ALU.max, K, ["b2", "scl"])
-        cp(T.t1[:], T.scl[:, 15:256:16], ["scl"], ["t1"])
-        ts(T.t2[:], T.t1[:], 8191, ALU.bitwise_and, rd=["t1"], wr=["t2"])
-        tt(T.eq[:, 15, :], bk[3][:, lo], T.scl[:], ALU.is_equal, ["scl"], ["b3", "eq15"])
+        cp(T.cu[:], T.scl[:, 15:256:16], ["scl"], ["cu"])
         act(T.crs[:], bk[3][:, lo], ACT.Copy, wr=["b3", "crs"])
-        cp(T.cu[:], T.t2[:], ["t2"], ["cu"])
         act(T.yk[:], win.indirect(T.cu[:]), ACT.Copy, rd=XK + ["cu"], wr=["yk"])
-        scan(T.sml[:], T.rm[:], bk[5][:, lo], 131072.0, ALU.min, ALU.max, K, ["b5", "sml"])
+        tt(T.tg[:], win.indirect(T.cu[:]), T.z[:, par, :], ALU.min, XK + ["cu", zk], ["tg"])
+        tt(T.eq[:, 15, :], bk[3][:, lo], T.scl[:], ALU.is_equal, ["scl"], ["b3", "eq15"])
 
         def equal_rows(bank, rep, lst, outs, extra):
             segs, o = [], 0
@@ -504,7 +559,7 @@ def rank_program(g, core, T, topo):
                 segs.append((c, o))
                 o += 256 - c
             if NA:
-                act(T.eqa[:, 0:o], T.ad[:, 0:o], ACT.Relu, 1.0, -1.0, rd=["ad"], wr=["eqa"])
+                act(T.eqa[:, 0:o], T.ad[:, 0:o], ACT.Relu, 1.0, -4.0, rd=["ad"], wr=["eqa"])
             for j in range(15 - NA):
                 c = 16 * j + 16
                 ts(T.eq[:, j, c:256], bk[bank][:, c:256], T[lst][:, c - 1:c], ALU.is_equal, rd=[lst], wr=["b%d" % bank, "eq%d" % j])
@@ -523,9 +578,6 @@ def rank_program(g, core, T, topo):
         zn, znk = T.z[:, 1 - par, :], "z%d" % (1 - par)
 
         def amounts():
-            ts(T.mu[:], T.sml[:, 15:256:16], -8192.0, ALU.add, rd=["sml"], wr=["mu"])
-            act(T.hm[:], win.indirect(T.mu[:]), ACT.Copy, rd=XK + ["mu"], wr=["hm"])
-            mm(bk[4][:, lo], T.bo32[:], T.pm[:], True, True, ["pm"] + K, "b4")
             act(T.mrs[:], bk[4][:, lo], ACT.Copy, wr=["b4", "mrs"])
 
         def relist():
@@ -539,57 +591,91 @@ def rank_program(g, core, T, topo):
 
         def newz():
             if t < R - 1:
-                mm(bk[7][:, hi], sh(T.iw, dn), z, True, False, [zk] + K, "b7")
-                mm(bk[7][:, hi], sh(T.inw, dn), T.yk[:], False, True, ["yk"] + K, "b7")
                 mm(bk[6][:, lo], I, z, True, False, [zk] + K, "b6")
                 mm(bk[6][:, lo], In, T.yk[:], False, True, ["yk"] + K, "b6")
-                act(T.zf[:], bk[7][:, hi], ACT.Abs, wr=["b7", "zf"])
-                spread(range(16))
                 act(zn, bk[6][:, lo], ACT.Abs, wr=["b6", znk])
+                mm(bk[7][:, hi], sh(T.iw, dn), z, True, False, [zk] + K, "b7")
+                mm(bk[7][:, hi], sh(T.inw, dn), T.yk[:], False, True, ["yk"] + K, "b7")
+                act(T.zf[:], bk[7][:, hi], ACT.Abs, wr=["b7", "zf", "zf1"])
+                for h in range(2):
+                    for j in range(16 - h * ZA[t]):
+                        op("G", lambda q, j=j, h=h: q.affine_select(T.zrep[:, 2048 * h + j:2048 * h + 2048:16], T.zf[:, H[h]], [[0, 128]],
+                                                                    ALU.is_ge, 0.0, 0, 0), ["zf", "zf1"], ["zrep%d" % h])
 
         mm(bk[1][:, lo], sh(T.bo8, d), T.eq[:, 15, :], False, False, ["eq15"] + K, "b1")
-        equal_rows(3, "crs", "scl", [(1, 0, sh(T.bo8, d))], {0: amounts, 1: newz})
-        mm(bk[0][:, hi], sh(T.iw, -d), T.hm[:], True, True, ["hm"] + K, "b0")
-        relist()
-        tt(T.tg[:], win.indirect(T.cu[:]), z, ALU.min, XK + ["cu", zk], ["tg"])
-        scan(T.sm2[:], T.rm[:], bk[1][:, lo], 131072.0, ALU.min, ALU.max, K, ["b1", "sm2"])
-        tt(T.c1s[:], bk[1][:, lo], T.nod[:], ALU.is_lt, K, ["b1", "c1s"])
-        tt(T.eq[:, 15, :], bk[4][:, lo], T.sm2[:], ALU.is_equal, ["sm2"], ["b4", "eq15"])
-        tt(T.v0[:], bk[0][:, hi], T.tg[:], ALU.min, ["tg"], ["b0", "v0"])
-        if t < R - 1:
-            mm(bk[6][:, hi], I4, T.od[:], True, False, K, "b6")
-            mm(bk[6][:, hi], sh(T.bow, dn), zn, False, True, [znk] + K, "b6")
-            mm(bk[7][:, lo], I, zn, True, True, [znk] + K, "b7")
-        for _ in range(2):
-            mm(bk[2][:, hi], sh(T.i8w, -d), T.c1s[:], False, False, ["c1s"] + K, "b2")
-        mm(bk[2][:, hi], sh(T.bo8, -d), T.eq[:, 15, :], False, False, ["eq15"] + K, "b2")
-        mm(bk[0][:, lo], sh(T.iw, d), T.v0[:], True, True, ["v0"] + K, "b0")
+        equal_rows(3, "crs", "scl", [(1, 0, sh(T.bo8, d))], {JZ: newz, JZ + 1: amounts})
+
+        def second():
+            relist()
+            scan(T.sm2[:], T.rm[:], bk[1][:, lo], 131072.0, ALU.min, ALU.max, K, ["b1", "sm2"])
+            tt(T.c1s[:], bk[1][:, lo], T.nod[:], ALU.is_lt, K, ["b1", "c1s"])
+            cp(T.mu[:], T.sm2[:, 15:256:16], ["sm2"], ["mu"])
+            act(T.hm[:], win.indirect(T.mu[:]), ACT.Copy, rd=XK + ["mu"], wr=["hm"])
+            tt(T.eq[:, 15, :], bk[4][:, lo], T.sm2[:], ALU.is_equal, ["sm2"], ["b4", "eq15"])
+            for _ in range(2):
+                mm(bk[2][:, hi], sh(T.i8w, -d), T.c1s[:], False, False, ["c1s"] + K, "b2")
+            mm(bk[2][:, hi], sh(T.bo8, -d), T.eq[:, 15, :], False, False, ["eq15"] + K, "b2")
+
+        def farbal():
+            mm(bk[0][:, hi], sh(T.iw, -d), T.hm[:], True, True, ["hm"] + K, "b0")
+
+        def amount():
+            tt(T.v0[:], bk[0][:, hi], T.tg[:], ALU.min, ["tg"], ["b0", "v0"])
+            mm(bk[0][:, lo], sh(T.iw, d), T.v0[:], True, True, ["v0"] + K, "b0")
+
+        def weighted():
+            if t < R - 1:
+                c2 = 128 - 16 * (dn % 8)
+                for il in range(16):
+                    mm(bk[6][:, 0:16], T.bow[:, 16 - il + c2:144 - il + c2], T.z[:, 1 - par, il:256:16], il == 0, il == 15, [znk, "bow"] + K, "b6")
+                mm(bk[7][:, lo], I, zn, True, True, [znk] + K, "b7")
+
         thr = XO + W0 - 0.5
-        equal_rows(4, "mrs", "sm2", [(2, 256, sh(T.bo8, -d))], {})
+
+        def closings():
+            if gens:
+                act(T.sgb[:], T.crs[:], ACT.Sign, thr + P * gens[0] * (len(gens) - 1), -1.0, rd=["crs"], wr=["sgb"])
+                mm(bk[3][:, hi], I, T.yk[:], True, False, ["yk"] + K, "b3")
+                turned(3, 256, T.foT, "foT", I8, False)
+                mm(bk[3][:, hi], I8, T.sgb[:], False, True, ["sgb"] + K, "b3")
+            if len(gens) > 1:
+                act(T.sga[:], T.crs[:], ACT.Sign, -thr, 1.0, rd=["crs"], wr=["sga"])
+                mm(bk[5][:, hi], I, T.yk[:], True, False, ["yk"] + K, "b5")
+                turned(5, 256, T.foT, "foT", I8, False)
+                mm(bk[5][:, hi], I4, T.sgb[:], False, False, ["sgb"] + K, "b5")
+                mm(bk[5][:, hi], I4, T.sga[:], False, True, ["sga"] + K, "b5")
+
+        def given():
+            for n, u in enumerate(gens):
+                b = (3, 5)[n]
+                act(T["wh%d" % n][:], bk[b][:, hi], ACT.Relu, -8192.0, wr=["b%d" % b, "wh%d" % n])
+
+        def emptied():
+            for n, u in enumerate(gens):
+                b = (3, 5)[n]
+                blk = X[:, XO + W0 + P * u:XO + W0 + P * u + P]
+                mm(bk[b][:, lo], I, blk, True, False, XK + K, "b%d" % b)
+                mm(bk[b][:, lo], In, T["wh%d" % n][:], False, True, ["wh%d" % n] + K, "b%d" % b)
+            act(T.nv0[:], T.v0[:], ACT.Identity, 0.0, -1.0, rd=["v0"], wr=["nv0"])
+            for n, u in enumerate(gens):
+                b = (3, 5)[n]
+                act(X[:, XO + W0 + P * u:XO + W0 + P * u + P], bk[b][:, lo], ACT.Copy, wr=["b%d" % b, "X"])
+
+        closings()
+        second()
+        if GE:
+            given()
+        equal_rows(4, "mrs", "sm2", [(2, 256, sh(T.bo8, -d))], {JF: farbal if GE else lambda: (farbal(), given()), JV: amount, JE: emptied})
         relist2()
-        act(T.nv0[:], T.v0[:], ACT.Identity, 0.0, -1.0, rd=["v0"], wr=["nv0"])
-        if t < R - 1:
-            scan(T.sm2[:], T.rs[:], bk[6][:, hi], 0.0, ALU.add, ALU.min, K, ["b6", "sm2"])
-        if gens:
-            act(T.sgb[:], T.crs[:], ACT.Sign, thr + P * gens[0] * (len(gens) - 1), -1.0, rd=["crs"], wr=["sgb"])
-            mm(bk[3][:, hi], I, T.yk[:], True, False, ["yk"] + K, "b3")
-            turned(3, 256, T.foT, "foT", I8, False)
-            mm(bk[3][:, hi], I8, T.sgb[:], False, True, ["sgb"] + K, "b3")
-        if len(gens) > 1:
-            act(T.sga[:], T.crs[:], ACT.Sign, -thr, 1.0, rd=["crs"], wr=["sga"])
-            mm(bk[1][:, hi], I, T.yk[:], True, False, ["yk"] + K, "b1")
-            mm(bk[1][:, hi], I4, T.sgb[:], False, False, ["sgb"] + K, "b1")
-            mm(bk[1][:, hi], I4, T.sga[:], False, True, ["sga"] + K, "b1")
-        if gens:
-            act(T.wh0[:], bk[3][:, hi], ACT.Relu, -8192.0, wr=["b3", "wh0"])
         act(T.vf[:], bk[0][:, lo], ACT.Copy, wr=["b0", "vf"])
-        if len(gens) > 1:
-            act(T.wh1[:], bk[1][:, hi], ACT.Relu, -8192.0, wr=["b1", "wh1"])
         act(T.nvf[:], bk[0][:, lo], ACT.Identity, 0.0, -1.0, wr=["b0", "nvf"])
+        for j in range(16 - ZA[t], 16):
+            act(T.zrep[:, 2048 + j:4096:16], T.zf[:, H[1]], ACT.Copy, rd=["zf", "zf1"], wr=["zrepV"])
         scan(T.scl[:], T.rm[:], bk[2][:, hi], 131072.0, ALU.min, ALU.max, K, ["b2", "scl"])
         tt(T.nbs[:], bk[2][:, hi], T.nod[:], ALU.is_lt, K, ["b2", "nbs"])
         cp(T.cs[:, t, :], T.scl[:, 15:256:16], ["scl"], ["cs%d" % t])
         mm(bk[5][:, hi], sh(T.i8w, d), T.nbs[:], False, True, ["nbs"] + K, "b5")
+        weighted()
         mm(bk[4][:, hi], I, T.v0[:], True, False, ["v0"] + K, "b4")
         mm(bk[4][:, hi], I8, T.nbs[:], False, True, ["nbs"] + K, "b4")
         for n in range(len(gens)):
@@ -601,83 +687,107 @@ def rank_program(g, core, T, topo):
 
         tt(win.indirect(T.cs[:, t, :]), T.yk[:], T.nv0[:], ALU.add, ["X", "cs%d" % t, "yk", "nv0"], ["X"])
         act(X[:, wt:wt + P], bk[4][:, hi], ACT.Relu, wr=["b4", "Xnew"])
+        if t == 0:
+            make_selm(1, range(SL, 16))
         scan(T.sml[:], T.rm[:], bk[5][:, hi], 131072.0, ALU.min, ALU.max, K, ["b5", "sml"])
-        for n, u in enumerate(gens):
-            blk = X[:, XO + W0 + P * u:XO + W0 + P * u + P]
-            tt(blk, blk, T["wh%d" % n][:], ALU.subtract, ["X", "wh%d" % n], ["X"])
         cp(T.ms[:, t, :], T.sml[:, 15:256:16], ["sml"], ["ms%d" % t])
+        if t < R - 1:
+            cp(T.t3[:], bk[6][:, 0:16], [], ["b6", "t3"])
         tt(T.tg[:], win.indirect(T.ms[:, t, :]), T.vf[:], ALU.max, ["X", "ms%d" % t, "vf"], ["tg"])
+        if t < R - 1:
+            ts(T.bl[:], T.t3[:], 511, ALU.bitwise_and, rd=["t3"], wr=["bl0", "bl1"])
         tt(win.indirect(T.ms[:, t, :]), T.tg[:], T.nvf[:], ALU.add, ["X", "tg", "nvf"], ["X"])
+        if t < R - 1:
+            cp(T.bu[:], T.bl[:], ["bl0"], ["bu"])
         for n, u in enumerate(gens):
+            old = X[:, 0:XO + W0 + P * u]
             for lst, w_, u_ in ((T.cs, "wh%d" % n, "uh%d" % n), (T.ms, "wf%d" % n, "uf%d" % n)):
-                tt(T.tg[:], win.indirect(lst[:, u, :]), T[u_][:], ALU.min, ["X", u_], ["tg"])
-                tt(win.indirect(lst[:, u, :]), T.tg[:], T[w_][:], ALU.add, ["X", "tg", w_], ["X"])
+                tt(T.tg[:], old.indirect(lst[:, u, :]), T[u_][:], ALU.min, ["X", u_], ["tg"])
+                tt(old.indirect(lst[:, u, :]), T.tg[:], T[w_][:], ALU.add, ["X", "tg", w_], ["X", "XA%d" % n])
 
         be, bek = T.bexp[:, par, :], "bexp%d" % par
         cn = T.CN[:, s:A:2]
-        if t < 2:
-            act(T.Ls[:, s, :], cn, ACT.Copy, rd=["CN"], wr=["Ls%d" % s])
         mm(bk[0][:, hi], I, T.i256[:], True, False, K, "b0")
         mm(bk[0][:, hi], T.ones[0:11 + t, 0:128], T.c256[0:11 + t, :], False, False, K, "b0")
         mm(bk[0][:, hi], sh(T.bof, -d), be, False, False, [bek] + K, "b0")
         turned(0, 256, T.nek, "nek", I8, False)
+        aside = len(gens) == 2
+        if aside:
+            mm(bk[0][:, hi], T.in32[:], cn, False, False, ["CN"] + K, "b0")
         mm(bk[0][:, hi], I8, T.nbs[:], False, True, ["nbs"] + K, "b0")
-        if gens:
-            src, key = (T.Ls, "Ls%d" % s) if len(gens) == 1 else (T.Us, "Us%d" % s)
-            mm(bk[1][:, hi], T.i32[:], src[:, s, :], True, False, [key] + K, "b1")
+        if len(gens) == 1:
+            mm(bk[1][:, hi], T.i32[:], T.Ls[:, s, :], True, False, ["Ls%d" % s] + K, "b1")
             turned(1, 256, T.nek, "nek", I4, False)
             turned(1, 256, T.foT, "foT", I4, True)
+        if aside:
+            act(T.crs[:], bk[0][:, hi], ACT.Relu, wr=["b0", "crs"])
+            src, key = T.Us, "Us%d" % s
+            mm(bk[1][:, hi], T.i32[:], cn, True, False, ["CN"] + K, "b1")
+            mm(bk[1][:, hi], T.in32[:], src[:, s, :], False, False, [key] + K, "b1")
+            turned(1, 256, T.nek, "nek", I8, False)
+            turned(1, 256, T.foT, "foT", I8, True)
+            act(T.mrs[:], bk[1][:, hi], ACT.Relu, wr=["b1", "mrs"])
+            mm(bk[6][:, hi], T.i32[:], cn, True, False, ["CN"] + K, "b6")
+            mm(bk[6][:, hi], T.i32[:], T.crs[:], False, False, ["crs"] + K, "b6")
+            mm(bk[6][:, hi], T.in32[:], T.mrs[:], False, True, ["mrs"] + K, "b6")
+            act(T.sm2[:], bk[6][:, hi], ACT.Identity, MAGIC, wr=["b6", "sm2"])
+            if t < R - 1:
+                act(T.Cf[:, s:A:2], T.sm2[:], ACT.Identity, -MAGIC, rd=["sm2"], wr=["Cf"])
+                act(cn, bk[6][:, hi], ACT.Copy, wr=["b6", "CN"])
+            else:
+                act(cn, T.sm2[:], ACT.Identity, -MAGIC - 256, rd=["sm2"], wr=["CN"])
+                act(T.CN[:, 1 - s:A:2], T.Cf[:, 1 - s:A:2], ACT.Identity, -256.0, rd=["Cf"], wr=["CN"])
         if len(gens) == 1:
             mm(bk[7][:, hi], T.i32[:], cn, True, False, ["CN"] + K, "b7")
             turned(7, 256, T.nek, "nek", I8, False)
             mm(bk[7][:, hi], I8, T.nbs[:], False, True, ["nbs"] + K, "b7")
+        if aside and t < R - 1:
+            mm(bk[2][:, hi], T.i32[:], cn, True, False, ["CN"] + K, "b2")
+            mm(bk[2][:, hi], T.in32[:], T.Cf[:, s:A:2], False, True, ["Cf"] + K, "b2")
         c1 = 128 - 16 * ((-d) % 8)
         mm(bk[4][:, lo], T.zw[:, 16 + c1:144 + c1], be, True, False, [bek] + K, "b4")
         mm(bk[4][:, lo], T.zw32[:, 15:143], T.pc[:], False, False, ["pc"] + K, "b4")
         mm(bk[4][:, lo], T.zw32[:, 14 + c1:142 + c1], T.pm[:], False, False, ["pm"] + K, "b4")
         mm(bk[4][:, lo], I8, T.nbs[:], False, True, ["nbs"] + K, "b4")
-        act(T.recb[:, P * t:P * t + P], bk[4][:, lo], ACT.Relu, T.col[:, 6:7], rd=K, wr=["b4", "recb"])
+        def record(t=t):
+            act(T.recb[:, P * t:P * t + P], bk[4][:, lo], ACT.Relu, T.col[:, 6:7], rd=K, wr=["b4", "recb"])
+
         if t == R - 1:
+            record()
+        if t == R - 1:
+            dma("A", T.stf[:, :, 0:128], T.CN[:], ["CN"], ["stf3"])
+            for e in range(3):
+                dma("A", T.stf[:, :, 128 + 24 * e:152 + 24 * e], T.recb[e:128:16, :], ["recb"], ["stf%d" % e])
+            SF = ["stf0", "stf1", "stf2", "stf3"]
+            dma("A", T.lnf[me], T.stf[me], SF, ["lnfo"])
+            for c, (a, b) in enumerate(CH):
+                dma("S", T["sto%d" % c][:], X[:, XO + a:XO + b], XK if c else ["XA0", "Xnew"], ["sto%d" % c])
             for c in range(NCH):
-                xs = slice(XO + CW * c, XO + CW * c + CW)
-                dma("S", T["sto%d" % c][:], X[:, xs], XK, ["sto%d" % c])
-            for c in range(NCH):
-                xs = slice(XO + CW * c, XO + CW * c + CW)
                 exchange(3 + c, T["sto%d" % c], T["lno%d" % c], ["sto%d" % c], ["lno%d" % c])
-            dma("S", T.xo[r32, :], X[r32, XO:XO + 4096], XK, [])
-        if t == 0:
-            make_selm(1)
-        if gens:
-            tt(cn, bk[1][:, hi], cn, ALU.min, ["CN"], ["b1", "CN"])
-        if t < R - 1:
-            cp(T.t3[:], T.sm2[:, 15:256:16], ["sm2"], ["t3"])
-        tt(cn, bk[0][:, hi], cn, ALU.max, ["CN"], ["b0", "CN"])
-        if t < R - 1:
-            ts(T.bl[:], T.t3[:], 511, ALU.bitwise_and, rd=["t3"], wr=["bl0", "bl1"])
-        ts(T.Cf[:, s:A:2], cn, MAGIC, ALU.add, -MAGIC, ALU.add, rd=["CN"], wr=["Cf"])
-        if t < R - 1:
-            cp(T.bu[:], T.bl[:], ["bl0"], ["bu"])
+                if c == 0:
+                    exchange(2, T.stf, T.lnf, SF, ["lnf"])
+            dma("A", T.xo[r32, :], X[r32, XO:XO + 4096], XK + ["sto1", "sto2"], [])
+        if not aside:
+            if gens:
+                tt(cn, bk[1][:, hi], cn, ALU.min, ["CN"], ["b1", "CN"])
+            tt(cn, bk[0][:, hi], cn, ALU.max, ["CN"], ["b0", "CN"])
+            ts(T.Cf[:, s:A:2], cn, MAGIC, ALU.add, -MAGIC, ALU.add, rd=["CN"], wr=["Cf"])
             mm(bk[2][:, hi], T.i32[:], cn, True, False, ["CN"] + K, "b2")
             mm(bk[2][:, hi], T.in32[:], T.Cf[:, s:A:2], False, True, ["Cf"] + K, "b2")
+        if t < R - 1:
             nbs_ = [lambda s=s: act(T.Nb[:, s:A:2], bk[2][:, hi], ACT.Copy, wr=["b2", "Nb"])]
+            recs = [record]
             cp(T.Mu[:], T.Cf[:].indirect(T.bu[:]), ["Cf", "bu"], ["Mu"])
             late = [lambda par=par: payee(1 - par, ["bl0", "bl1"], False)]
             if len(gens) == 1:
-                tt(T.Us[:, s, :], bk[7][:, hi], T.Ls[:, s, :], ALU.max, ["Ls%d" % s], ["b7", "Us%d" % s])
+                late.append(lambda s=s: tt(T.Us[:, s, :], bk[7][:, hi], T.Ls[:, s, :], ALU.max, ["Ls%d" % s], ["b7", "Us%d" % s]))
             if t < R - 2:
                 late.append(lambda s=s: cp(T.Lu[:, s, :], T.Cf[:, s:A:2], ["Cf"], ["Lu%d" % s]))
 
-    ts(T.CN[:], T.Cf[:], -256.0, ALU.add, rd=["Cf"], wr=["CN"])
-    dma("A", T.stf[:, :, 0:128], T.CN[:], ["CN"], ["stf3"])
-    for e in range(3):
-        dma("A", T.stf[:, :, 128 + 24 * e:152 + 24 * e], T.recb[e:128:16, :], ["recb"], ["stf%d" % e])
-    SF = ["stf0", "stf1", "stf2", "stf3"]
-    exchange(2, T.stf, T.lnf, SF, ["lnf"])
-    dma("A", T.lnf[me], T.stf[me], SF, ["lnfo"])
     for c in range(NCH):
         for a, b in ((0, me), (me + 1, N)):
             if b > a:
-                dma("S", T.xo[32 * a:32 * b, CW * c:CW * c + CW], T["lno%d" % c][a:b], ["lno%d" % c], [])
+                dma("S", T.xo[32 * a:32 * b, CH[c][0]:CH[c][1]], T["lno%d" % c][a:b], ["lno%d" % c], [])
     dma("A", T.co[:], T.lnf[:, :, 0:128], ["lnf", "lnfo"], [])
     for e in range(3):
         dma("A", T.rec[8 * e:8 * e + 8, :], T.lnf[:, :, 128 + 24 * e:152 + 24 * e], ["lnf", "lnfo"], [])

@@ -1,3 +1,4 @@
+import math
 from concourse.bass import DstId, RemoteDMATransfer
 from concourse.mybir import AluOpType, ActivationFunctionType, AxisListType
 
@@ -6,22 +7,30 @@ ALU, ACT = AluOpType, ActivationFunctionType
 N = 4
 W0, P, R, A = 2560, 256, 6, 512
 WT = [1, 64, 5, 83, 17, 131, 29, 211, 43, 157, 61, 239, 71, 113, 97, 199]
-ZA = [8, 8, 4, 4, 0, 0]
-KRS = [7, 7, 7, 8, 8, 6]
-ORDER = "y0 d0 n0 r0 h0 p0 y1 m0 s0 P0 h1 d1 e0 E0 o0 r1 m1 p1 g0 b0 s1 B0 t0 P1 e1 o1 E1 l0 g1 f0 b1 B1"
-ORDER0 = "y0 d0 r0 h0 y1 m0 s0 h1 d1 n0 o0 r1 p0 m1 P0 s1 e0 t0 E0 p1 o1 g0 P1 b0 g1 f0 B0 e1 E1 l0 b1 B1 c0"
-JZ, JF, JV, JE = 0, 1, 3, 4
-GE = True
+KRS = [(8, 8)] * 6
+ORDER = ["y0 h0 n0 r0 y1 m0 h1 s0 p0 r1 b0 m1 s1 l0 p1 b1"] + ["y0 h0 r0 y1 m0 h1 n0 s0 r1 p0 b0 m1 s1 l0 p1 b1"] * 5
+FAST = True
+HA = False
+PASSES = 1
+WAKE = 150
+GAP = 100
+OVER = 200
+ZW = [8, 8, 4, 4, 0, 0]
+ZV = [2, 2, 0, 0, 0, 0]
+ASIDE = (5,)
 NP = 3
-SL = 6
-NA = 6
+NA = (4, 4)
 MAGIC = 1.5 * 2 ** 23
 XO = 256
+BIG = 8192.0
+LOW, MID = 2048.0, 2303.0
+OFF = MID + 15 * LOW
 CH = [(2816, 4096), (0, 1408), (1408, 2816)]
 NCH = len(CH)
 XH = W0 // 2
+NF = 56
 
-F, B, I32, U16 = "float32", "bfloat16", "int32", "uint16"
+F, B, I32, U16, H16 = "float32", "bfloat16", "int32", "uint16", "float16"
 SCRATCH = {
     "sti": ("dram", [N, 128, 132], I32), "lni": ("dram", [N, 128, 132], I32),
     "stn": ("dram", [N, 128, 128], B), "lnn": ("dram", [N, 128, 128], B), "plh": ("sbuf", [128, A + 160], I32),
@@ -29,33 +38,31 @@ SCRATCH = {
     "stc": ("dram", [N, 128, 320], B), "lnc": ("dram", [N, 128, 320], B),
     "stf": ("dram", [N, 128, 200], F), "lnf": ("dram", [N, 128, 200], F),
     "X": ("sbuf", [128, XO + 4096], B), "y": ("sbuf", [128, 4096], B), "mh": ("sbuf", [128, 4096], B),
-    "my": ("sbuf", [128, 4096], B), "zrep": ("sbuf", [128, 4096], B), "zf": ("sbuf", [128, 256], B),
-    "crs": ("sbuf", [128, 256], F), "mrs": ("sbuf", [128, 256], F), "ad": ("sbuf", [128, 2048], B), "eqa": ("sbuf", [128, 2048], B),
-    "i18": ("sbuf", [128, 128], B), "in32": ("sbuf", [128, 128], F),
-    "Eb": ("sbuf", [128, 4352], F), "d0": ("sbuf", [128, 1280], F), "So": ("sbuf", [128, 4416], F),
-    "selm": ("sbuf", [128, 4096], B), "nil": ("sbuf", [128, 512], B), "eq": ("sbuf", [128, 16, 256], B),
+    "my": ("sbuf", [128, 4096], B), "zrep": ("sbuf", [128, 4096], B), "zf": ("sbuf", [128, 2, 256], B),
+    "Eb": ("sbuf", [128, 4096], F), "ad": ("sbuf", [128, 2048], B), "eqa": ("sbuf", [128, 2048], B),
+    "in32": ("sbuf", [128, 128], F), "w2": ("sbuf", [128, 272], F), "d0": ("sbuf", [128, 1280], F), "So": ("sbuf", [128, 4416], F),
+    "selm": ("sbuf", [128, 4096], B), "nil": ("sbuf", [128, 512], B), "eq": ("sbuf", [128, 32, 256], B),
     "nmb": ("sbuf", [128, W0], B), "pli": ("sbuf", [128, A], I32), "plu": ("sbuf", [128, A], U16),
     "CN": ("sbuf", [128, A], F), "Cf": ("sbuf", [128, A], F), "Nb": ("sbuf", [128, A], B),
-    "Lu": ("sbuf", [128, 2, 256], U16), "Mu": ("sbuf", [128, 256], U16), "Mf": ("sbuf", [128, 256], F), "NM": ("sbuf", [128, 256], B),
-    "Ls": ("sbuf", [128, 2, 256], F), "Us": ("sbuf", [128, 2, 256], F), "recb": ("sbuf", [128, 1536], F), "nod": ("sbuf", [128, 256], B),
-    "z": ("sbuf", [128, 2, 256], B), "bexp": ("sbuf", [128, 2, 256], B), "Gs": ("sbuf", [128, 256], F),
-    "bi": ("sbuf", [128, 16], I32), "ki": ("sbuf", [128, 16], I32), "li": ("sbuf", [128, 16], I32), "lf": ("sbuf", [128, 16], F),
-    "t3": ("sbuf", [128, 16], I32), "bl": ("sbuf", [128, 16], I32),
+    "Lu": ("sbuf", [128, 2, 256], U16), "Mu": ("sbuf", [128, 256], U16), "NM": ("sbuf", [128, 256], B),
+    "Ls": ("sbuf", [128, 2, 256], F), "Us": ("sbuf", [128, 2, 256], F), "recb": ("sbuf", [128, 1536], F),
+    "wh": ("sbuf", [128, 2, 256], B), "wf": ("sbuf", [128, 2, 256], B), "uh": ("sbuf", [128, 2, 256], B), "uf": ("sbuf", [128, 2, 256], B),
+    "z": ("sbuf", [128, 2, 256], B), "r16": ("sbuf", [128, 2, 256], U16),
+    "bi": ("sbuf", [128, 16], I32), "it": ("sbuf", [128, 48], I32), "PT": ("sbuf", [128, 112], B), "lf": ("sbuf", [128, 16], F),
+    "t3": ("sbuf", [128, 32], I32), "bl": ("sbuf", [128, 32], I32),
     "bc": ("sbuf", [128, 16], F), "bu": ("sbuf", [128, 16], U16), "cu": ("sbuf", [128, 16], U16), "mu": ("sbuf", [128, 16], U16),
-    "cs": ("sbuf", [128, R, 16], U16), "ms": ("sbuf", [128, R, 16], U16), "ex": ("sbuf", [128, 3, 16], U16), "exi": ("sbuf", [128, 3, 16], I32),
-    "iw": ("sbuf", [128, 256], B), "inw": ("sbuf", [128, 256], B), "i8w": ("sbuf", [128, 256], B), "i4": ("sbuf", [128, 128], B),
-    "i32": ("sbuf", [128, 128], F), "bo": ("sbuf", [128, 256], B), "bo8": ("sbuf", [128, 256], B), "bo32": ("sbuf", [128, 128], F),
-    "bop": ("sbuf", [128, 256], B), "bon": ("sbuf", [128, 256], B), "bof": ("sbuf", [128, 256], B), "bow": ("sbuf", [128, 272], B),
-    "zw": ("sbuf", [128, 272], B), "zw32": ("sbuf", [128, 272], F), "od": ("sbuf", [128, 256], B), "od8": ("sbuf", [128, 256], B),
-    "dm": ("sbuf", [128, 256], B), "rm": ("sbuf", [128, 256], F), "i16": ("sbuf", [128, 256], F),
-    "i256": ("sbuf", [128, 256], B), "c256": ("sbuf", [128, 256], B), "ones": ("sbuf", [128, 256], B),
-    "w1": ("sbuf", [128, 272], F), "col": ("sbuf", [128, 16], F),
-    "coli": ("sbuf", [128, 4], I32), "wrow": ("sbuf", [128, 32], F),
+    "cs": ("sbuf", [128, R, 16], U16), "ms": ("sbuf", [128, R, 16], U16), "ex": ("sbuf", [128, 16], U16),
+    "i4": ("sbuf", [128, 128], B), "i32": ("sbuf", [128, 128], F), "bow": ("sbuf", [128, 272], B),
+    "zw": ("sbuf", [128, 272], B), "zw32": ("sbuf", [128, 272], F), "zw16": ("sbuf", [128, 272], H16), "bo16": ("sbuf", [128, 128], H16),
+    "pc": ("sbuf", [128, 256], H16), "pm": ("sbuf", [128, 256], H16),
+    "w1": ("sbuf", [128, 272], F), "col": ("sbuf", [128, 16], F), "oh": ("sbuf", [128, 32], F),
+    "coli": ("sbuf", [128, 8], I32), "wrow": ("sbuf", [128, 32], F),
 }
-for _n in ["nek", "nel", "nfT", "foT", "yk", "hm", "v0", "nv0", "vf", "nvf", "c1s", "nbs", "sga", "sgb", "tg",
-           "wh0", "wh1", "wf0", "wf1", "uh0", "uh1", "uf0", "uf1"]:
+for _n in ["FL", "ya", "yk", "hm", "cn", "vf", "nvf", "nbs", "sga", "sgb", "tg",
+           "iw", "inw", "i8w", "bo", "bo8", "bop", "bon", "od", "od8", "dm", "i256", "c256", "ones",
+           "Sel", "SG", "LP", "WC", "KW", "KN", "WQ", "WR"]:
     SCRATCH[_n] = ("sbuf", [128, 256], B)
-for _n in ["pc", "pm", "scl", "sml", "sm2"]:
+for _n in ["scl", "sml", "sm2", "crs", "mrs", "Gs", "Mf", "rm", "i16"]:
     SCRATCH[_n] = ("sbuf", [128, 256], F)
 for _c in range(NCH):
     SCRATCH["sto%d" % _c] = ("dram", [N, 128, (CH[_c][1] - CH[_c][0]) // 4], B)
@@ -84,56 +91,108 @@ def engine_split(core, peers, topo):
 
 def apart(k):
     return (len(k) == 2 and k[0] == "b" and k[1].isdigit()) or k.rstrip("01") in (
-        "K", "KA", "KB", "So", "zrep", "zrepV", "ad", "mym", "myr", "wrow", "selm", "recb")
+        "K", "KA", "KB", "KF", "So", "zrep", "zrepV", "ad", "mym", "myr", "wrow", "selm", "recb", "bi")
 
 
-def emit(g, T, ops):
-    Q = {"V": g.vector, "A": g.scalar, "T": g.tensor, "G": g, "S": g.sync}
-    lastw, readers, clock, pos, need, waits = {}, {}, {k: {} for k in Q}, {k: 0 for k in Q}, set(), []
-    done = []
-    for i, (e, fn, rd, wr, sig) in enumerate(ops):
-        deps = set()
-        for k in rd:
-            if k in lastw:
-                deps.add(lastw[k])
+def arrange(ops, lazy):
+    lastw, readers, sure, after = {}, {}, [], []
+    for i, (e, fn, rd, wr, sig, busy, lat) in enumerate(ops):
+        s, a = set(lastw[k] for k in rd if k in lastw), set()
         for k in wr:
             j = lastw.get(k)
-            if j is not None and (ops[j][0] != e or ops[j][4] is not None or sig is not None or not apart(k)):
-                deps.add(j)
-            deps.update(readers.get(k, []))
-        mine = []
-        if e is not None:
-            ck = clock[e]
-            for j in sorted(deps, reverse=True):
-                src, val, know = done[j]
-                if ck.get(src, -1) >= val:
-                    continue
-                mine.append(j)
-                need.add(j)
-                for a, b in know.items():
-                    ck[a] = max(ck.get(a, -1), b)
-                ck[src] = val
-            pos[e] += 1
-        waits.append(mine)
-        done.append((e if sig is None else sig[0], pos[e] if sig is None else 0, dict(clock[e]) if e is not None else {}))
+            if j is not None:
+                weak = k[:2] == "o:" or (ops[j][0] == e and ops[j][4] is None and sig is None and apart(k))
+                (a if weak else s).add(j)
+            s.update(readers.get(k, []))
+        sure.append(s)
+        after.append(a - s)
         for k in rd:
             readers.setdefault(k, []).append(i)
         for k in wr:
             lastw[k] = i
             readers[k] = []
-    last = {}
-    for i, o in enumerate(ops):
-        if o[0] is not None and o[4] is None:
-            last[o[0]] = i
+
+    def gap(j, i, strong):
+        return ops[j][5] + (ops[j][6] + WAKE if strong else 0)
+
+    rank = [len(ops) if i in lazy else i for i in range(len(ops))]
+    for i in range(len(ops) - 1, -1, -1):
+        for j in sure[i] | after[i]:
+            rank[j] = min(rank[j], rank[i])
+    ahead, behind = [[] for _ in ops], [[] for _ in ops]
+    for i in range(len(ops)):
+        for js, strong in ((sure[i], True), (after[i], False)):
+            for j in js:
+                ahead[i].append((j, gap(j, i, strong)))
+                behind[j].append((i, gap(j, i, strong) + ops[i][5] - ops[j][5]))
+
+    def place(turn, edges, first):
+        start, slots = [0.0] * len(ops), {}
+        for i in turn:
+            t = max([first[i]] + [start[j] + w for j, w in edges[i]])
+            if ops[i][0] is not None:
+                sl = slots.setdefault(ops[i][0], [])
+                n = bisect(sl, t)
+                while n < len(sl) and sl[n][0] < t + min(ops[i][5], max(GAP, ops[i][5] - OVER)):
+                    t = max(t, sl[n][1])
+                    n += 1
+                sl.insert(n, (t, min([t + ops[i][5]] + [x[0] for x in sl[n:n + 1]])))
+            start[i] = t
+        return start
+
+    every, zero = range(len(ops)), [0.0] * len(ops)
+    start = place(sorted(every, key=lambda i: (rank[i], i)), ahead, zero)
+    for _ in range(PASSES):
+        back = place(sorted(every, key=lambda i: (-start[i] - ops[i][5], -i)), behind, [o[6] for o in ops])
+        start = place(sorted(every, key=lambda i: (-back[i] - ops[i][5], i)), ahead, zero)
+    return sure, sorted(every, key=lambda i: (start[i], i))
+
+
+def bisect(slots, t):
+    a, b = 0, len(slots)
+    while a < b:
+        m = (a + b) // 2
+        if slots[m][1] > t:
+            b = m
+        else:
+            a = m + 1
+    return a
+
+
+def emit(g, T, ops, lazy):
+    Q = {"V": g.vector, "A": g.scalar, "T": g.tensor, "G": g, "S": g.sync}
+    sure, order = arrange(ops, lazy)
+    place = {i: n for n, i in enumerate(order)}
+    clock, pos, need, waits, done, last = {k: {} for k in Q}, {k: 0 for k in Q}, set(), {}, {}, {}
+    for i in order:
+        e, sig = ops[i][0], ops[i][4]
+        waits[i] = []
+        if e is not None:
+            ck = clock[e]
+            for j in sorted(sure[i], key=lambda j: -place[j]):
+                src, val, know = done[j]
+                if ck.get(src, -1) >= val:
+                    continue
+                waits[i].append(j)
+                need.add(j)
+                for a, b in know.items():
+                    ck[a] = max(ck.get(a, -1), b)
+                ck[src] = val
+            pos[e] += 1
+            if sig is None:
+                last[e] = i
+        done[i] = (e if sig is None else sig[0], pos[e] if sig is None else 0, dict(clock[e]) if e is not None else {})
     need |= set(last.values())
     cnt, at = {k: 0 for k in Q}, {}
-    for i, (e, fn, rd, wr, sig) in enumerate(ops):
+    for i in order:
+        e, sig = ops[i][0], ops[i][4]
         if sig is not None:
             at[i] = sig
         elif i in need:
             cnt[e] += 1
             at[i] = ("s" + e, cnt[e])
-    for i, (e, fn, rd, wr, sig) in enumerate(ops):
+    for i in order:
+        e, fn, sig = ops[i][0], ops[i][1], ops[i][4]
         if e is None:
             continue
         for j in waits[i]:
@@ -144,7 +203,7 @@ def emit(g, T, ops):
                 ins.then_inc(T.sem[sig[0]], 16)
         elif i in need:
             ins.then_inc(T.sem[at[i][0]], 1)
-    for i, o in enumerate(ops):
+    for o in ops:
         if o[4] is not None:
             g.wait_ge(T.sem[o[4][0]], o[4][1])
     for k in cnt:
@@ -160,16 +219,23 @@ def rank_program(g, core, T, topo):
     peers = [c for c in cores if c != core]
     mine = engine_split(core, peers, topo)
     arrive = sum(len(engine_split(c, [x for x in cores if x != c], topo)[core]) for c in peers)
-    ops, nd, stops = [], [0], set()
+    ops, nd, stops, lazy = [], [0], set(), set()
+    GATHER, SCATTER = 1.4, 3.0
 
-    def op(e, fn, rd, wr):
-        ops.append((e, fn, list(rd), list(wr), None))
+    def aside(fn, *args):
+        n = len(ops)
+        fn(*args)
+        lazy.update(range(n, len(ops)))
 
-    def dma(e, out, in_, rd, wr):
-        ops.append((e, lambda q: q.dma_start(out, in_), list(rd), list(wr), ("d%d" % nd[0], 16)))
+    def op(e, fn, rd, wr, n):
+        busy = {"V": 55 + 0.87 * n, "A": 70 + 0.87 * n, "T": 10 + 0.44 * n, "G": 170 + 0.87 * n}[e]
+        ops.append((e, fn, list(rd), list(wr), None, busy, 0))
+
+    def dma(e, out, in_, rd, wr, kb):
+        ops.append((e, lambda q: q.dma_start(out, in_), list(rd), list(wr) + ["o:" + e], ("d%d" % nd[0], 16), 60, 2000 + 8 * kb))
         nd[0] += 1
 
-    def exchange(n, st, ln, rd, wr):
+    def exchange(n, st, ln, rd, wr, kb):
         def fn(q):
             tr = []
             for c in peers:
@@ -177,223 +243,220 @@ def rank_program(g, core, T, topo):
                 tr.append(RemoteDMATransfer(dst_ids=[DstId(rid=rid, pnc=pid)], dma_engine_mask=sum(1 << e for e in mine[c]),
                                             remote_sem=T.sem["ar%d" % n], src=st[T.rank_of(c)], dst=ln[me]))
             return q.remote_dma_fused(tr, local_sem=T.sem["ls%d" % n])
-        ops.append(("G", fn, list(rd), [], ("ls%d" % n, sum(len(v) for v in mine.values()))))
-        ops.append((None, None, [], list(wr), ("ar%d" % n, arrive)))
+        ops.append(("G", fn, list(rd), ["o:G", "o:x%d" % n], ("ls%d" % n, sum(len(v) for v in mine.values())), 600, 3000 + 30 * kb))
+        ops.append((None, None, [], list(wr) + ["o:x%d" % n], ("ar%d" % n, arrive), 1, 3000 + 30 * kb))
 
-    def ts(out, in0, s1, o0, s2=None, o1=None, rd=(), wr=()):
+    def ts(out, in0, s1, o0, s2=None, o1=None, rd=(), wr=(), n=256):
         if o1 is None:
-            op("V", lambda q: q.tensor_scalar(out, in0, s1, None, o0), rd, wr)
+            op("V", lambda q: q.tensor_scalar(out, in0, s1, None, o0), rd, wr, n)
         else:
-            op("V", lambda q: q.tensor_scalar(out, in0, s1, s2, o0, o1), rd, wr)
+            op("V", lambda q: q.tensor_scalar(out, in0, s1, s2, o0, o1), rd, wr, n)
 
-    def tt(out, in0, in1, o, rd=(), wr=()):
-        op("V", lambda q: q.tensor_tensor(out, in0, in1, o), rd, wr)
+    def tt(out, in0, in1, o, rd=(), wr=(), n=256):
+        op("V", lambda q: q.tensor_tensor(out, in0, in1, o), rd, wr, n)
 
-    def cp(out, in_, rd=(), wr=()):
-        op("V", lambda q: q.tensor_copy(out, in_), rd, wr)
+    def cp(out, in_, rd=(), wr=(), n=256):
+        op("V", lambda q: q.tensor_copy(out, in_), rd, wr, n)
 
-    def ms(ap, v, wr):
-        op("V", lambda q: q.memset(ap, v), [], wr)
+    def ms(ap, v, wr, n=16):
+        op("V", lambda q: q.memset(ap, v), [], wr, n)
 
-    def scan(out, a, b, init, o0, o1, rd=(), wr=()):
-        op("V", lambda q: q.tensor_tensor_scan(out, a, b, init, o0, o1), rd, wr)
+    def scan(out, a, b, init, o0, o1, rd=(), wr=(), n=256):
+        op("V", lambda q: q.tensor_tensor_scan(out, a, b, init, o0, o1), rd, wr, n)
 
-    def act(out, in_, func, bias=0.0, scale=1.0, rd=(), wr=()):
+    def act(out, in_, func, bias=0.0, scale=1.0, rd=(), wr=(), n=256):
         if func == ACT.Copy:
-            op("A", lambda q: q.activation(out, in_, func), rd, wr)
+            op("A", lambda q: q.activation(out, in_, func), rd, wr, n)
         else:
-            op("A", lambda q: q.activation(out, in_, func, bias=bias, scale=scale), rd, wr)
+            op("A", lambda q: q.activation(out, in_, func, bias=bias, scale=scale), rd, wr, n)
 
-    def mm(out, lhsT, rhs, st, sp, rd, bank):
+    def mm(out, lhsT, rhs, st, sp, rd, bank, n=256):
         def fn(q):
             return q.matmul(out, lhsT, rhs, st, sp or fn in stops)
-        op("T", fn, rd, [bank])
+        op("T", fn, rd, [bank], max(64, n))
 
-    def iota(out, pat, base, cm, wr, flt=True):
+    def iota(out, pat, base, cm, wr, flt=True, rd=()):
+        n = 2 * math.prod(p[1] for p in pat)
         if flt:
-            op("G", lambda q: q.iota(out, pat, base, cm, allow_small_or_imprecise_dtypes=True), [], wr)
+            op("G", lambda q: q.iota(out, pat, base, cm, allow_small_or_imprecise_dtypes=True), rd, wr, n)
         else:
-            op("G", lambda q: q.iota(out, pat, base, cm), [], wr)
+            op("G", lambda q: q.iota(out, pat, base, cm), rd, wr, n)
 
-    def sh(w, d):
+    def sh(w, d, p=128):
         c = 128 - 16 * (d % 8)
-        return w[:, c:c + 128]
+        return w[0:p, c:c + 128]
 
     bk = [T["pb%d" % i] for i in range(8)]
     X, I, In, I8, I4 = T.X, T.iw[:, 128:256], T.inw[:, 128:256], T.i8w[:, 128:256], T.i4[:]
     lo, hi = slice(0, 256), slice(256, 512)
     H = [slice(0, 128), slice(128, 256)]
     r32 = slice(32 * me, 32 * me + 32)
+    G256, S256 = 256 * GATHER, 256 * SCATTER
 
-    ms(T.nmb[:], 0.0, ["nm0"])
-    dma("S", T.plh[:, A:A + 160], T.fr0[:], [], ["nm"])
-    dma("A", T.stb[:, :, 0:320], T.x0[:, 0:XH], [], ["stb0"])
-    dma("S", T.stb[:, :, 320:384], T.z0[:], [], ["stb1"])
-    dma("A", T.plh[:, 0:A], T.pl[:], [], ["plh"])
-    dma("S", T.sti[:, :, 0:128], T.pl[:], [], ["sti0"])
-    dma("S", T.sti[:, :, 128:132], T.b0[:], [], ["sti2"])
-    dma("A", T.stc[:], T.x0[:, XH:W0], [], ["stc"])
-    dma("A", T.lni[me, :, 0:128], T.pl[r32, :], [], ["lni0"])
-    dma("A", T.lni[me, :, 128:132], T.b0[r32, :], [], ["lni2"])
-    dma("S", T.lnb[me, :, 320:384], T.z0[r32, :], [], ["lnb1"])
+    ms(T.nmb[:], 0.0, ["nm0"], 1280)
+    dma("S", T.plh[:, A:A + 160], T.fr0[:], [], ["nm"], 80)
+    dma("A", T.stb[:, :, 0:320], T.x0[:, 0:XH], [], ["stb0"], 320)
+    dma("S", T.stb[:, :, 320:384], T.z0[:], [], ["stb1"], 64)
+    dma("A", T.plh[:, 0:A], T.pl[:], [], ["plh"], 256)
+    dma("S", T.sti[:, :, 0:128], T.pl[:], [], ["sti0"], 256)
+    dma("S", T.sti[:, :, 128:132], T.b0[:], [], ["sti2"], 64)
+    dma("A", T.stc[:], T.x0[:, XH:W0], [], ["stc"], 500)
+    dma("A", T.lni[me, :, 0:128], T.pl[r32, :], [], ["lni0"], 64)
+    dma("A", T.lni[me, :, 128:132], T.b0[r32, :], [], ["lni2"], 16)
+    dma("S", T.lnb[me, :, 320:384], T.z0[r32, :], [], ["lnb1"], 16)
 
     iota(T.coli[:, 0:1], [[0, 1]], 0, 1, ["coli0"], False)
     iota(T.w1[:, 0:256], [[0, 2], [1, 128]], 0, 0, ["w1"])
-    iota(T.Eb[:, 0:256], [[0, 2], [1, 8], [0, 16]], 0, 0, ["w2"])
+    iota(T.w2[:, 0:256], [[0, 2], [1, 8], [0, 16]], 0, 0, ["w2"])
     iota(T.i16[:], [[0, 16], [1, 16]], 0, 0, ["i16"])
     iota(T.So[:, 0:272], [[1, 272]], -16, 0, ["w3"])
-    exchange(1, T.stb, T.lnb, ["stb0", "stb1"], ["lnb"])
-    exchange(0, T.sti, T.lni, ["sti0", "sti2"], ["lni"])
-    exchange(4 + NCH, T.stc, T.lnc, ["stc"], ["lnc"])
-    iota(T.exi[:, 0, :], [[1, 16]], 0, 0, ["exi"], False)
-    for s in range(2):
-        d = 2 * (1 + s)
-        for h in range(2):
-            iota(T.exi[:, 1 + s, 8 * h:8 * h + d], [[1, d]], 8 * h + 8 - d, 0, ["exi"], False)
-            iota(T.exi[:, 1 + s, 8 * h + d:8 * h + 8], [[1, 8 - d]], 8 * h, 0, ["exi"], False)
-    iota(T.lf[:], [[-16, 16]], 255, 0, ["lf"])
-    iota(T.i256[:], [[1, 256]], 0, 0, ["i256"])
-    cp(T.col[:, 0:1], T.coli[:, 0:1], ["coli0"], ["colp"])
-    ts(T.coli[:, 1:2], T.coli[:, 0:1], 4, ALU.arith_shift_right, rd=["coli0"], wr=["coli1"])
-    ts(T.coli[:, 2:3], T.coli[:, 0:1], 15, ALU.bitwise_and, rd=["coli0"], wr=["coli2"])
-    cp(T.col[:, 1:3], T.coli[:, 1:3], ["coli1", "coli2"], ["colg"])
+    exchange(1, T.stb, T.lnb, ["stb0", "stb1"], ["lnb"], 96)
+    exchange(0, T.sti, T.lni, ["sti0", "sti2"], ["lni"], 66)
+    exchange(4 + NCH, T.stc, T.lnc, ["stc"], ["lnc"], 80)
+    iota(T.lf[:], [[-16, 16]], 255 - int(OFF), 0, ["lf"])
+    iota(T.i256[:], [[1, 256]], 0, 0, ["KG"])
+    cp(T.col[:, 0:1], T.coli[:, 0:1], ["coli0"], ["colp"], 1)
+    for c, (v, o) in enumerate(((4, ALU.arith_shift_right), (15, ALU.bitwise_and), (3, ALU.arith_shift_right), (7, ALU.bitwise_and))):
+        ts(T.coli[:, 1 + c:2 + c], T.coli[:, 0:1], v, o, rd=["coli0"], wr=["coli%d" % (1 + c)], n=1)
+    cp(T.col[:, 1:5], T.coli[:, 1:5], ["coli1", "coli2", "coli3", "coli4"], ["colg"], 4)
     cp_, cg, ce = T.col[:, 0:1], T.col[:, 1:2], T.col[:, 2:3]
     ts(T.iw[:], T.w1[:, 0:256], cp_, ALU.is_equal, rd=["w1", "colp"], wr=["iw"])
-    ts(T.bo[:], T.Eb[:, 0:256], cg, ALU.is_equal, rd=["w2", "colg"], wr=["bo"])
-    ts(T.hm[:, 0:160], T.plh[:, A:A + 160], -256.0, ALU.add, 1.0 / 1024, ALU.mult, rd=["nm"], wr=["hm"])
-    dma("S", T.nmb[0:128:16, :], T.hm[:, 0:160], ["nm0", "hm"], ["nmb"])
-    dma("S", X[r32, XO:XO + W0], T.x0[r32, :], ["stc"], ["Xown"])
-    ts(T.wrow[:, 16:32], T.i16[:, 0:16], ce, ALU.is_equal, 2.0 ** 32, ALU.mult, rd=["i16", "colg"], wr=["rowm"])
+    ts(T.bo[:], T.w2[:, 0:256], cg, ALU.is_equal, rd=["w2", "colg"], wr=["bo"])
+    ts(T.Sel[:], T.w2[:, 0:256], T.col[:, 4:5], ALU.is_equal, rd=["w2", "colg"], wr=["Sel"])
+    ts(T.hm[:, 0:160], T.plh[:, A:A + 160], -256.0, ALU.add, 1.0 / 1024, ALU.mult, rd=["nm"], wr=["hm"], n=160)
+    dma("S", T.nmb[0:128:16, :], T.hm[:, 0:160], ["nm0", "hm"], ["nmb"], 40)
+    dma("S", X[r32, XO:XO + W0], T.x0[r32, :], ["stc"], ["Xown"], 160)
+    ts(T.wrow[:, 16:32], T.i16[:, 0:16], ce, ALU.is_equal, 2.0 ** 32, ALU.mult, rd=["i16", "colg"], wr=["rowm"], n=16)
     act(T.inw[:], T.iw[:], ACT.Identity, 0.0, -1.0, rd=["iw"], wr=["KA"])
     act(X[:, 0:XO], T.iw[:], ACT.Identity, 0.0, 0.0, rd=["iw"], wr=["X"])
+    for j in range(4):
+        act(T.nil[:, j:512:4], T.iw[:, 0:128], ACT.Identity, 0.0, -2.0 ** 32, rd=["iw"], wr=["KA"], n=128)
+    for out, v in ((T.bop, 512.0), (T.bon, -512.0)):
+        act(out[:], T.bo[:], ACT.Identity, 0.0, v, rd=["bo"], wr=["KA"])
 
-    def scaled(part):
-        if part == 0:
-            for j in range(4):
-                act(T.nil[:, j:512:4], T.iw[:, 0:128], ACT.Identity, 0.0, -2.0 ** 32, rd=["iw"], wr=["KA"])
-            for out, v in ((T.bop, 512.0), (T.bon, -512.0)):
-                act(out[:], T.bo[:], ACT.Identity, 0.0, v, rd=["bo"], wr=["KA"])
-        elif part == 2:
-            for out, v in ((T.bo8, -8192.0), (T.bof, 1.0 / 1024)):
-                act(out[:], T.bo[:], ACT.Identity, 0.0, v, rd=["bo"], wr=["KB"])
-            for out, v, n in ((T.i8w, -8192.0, 256), (T.i4, 4096.0, 128), (T.i32, 1.0, 128), (T.in32, -1.0, 128)):
-                act(out[:, 0:n], T.iw[:, 0:n], ACT.Identity, 0.0, v, rd=["iw"], wr=["KB"])
-            act(T.bo32[:], T.bo[:, 0:128], ACT.Copy, rd=["bo"], wr=["KB"])
-        else:
-            ts(T.od8[:], T.od[:], -8192.0, ALU.add, rd=["od"], wr=["K"])
-            ts(T.i18[:], T.iw[:, 0:128], 0.125, ALU.mult, rd=["iw"], wr=["K"])
-            ts(T.nod[:], T.od[:], -1.0, ALU.mult, rd=["od"], wr=["K"])
-
-
-    def make_selm(s, ls=range(16)):
-        for l in ls:
+    def make_selm(s):
+        for l in range(16):
             c = 2048 * s + 512 * (l // 4)
-            act(T.selm[:, c + l % 4:c + 512:4], sh(T.bo, -2 * (1 + s)), ACT.Identity, 0.0, T.wrow[:, 16 + l:17 + l], rd=["rowm", "bo"], wr=["selm%d" % s])
+            act(T.selm[:, c + l % 4:c + 512:4], sh(T.bo, -2 * (1 + s)), ACT.Identity, 0.0, T.wrow[:, 16 + l:17 + l], rd=["rowm", "bo"], wr=["selm%d" % s], n=128)
     ts(T.od[:], T.i16[:], ce, ALU.not_equal, 32768.0, ALU.mult, rd=["i16", "colg"], wr=["od"])
 
-    cp(T.plu[:], T.plh[:, 0:A], ["plh"], ["plu"])
-    scaled(0)
-    make_selm(0, range(6))
+    cp(T.plu[:], T.plh[:, 0:A], ["plh"], ["plu"], 512)
     for h in range(2):
-        act(T.mh[:, 2048 * h:2048 * h + 2048], T.nmb[:].indirect(T.plu[:, 256 + 128 * h:384 + 128 * h]), ACT.Copy, rd=["nmb", "plu"], wr=["mh%d" % h])
-    ts(T.col[:, 5:6], cg, 16.0, ALU.mult, rd=["colg"], wr=["col5"])
+        act(T.mh[:, 2048 * h:2048 * h + 2048], T.nmb[:].indirect(T.plu[:, 256 + 128 * h:384 + 128 * h]), ACT.Copy, rd=["nmb", "plu"], wr=["mh%d" % h], n=8 * G256)
+    ts(T.col[:, 5:6], cg, 16.0, ALU.mult, rd=["colg"], wr=["col5"], n=1)
     ts(T.w1[:], T.So[:, 0:272], T.col[:, 5:6], ALU.subtract, rd=["w3", "col5"], wr=["w1"])
-    ts(T.Eb[:, 0:272], T.w1[:], 0.0, ALU.is_equal, rd=["w1"], wr=["w2"])
+    ts(T.w2[:], T.w1[:], 0.0, ALU.is_equal, rd=["w1"], wr=["w2"])
     ts(T.So[:, 0:272], T.w1[:], 128.0, ALU.is_equal, rd=["w1"], wr=["w3"])
-    tt(T.zw32[:], T.Eb[:, 0:272], T.So[:, 0:272], ALU.add, ["w2", "w3"], ["zw32"])
+    tt(T.zw32[:], T.w2[:], T.So[:, 0:272], ALU.add, ["w2", "w3"], ["zw32"], 544)
     cp(T.zw[:], T.zw32[:], ["zw32"], ["zw"])
     for h in range(2):
-        cp(T.my[:, 2048 * h:2048 * h + 2048], T.nmb[:].indirect(T.plu[:, H[h]]), ["nmb", "plu"], ["myn%d" % h])
+        cp(T.my[:, 2048 * h:2048 * h + 2048], T.nmb[:].indirect(T.plu[:, H[h]]), ["nmb", "plu"], ["myn%d" % h], 8 * G256)
     for h in range(2):
-        for c, buf, keys in ((1, T.mh, ["mh%d" % h]), (0, T.my, ["myn%d" % h, "myr0", "myr1", "mym0", "mym1"])):
+        for c, buf, keys in ((1, T.mh, ["mh%d" % h]), (0, T.my, ["myn%d" % h, "mym%d" % h] + ["myr%d%d" % (h, n) for n in range(4)])):
             b = 2 * h + c
             for k in range(16):
-                mm(bk[b][:, 0:128], T.zw[:, 16 - k:144 - k], buf[:, 2048 * h + k:2048 * h + 2048:16], k == 0, k == 15, keys + ["zw"], "b%d" % b)
+                mm(bk[b][:, 0:128], T.zw[:, 16 - k:144 - k], buf[:, 2048 * h + k:2048 * h + 2048:16], k == 0, k == 15, keys + ["zw"], "b%d" % b, 128)
     for b in (1, 0, 3, 2):
         c = 256 * (b % 2) + 128 * (b // 2)
-        act(T.ad[:, c:c + 128], bk[b][:, 0:128], ACT.Copy, wr=["b%d" % b, "ad"])
-        if b == 0:
-            make_selm(0, range(6, 12))
-    dma("A", T.stn[:], T.ad[:, 0:512], ["ad"], ["stn"])
-    dma("A", T.Nb[r32, :], T.ad[r32, 0:512], ["ad"], ["Nbo"])
-    make_selm(0, range(12, 16))
-    scaled(2)
-    scaled(1)
+        act(T.ad[:, c:c + 128], bk[b][:, 0:128], ACT.Copy, wr=["b%d" % b, "ad"], n=128)
+    dma("A", T.stn[:], T.ad[:, 0:512], ["ad"], ["stn"], 128)
+    dma("A", T.Nb[r32, :], T.ad[r32, 0:512], ["ad"], ["Nbo"], 32)
+    make_selm(0)
+    make_selm(1)
+    act(T.bo8[:], T.bo[:], ACT.Identity, 0.0, -BIG, rd=["bo"], wr=["KB"])
+    for out, v, n in ((T.i8w, -BIG, 256), (T.i4, BIG / 2, 128), (T.i32, 1.0, 128), (T.in32, -1.0, 128)):
+        act(out[:, 0:n], T.iw[:, 0:n], ACT.Identity, 0.0, v, rd=["iw"], wr=["KB"], n=n)
+    cp(T.bo16[:], T.bo[:, 0:128], ["bo"], ["K"], 64)
+    cp(T.zw16[:], T.zw[:], ["zw"], ["K"], 136)
+    ts(T.od8[:], T.od[:], -BIG, ALU.add, rd=["od"], wr=["K"], n=128)
     ts(T.dm[:], T.i16[:], ce, ALU.is_equal, rd=["i16", "colg"], wr=["dm"])
-    ts(T.col[:, 4:5], ce, 0.0, ALU.is_equal, 512.0, ALU.mult, rd=["colg"], wr=["col4"])
-    ts(T.col[:, 6:7], T.col[:, 4:5], -256.0, ALU.add, rd=["col4"], wr=["K"])
+    ts(T.col[:, 8:9], ce, 0.0, ALU.is_equal, 512.0 - OFF, ALU.mult, rd=["colg"], wr=["col8"], n=1)
+    ts(T.col[:, 6:7], T.col[:, 8:9], OFF - 256.0, ALU.add, rd=["col8"], wr=["K"], n=1)
     iota(T.rm[:], [[0, 256]], 131072, 0, ["rm"])
-
-    def weights():
-        tt(T.wrow[:, 0:16], T.wrow[:, 0:16], T.dm[:, 0:16], ALU.mult, ["wrow", "dm"], ["wrow2"])
-        op("V", lambda q: q.tensor_reduce(T.col[:, 9:10], T.wrow[:, 0:16], AxisListType.X, ALU.add), ["wrow2"], ["col9"])
-        act(T.bow[:], T.zw[:], ACT.Identity, 0.0, T.col[:, 9:10], rd=["col9", "zw"], wr=["bow"])
-
-    ts(T.rm[:, 0:256:16], T.lf[:], ce, ALU.subtract, rd=["rm", "lf", "colg"], wr=["rm"])
-    cp(T.ex[:], T.exi[:], ["exi"], ["K"])
+    ts(T.rm[:, 0:256:16], T.lf[:], ce, ALU.subtract, rd=["rm", "lf", "colg"], wr=["rm"], n=16)
+    cp(T.ex[:], T.i16[:, 0:16], ["i16"], ["K"], 16)
     iota(T.c256[:], [[0, 256]], 256, 0, ["KG"])
     iota(T.ones[:, 0:128], [[0, 128]], 1, 0, ["KG"])
-    ts(T.col[:, 7:8], T.col[:, 0:1], 1.0, ALU.mult, rd=["colp", "rm", "od", "dm", "zw32", "i256", "i16", "K"], wr=["K"])
-    K = ["K", "KA", "KG"]
+    ms(T.ones[0:2, 128:256], 496.0, ["c496"], 64)
+    ms(T.ones[0:1, 128:256], 2.0 ** 20, ["c496"], 64)
+    ms(T.PT[:, 96:112], 1.0, ["PT1"])
 
-    dma("S", T.zf[32:128, :], T.lnb[0:3, :, 320:384], ["lnb", "lnb1"], ["zf1"])
-    dma("S", T.zf[0:32, :], T.lnb[3, :, 320:384], ["lnb", "lnb1"], ["zf"])
+    oh = [T.oh[:, j:j + 1] for j in range(32)]
+    ts(T.oh[:, 0:8], T.i16[:, 0:8], T.col[:, 3:4], ALU.is_equal, rd=["i16", "colg"], wr=["oh"], n=8)
+    ts(T.oh[:, 8:16], T.oh[:, 0:8], -BIG, ALU.mult, rd=["oh"], wr=["ohb"], n=8)
+    tt(T.oh[:, 16:20:3], T.oh[:, 0:4:3], T.oh[:, 1:5:3], ALU.add, ["oh"], ["oh1"], 4)
+    ts(T.oh[:, 20:22], T.oh[:, 11:13], oh[14], ALU.add, rd=["ohb"], wr=["oh2"], n=2)
+    ts(oh[22], oh[8], -2.0, ALU.mult, oh[20], ALU.add, rd=["ohb", "oh2"], wr=["KF"], n=1)
+    ts(oh[23], oh[9], -2.0, ALU.mult, oh[21], ALU.add, rd=["ohb", "oh2"], wr=["KF"], n=1)
+    ts(oh[24], oh[10], -1.0 / 16, ALU.mult, oh[14], ALU.add, rd=["ohb"], wr=["KF"], n=1)
+    ts(oh[25], oh[2], -2048.0, ALU.mult, rd=["oh"], wr=["KF"], n=1)
+    ts(oh[26], oh[2], 1.0 / 64, ALU.mult, rd=["oh"], wr=["KF"], n=1)
+    ts(oh[27], oh[5], 1.0 / 1024, ALU.mult, rd=["oh"], wr=["KF"], n=1)
+    ts(T.crs[:], T.i16[:], oh[6], ALU.mult, oh[16], ALU.add, rd=["i16", "oh", "oh1"], wr=["crs"])
+    tt(T.mrs[:], T.crs[:], T.i16[:], ALU.mult, ["crs", "i16"], ["mrs"], 512)
+    ts(T.tg[:], T.mrs[:], oh[19], ALU.add, rd=["mrs", "oh1"], wr=["tg"])
+    tt(T.SG[:], T.tg[:], T.Sel[:], ALU.mult, ["tg", "Sel"], ["SG"], 512)
+    ts(T.cn[:, 0:128], T.i16[:, 0:128], 0.0, ALU.is_equal, oh[5], ALU.mult, rd=["i16", "oh"], wr=["cn"], n=128)
+    tt(T.WR[:, 0:128], T.cn[:, 0:128], T.Sel[:, 0:128], ALU.mult, ["cn", "Sel"], ["K"])
+    act(T.KW[:, 0:128], T.SG[:, 0:128], ACT.Identity, 0.0, oh[22], rd=["SG", "KF"], wr=["KW0"], n=128)
+    act(T.KW[:, 128:256], T.Sel[:, 0:128], ACT.Identity, 0.0, oh[24], rd=["Sel", "KF"], wr=["KW1"], n=128)
+    act(T.LP[:], T.SG[:], ACT.Identity, 0.0, oh[23], rd=["SG", "KF"], wr=["KB"])
+    act(T.WC[:], T.Sel[:], ACT.Identity, 0.0, oh[25], rd=["Sel", "KF"], wr=["KB"])
+    act(T.WQ[:, 0:128], T.Sel[:, 0:128], ACT.Identity, 0.0, oh[26], rd=["Sel", "KF"], wr=["KB"], n=128)
+    act(T.WQ[:, 128:256], T.Sel[:, 0:128], ACT.Identity, 0.0, oh[27], rd=["Sel", "KF"], wr=["KB"], n=128)
+    tt(T.KN[:, 0:128], T.KW[:, 0:128], T.KW[:, 128:256], ALU.add, ["KW0", "KW1"], ["KN0"])
+    ts(T.KN[:, 128:256], T.KN[:, 0:128], -1.0, ALU.mult, rd=["KN0"], wr=["K"], n=64)
+    KP, WD, KD, KN = T.KW[0:NF, 0:128], T.KW[0:NF, 128:256], T.KN[0:NF, 0:128], T.KN[0:NF, 128:256]
+    WQ, WB, WR, FL = T.WQ[0:NF, 0:128], T.WQ[0:NF, 128:256], T.WR[0:NF, 0:128], T.FL[0:NF, :]
+    ts(T.col[:, 7:8], T.col[:, 0:1], 1.0, ALU.mult, rd=["colp", "rm", "od", "dm", "zw32", "i16", "c496", "K"], wr=["K"], n=1)
+    K1 = ["iw", "KA", "KG", "c496"]
+    K = ["K", "KA", "KB", "KG"]
+
+    dma("S", T.zf[32:128, 0, :], T.lnb[0:3, :, 320:384], ["lnb", "lnb1"], ["zfa"], 48)
+    dma("S", T.zf[0:32, 0, :], T.lnb[3, :, 320:384], ["lnb", "lnb1"], ["zf0"], 16)
     for n, (a, b) in enumerate(((0, me), (me + 1, N))):
         if b > a:
-            dma("S", X[32 * a:32 * b, XO:XO + XH], T.lnb[a:b, :, 0:320], ["lnb"], ["Xin%d" % n])
-    dma("S", T.z[:, 0, :], T.lnb[:, :, 320:384], ["lnb", "lnb1"], ["z0"])
-    dma("S", T.pli[:], T.lni[:, :, 0:128], ["lni", "lni0"], ["pli"])
-    dma("S", T.bl[32:128, :], T.lni[0:3, :, 128:132], ["lni", "lni2"], ["bl0"])
-    dma("S", T.bl[0:32, :], T.lni[3, :, 128:132], ["lni", "lni2"], ["bl1"])
+            dma("S", X[32 * a:32 * b, XO:XO + XH], T.lnb[a:b, :, 0:320], ["lnb"], ["Xin%d" % n], 160)
+    dma("S", T.z[:, 0, :], T.lnb[:, :, 320:384], ["lnb", "lnb1"], ["z0"], 64)
+    dma("S", T.pli[:], T.lni[:, :, 0:128], ["lni", "lni0"], ["pli"], 256)
+    dma("S", T.bl[32:128, 0:16], T.lni[0:3, :, 128:132], ["lni", "lni2"], ["bl0"], 16)
+    dma("S", T.bl[0:32, 0:16], T.lni[3, :, 128:132], ["lni", "lni2"], ["bl1"], 16)
     for n, (a, b) in enumerate(((0, me), (me + 1, N))):
         if b > a:
-            dma("S", X[32 * a:32 * b, XO + XH:XO + W0], T.lnc[a:b], ["lnc"], ["Xin%d" % (2 + n)])
+            dma("S", X[32 * a:32 * b, XO + XH:XO + W0], T.lnc[a:b], ["lnc"], ["Xin%d" % (2 + n)], 160)
 
     ts(T.Lu[:, 0, :], T.pli[:, 0:A:2], 256.0, ALU.add, rd=["pli"], wr=["Lu0"])
-    ts(T.Cf[:], T.pli[:], 256.0, ALU.add, rd=["pli"], wr=["Cf"])
+    ts(T.Cf[:], T.pli[:], 256.0, ALU.add, rd=["pli"], wr=["Cf"], n=512)
+    cp(T.bu[:], T.bl[:, 0:16], ["bl0", "bl1"], ["bu"], 16)
+    cp(T.Mu[:], T.Cf[:].indirect(T.bu[:]), ["Cf", "bu"], ["Mu"], G256)
 
-    def payee(par, keys, lst=True):
-        if lst:
-            cp(T.bu[:], T.bl[:], keys, ["bu"])
-        ts(T.bc[:], T.bl[:], -256.0, ALU.add, rd=keys, wr=["bc"])
-        tt(T.bexp[:, par, :], T.bc[:].indirect(T.ex[:, 0, :]), T.dm[:], ALU.mult, ["bc"] + K, ["bexp%d" % par])
+    def repeat(j, par, a, b, keys):
+        op("G", lambda q: q.affine_select(T.zrep[:, 16 * a + j:16 * b:16], T.zf[:, par, a:b], [[0, b - a]], ALU.is_ge, 0.0, 0, 0),
+           ["zf%d" % par, "zfa"], keys, 2 * (b - a))
 
-    def spread(js):
-        for j in js:
-            op("G", lambda q, j=j: q.affine_select(T.zrep[:, j:4096:16], T.zf[:], [[0, 256]], ALU.is_ge, 0.0, 0, 0), ["zf", "zf1"], ["zrep0", "zrep1"])
-
-    cp(T.bu[:], T.bl[:], ["bl0", "bl1"], ["bu"])
-    cp(T.Mu[:], T.Cf[:].indirect(T.bu[:]), ["Cf", "bu"], ["Mu"])
-    spread(range(NP))
-    exchange(3 + NCH, T.stn, T.lnn, ["stn"], ["lnn"])
+    for j in range(NP):
+        repeat(j, 0, 0, 256, ["zrep0", "zrep1"])
+    exchange(3 + NCH, T.stn, T.lnn, ["stn"], ["lnn"], 32)
     iota(T.d0[:, 0:1024], [[0, 1024]], -1, 0, ["d00", "d01"])
-    iota(T.d0[:, 1024:1280], [[0, 256]], -32, 0, ["d00", "d01"])
-    op("G", lambda q: q.iota(T.d0[:, 0:1024:512], [[0, 2]], 2 ** 23, 0, allow_small_or_imprecise_dtypes=True), ["d00"], ["d00", "d01"])
-    op("G", lambda q: q.iota(T.d0[:, 1024:1280:16], [[0, 16]], 2 ** 23, 0, allow_small_or_imprecise_dtypes=True), ["d00"], ["d00", "d01"])
+    iota(T.d0[:, 1024:1280], [[0, 256]], -32, 0, ["d0l"])
+    iota(T.d0[:, 0:1024:512], [[0, 2]], 2 ** 23, 0, ["d00", "d01"])
+    iota(T.d0[:, 1024:1280:16], [[0, 16]], 2 ** 23, 0, ["d0l"])
     for j in range(16):
-        op("G", lambda q, j=j: q.iota(T.wrow[:, j:j + 1], [[0, 1]], WT[j], 0, allow_small_or_imprecise_dtypes=True), [], ["wrow"])
+        iota(T.wrow[:, j:j + 1], [[0, 1]], WT[j], 0, ["wrow"])
     for n, (a, b) in enumerate(((0, me), (me + 1, N))):
         if b > a:
-            dma("S", T.Nb[32 * a:32 * b, :], T.lnn[a:b], ["lnn"], ["Nbi%d" % n])
+            dma("S", T.Nb[32 * a:32 * b, :], T.lnn[a:b], ["lnn"], ["Nbi%d" % n], 64)
     for j in range(NP, 16):
-        cp(T.zrep[:, j:4096:16], T.zf[:], ["zf", "zf1"], ["zrepV"])
-    mm(bk[7][:, lo], I, T.z[:, 0, :], True, True, ["z0"] + K, "b7")
+        cp(T.zrep[:, j:4096:16], T.zf[:, 0, :], ["zf0", "zfa"], ["zrepV0", "zrepV1"], 128)
+    mm(bk[7][:, lo], I, T.z[:, 0, :], True, True, ["z0", "iw"], "b7")
+    act(T.col[:, 10:11], T.col[:, 0:1], ACT.Copy, rd=["Nbo", "Nbi0", "Nbi1", "colp"], wr=["Nb"], n=1)
+    tt(T.wrow[:, 0:16], T.wrow[:, 0:16], T.dm[:, 0:16], ALU.mult, ["wrow", "dm"], ["wrow2"], 32)
+    op("V", lambda q: q.tensor_reduce(T.col[:, 9:10], T.wrow[:, 0:16], AxisListType.X, ALU.add), ["wrow2"], ["col9"], 16)
+    act(T.bow[:], T.zw[:], ACT.Identity, 0.0, T.col[:, 9:10], rd=["col9", "zw"], wr=["bow"])
+    ts(T.bc[:], T.bl[:, 0:16], -256.0, ALU.add, rd=["bl0", "bl1"], wr=["bc"], n=16)
+    ts(T.Lu[:, 1, :], T.pli[:, 1:A:2], 256.0, ALU.add, rd=["pli"], wr=["Lu1"])
+    tt(T.nbs[:], T.bc[:].indirect(T.ex[:]), T.dm[:], ALU.mult, ["bc", "dm", "K"], ["nbs"], G256)
 
-    def first_names():
-        act(T.col[:, 10:11], T.col[:, 0:1], ACT.Copy, rd=["Nbo", "Nbi0", "Nbi1"], wr=["Nb"])
-
-    def first_lists():
-        weights()
-        ts(T.bc[:], T.bl[:], -256.0, ALU.add, rd=["bl0", "bl1"], wr=["bc"])
-        ts(T.Lu[:, 1, :], T.pli[:, 1:A:2], 256.0, ALU.add, rd=["pli"], wr=["Lu1"])
-        tt(T.bexp[:, 0, :], T.bc[:].indirect(T.ex[:, 0, :]), T.dm[:], ALU.mult, ["bc"] + K, ["bexp0"])
-
-    def first_cn():
-        mm(bk[4][:], T.i32[:], T.Cf[:], True, False, ["Cf", "KB"], "b4")
-        mm(bk[4][:], I, T.Nb[:], False, True, ["Nb"] + K, "b4")
-        act(T.CN[:], bk[4][:], ACT.Copy, wr=["b4", "CN"])
-
-    late, nbs_, recs = [first_lists], [first_names], []
     for t in range(R):
         s, par = t % 2, t % 2
         d = 2 * (1 + s)
@@ -404,391 +467,357 @@ def rank_program(g, core, T, topo):
         XK = ["X", "Xnew", "Xown", "Xin0", "Xin1", "Xin2", "Xin3"]
         gens = [u for u in (t - 2, t - 4) if u >= 0]
 
-        def ygather(h):
-            act(T.y[:, 2048 * h:2048 * h + 2048], win.indirect(T.Lu[:, s, H[h]]), ACT.Copy, rd=XK + ["Lu%d" % s], wr=["y%d" % h])
-
-        def hgather(h):
-            tt(T.mh[:, 2048 * h:2048 * h + 2048], win.indirect(T.Mu[:, H[h]]), T.zrep[:, 2048 * h:2048 * h + 2048], ALU.min,
-               XK + ["Mu", "zrep%d" % h, "zrepV"], ["mh%d" % h])
-
         def ycol(h, k):
             return T.y[:, 2048 * h + k:2048 * h + 2048:16]
 
         def myk(h, k, n=1):
-            m = 16 - KRS[t]
-            c = (2 * k + h) * 128 if k < m else (2 * m + KRS[t] * h + k - m) * 128
-            return T.my[:, c:c + 128 * n]
+            return T.my[:, 2048 * h + 128 * k:2048 * h + 128 * (k + n)]
 
-        KR = KRS[t]
-        quads = [(k0, min(4, 16 - k0)) for k0 in range(16 - KR, 16, 4)]
+        def home(h):
+            act(T.y[:, 2048 * h:2048 * h + 2048], win.indirect(T.Lu[:, s, H[h]]), ACT.Copy, rd=XK + ["Lu%d" % s], wr=["y%d" % h], n=8 * G256)
 
-        def differ(h, ns=(0, 1)):
-            while recs:
-                recs.pop()()
-            for n in ns:
-                if n < len(quads):
-                    b = 4 + n % 2
-                    for j in range(quads[n][1]):
-                        o = bk[b][:, 128 * j:128 * j + 128]
-                        mm(o, I, T.z[:, par, H[h]], True, False, [zk] + K, "b%d" % b)
-                        mm(o, In, ycol(h, quads[n][0] + j), False, True, ["y%d" % h] + K, "b%d" % b)
+        def far(h):
+            tt(T.mh[:, 2048 * h:2048 * h + 2048], win.indirect(T.Mu[:, H[h]]), T.zrep[:, 2048 * h:2048 * h + 2048], ALU.min,
+               XK + ["Mu", "zrep%d" % h, "zrepV%d" % h], ["mh%d" % h], 8 * G256)
 
-        def relu_part(h):
-            for n, (k0, w) in enumerate(quads):
-                act(myk(h, k0, w), bk[4 + n % 2][:, 0:128 * w], ACT.Relu, wr=["b%d" % (4 + n % 2), "myr%d" % h])
-                differ(h, (n + 2,))
+        def relus(h):
+            for n, k0 in enumerate(range(16 - KRS[t][h], 16, 4)):
+                b, w = 4 + n % 2, min(4, 16 - k0)
+                for j in range(w):
+                    o = bk[b][:, 128 * j:128 * j + 128]
+                    mm(o, I, T.z[:, par, H[h]], True, False, [zk] + K1, "b%d" % b, 128)
+                    mm(o, In, ycol(h, k0 + j), False, True, ["y%d" % h] + K1, "b%d" % b, 128)
+                act(myk(h, k0, w), bk[b][:, 0:128 * w], ACT.Relu, wr=["b%d" % b, "myr%d%d" % (h, n)], n=128 * w)
 
-        def min_part(h):
-            for k in range(16 - KR):
-                tt(myk(h, k), bk[7][:, H[h]], ycol(h, k), ALU.min, ["y%d" % h], ["b7", "mym%d" % h])
+        def mins(h):
+            for k in range(16 - KRS[t][h]):
+                tt(myk(h, k), bk[7][:, H[h]], ycol(h, k), ALU.min, ["y%d" % h], ["b7", "mym%d" % h], 128)
 
-        def min_both(h):
-            for k in range(16 - KR):
-                tt(myk(0, k, 2), bk[7][:, lo], T.y[:, k:4096:16], ALU.min, ["y0", "y1"], ["b7", "mym0", "mym1"])
+        def sums(h):
+            kr, a = KRS[t][h], 128 * h
+            mm(bk[6][:, H[h]], T.ones[0:2, 0:128], T.ones[0:2, 128:256], True, False, K1, "b6", 128)
+            for k in range(16 - kr, 16 if kr < 16 else 0):
+                mm(bk[6][:, a + k:a + 128:16], T.z[:, par, H[h]], T.bop[:, 128:256:16], False, False, [zk] + K1, "b6", 8)
+            for k in range(16):
+                w, key = (T.bon, "myr%d%d" % (h, (k - 16 + kr) // 4)) if k >= 16 - kr else (T.bop, "mym%d" % h)
+                mm(bk[6][:, a + k:a + 128:16], myk(h, k), w[:, 128:256:16], False, k == 15, [key] + K1, "b6", 8)
+            act(T.Gs[:, H[h]], bk[6][:, H[h]], ACT.Identity, -29.0, wr=["b6", "Gs%d" % h], n=128)
+            act(T.Gs[:, a:a + 128:16], bk[6][:, a:a + 128:16], ACT.Identity, 2.0 ** 23, rd=["Gs%d" % h], wr=["b6", "Gs%d" % h], n=8)
+            tt(T.d0[:, 4 * a + 4:4 * a + 512:4], T.Gs[:, a + 1:a + 128], bk[6][:, a:a + 127], ALU.subtract, ["Gs%d" % h], ["b6", "d0%d" % h], 128)
 
-        def fsum(h):
-            for k in list(range(16 - KR, 16)) + list(range(16 - KR)):
-                o = bk[6][:, 128 * h + k:128 * h + 128:16]
-                if k >= 16 - KR:
-                    mm(o, T.z[:, par, H[h]], T.bop[:, 128:256:16], True, False, [zk] + K, "b6")
-                    mm(o, myk(h, k), T.bon[:, 128:256:16], False, True, ["myr%d" % h] + K, "b6")
-                else:
-                    mm(o, myk(h, k), T.bop[:, 128:256:16], True, True, ["mym%d" % h] + K, "b6")
+        def names(h):
+            act(T.NM[:], T.Nb[:].indirect(T.bu[:]), ACT.Copy, rd=["Nb", "bu"], wr=["NM"], n=G256)
 
-        def fout(h):
-            act(T.Gs[:, H[h]], bk[6][:, H[h]], ACT.Identity, -29.0, wr=["b6", "Gs%d" % h])
-            if h:
-                act(T.Eb[:, 4096:4352], bk[6][:, lo], ACT.Identity, 2.0 ** 20 + 496, wr=["b6", "Ef"])
-            act(T.Gs[:, 128 * h:128 * h + 128:16], bk[6][:, 128 * h:128 * h + 128:16], ACT.Identity, 2.0 ** 23, rd=["Gs%d" % h], wr=["b6", "Gs%d" % h])
-
-        def pairs(h, b0):
-            for b in (b0, b0 + 1):
-                c0 = 2048 * s + 512 * b
-                mm(bk[b][:], T.NM[:, H[h]], T.selm[:, c0:c0 + 512], True, False, ["NM", "selm%d" % s] + K, "b%d" % b)
-                mm(bk[b][:], T.Nb[:, 256 * h + s:256 * h + 256:2], T.nil[:], False, False, ["Nb"] + K, "b%d" % b)
+        def pairs(h):
+            for b in range(4):
+                c = 2048 * h + 512 * b
+                mm(bk[b][:], T.NM[:, H[h]], T.selm[:, 2048 * s + 512 * b:2048 * s + 512 * b + 512], True, False, ["NM", "selm%d" % s], "b%d" % b, 512)
+                mm(bk[b][:], T.Nb[:, 256 * h + s:256 * h + 256:2], T.nil[:], False, False, ["Nb", "KA"], "b%d" % b, 512)
                 for j in range(4):
-                    mm(bk[b][:, j:512:4], T.mh[:, 2048 * h + 4 * b + j:2048 * h + 2048:16], sh(T.bon, -d), False, j == 3, ["mh%d" % h] + K, "b%d" % b)
+                    mm(bk[b][:, j:512:4], T.mh[:, 2048 * h + 4 * b + j:2048 * h + 2048:16], sh(T.bon, -d), False, j == 3, ["mh%d" % h] + K1, "b%d" % b, 128)
+                act(T.Eb[:, c:c + 512], bk[b][:], ACT.Abs, 512.0 * 1008 + 483 + 4 * b, wr=["b%d" % b, "E%d%d" % (h, b)], n=512)
 
-        def fold(h, b0):
-            for b in (b0, b0 + 1):
+        def bests(h):
+            for b in range(4):
                 c = 1024 * b + 512 * h
-                act(T.Eb[:, c:c + 512], bk[b][:], ACT.Abs, 512.0 * 2016 + 454 + 4 * b, wr=["b%d" % b, "Ep%d%d" % (h, b)])
-
-        def step(h):
-            a = 128 * h
-            tt(T.d0[:, 4 * a + 4:4 * a + 512:4], T.Gs[:, a + 1:a + 128], bk[6][:, a:a + 127], ALU.subtract, ["Gs%d" % h], ["b6", "d0%d" % h])
-
-        def best(h, b0):
-            for b in (b0, b0 + 1):
-                c = 1024 * b + 512 * h
-                scan(T.So[:, c:c + 512], T.d0[:, 512 * h:512 * h + 512], T.Eb[:, c:c + 512], 0.0, ALU.add, ALU.min,
-                     ["d0%d" % h, "Ep%d%d" % (h, b)], ["So"])
+                scan(T.So[:, c:c + 512], T.d0[:, 512 * h:512 * h + 512], T.Eb[:, 2048 * h + 512 * b:2048 * h + 512 * b + 512], 0.0, ALU.add, ALU.min,
+                     ["d0%d" % h, "w3", "E%d%d" % (h, b)], ["So%d%d" % (h, b)], 512)
+                if (h, b) == (1, 0):
+                    tt(T.So[:, 4352:4368], T.So[:, 4111:4352:16], T.lf[:], ALU.add, ["Sol", "lf"], ["am0"], 32)
+                if (h, b) == (1, 2):
+                    tt(T.So[:, 4368:4384], T.So[:, 63:1024:64], T.So[:, 1087:2048:64], ALU.min, ["So00", "So01", "So10", "So11"], ["am1"], 32)
+            if h:
+                tt(T.So[:, 4384:4400], T.So[:, 4352:4368], T.So[:, 2111:3072:64], ALU.min, ["am0", "So02", "So12"], ["am2"], 32)
 
         def least(h):
-            scan(T.So[:, 4096:4352], T.d0[:, 1024:1280], T.Eb[:, 4096:4352], 0.0, ALU.add, ALU.min, ["Ef"], ["So"])
+            scan(T.So[:, 4096:4352], T.d0[:, 1024:1280], bk[6][:, lo], 0.0, ALU.add, ALU.min, ["d0l"], ["b6", "Sol"])
+            act(T.lf[:], bk[6][:, 15:256:16], ACT.Identity, -496.0, wr=["b6", "lf"], n=16)
 
-        def names():
-            for fn in nbs_:
-                fn()
-            act(T.NM[:], T.Nb[:].indirect(T.bu[:]), ACT.Copy, rd=["Nb", "bu"], wr=["NM"])
-
-        def farlist():
-            act(T.Mf[:], T.Cf[:].indirect(T.bu[:]), ACT.Copy, rd=["Cf", "bu"], wr=["Mf"])
-
-        def rest(h):
-            first_cn()
-            make_selm(1, range(SL))
-
-        def tidy():
-            for fn in late:
-                fn()
-
-        steps = {"y": ygather, "h": hgather, "r": relu_part, "m": min_part, "s": fsum, "o": fout, "d": differ,
-                 "g": step, "M": min_both, "c": rest, "f": least, "b": lambda h: best(h, 0), "B": lambda h: best(h, 2),
-                 "p": lambda h: pairs(h, 0), "P": lambda h: pairs(h, 2), "e": lambda h: fold(h, 0), "E": lambda h: fold(h, 2),
-                 "n": lambda h: names(), "l": lambda h: farlist(), "t": lambda h: tidy()}
-        for w in (ORDER if t else ORDER0).split():
+        steps = {"y": home, "h": far, "r": relus, "m": mins, "s": sums, "n": names, "p": pairs, "b": bests, "l": least}
+        for w in ORDER[t].split():
             steps[w[0]](int(w[1]))
-
-        K = ["K", "KA", "KB", "KG"]
-        mm(bk[0][:, lo], T.i32[:], T.Cf[:, s:A:2], True, False, ["Cf"] + K, "b0")
-        mm(bk[1][:, lo], T.i32[:], T.Mf[:], True, False, ["Mf"] + K, "b1")
-        mm(bk[2][:, lo], In, T.od[:], True, False, K, "b2")
-        tt(T.So[:, 4352:4384], T.So[:, 63:2048:64], T.So[:, 2111:4096:64], ALU.min, ["So"], ["am0"])
-        tt(T.So[:, 4384:4400], T.So[:, 4352:4368], T.So[:, 4368:4384], ALU.min, ["am0"], ["am1"])
-        tt(T.So[:, 4400:4416], T.So[:, 4384:4400], T.Gs[:, 15:256:16], ALU.subtract, ["am1", "Gs0", "Gs1"], ["am2"])
-        tt(T.bi[:], T.So[:, 4400:4416], T.So[:, 4111:4352:16], ALU.min, ["am2", "So"], ["bi"])
-        ts(T.li[:], T.bi[:], 31, ALU.bitwise_and, rd=["bi"], wr=["li"])
-        ts(T.ki[:], T.bi[:], 5, ALU.arith_shift_right, 15, ALU.bitwise_and, rd=["bi"], wr=["ki"])
-        cp(T.lf[:], T.li[:], ["li"], ["lf"])
-        tt(T.nek[:], T.ki[:].indirect(T.ex[:, 0, :]), T.i16[:], ALU.not_equal, ["ki"] + K, ["nek"])
-        act(T.nfT[:], T.lf[:].indirect(T.ex[:, 0, :]), ACT.Relu, -30.0, 2.0, rd=["lf"] + K, wr=["nfT"])
-        tt(T.nel[:], T.li[:].indirect(T.ex[:, 1 + s, :]), T.i16[:], ALU.not_equal, ["li"] + K, ["nel"])
-
-        def turned(bank, c0, src, key, w, stop):
+        aside(act, T.Mf[:], T.Cf[:].indirect(T.bu[:]), ACT.Copy, 0.0, 1.0, ["Cf", "bu"], ["Mf"], G256)
+        if t == 0:
+            mm(bk[4][:], T.i32[:], T.Cf[:], True, False, ["Cf", "KB"], "b4", 2048)
+            mm(bk[4][:], I, T.Nb[:], False, True, ["Nb", "iw"], "b4", 512)
+            act(T.CN[:], bk[4][:], ACT.Copy, wr=["b4", "CN"], n=512)
+            c0 = 128 - 16 * ((-d) % 8)
             for h in range(2):
-                mm(bk[bank][:, c0 + 128 * h:c0 + 128 * h + 128], src[:, H[h]], w, False, stop and h == 1, [key] + K, "b%d" % bank)
+                mm(bk[5][:, h:16:2], T.nbs[:, H[h]], T.bo[:, c0:c0 + 128:16], True, True, ["nbs", "bo"], "b5", 8)
+            cp(T.PT[:, 80:96], bk[5][:, 0:16], [], ["b5", "PTb"], 16)
 
-        turned(0, 0, T.nek, "nek", I8, True)
-        act(T.pc[:], bk[0][:, lo], ACT.Relu, wr=["b0", "pc"])
-        if gens:
-            act(T.foT[:], T.lf[:].indirect(T.ex[:, 0, :]), ACT.Relu, 16.0, -1.0, rd=["lf"] + K, wr=["foT"])
-        else:
-            act(T.Ls[:, s, :], T.CN[:, s:A:2], ACT.Copy, rd=["CN"], wr=["Ls%d" % s])
-        turned(1, 0, T.nel, "nel", I8, True)
-        ts(T.pm[:], bk[1][:, lo], 0.0, ALU.max, wr=["b1", "pm"])
-        turned(2, 0, T.nfT, "nfT", T.i18[:], False)
-        mm(bk[2][:, lo], T.bo32[:], T.pc[:], False, True, ["pc"] + K, "b2")
-        mm(bk[3][:, lo], T.bo32[:], T.pc[:], True, False, ["pc"] + K, "b3")
-        turned(3, 0, T.nfT, "nfT", T.i18[:], True)
+        mm(bk[4][:, lo], T.i32[:], T.Cf[:, s:A:2], True, False, ["Cf"] + K, "b4", 1024)
+        mm(bk[5][:, lo], T.i32[:], T.Mf[:], True, False, ["Mf"] + K, "b5", 1024)
+        mm(bk[0][:, lo], In, T.od[:], True, False, K, "b0")
         mm(bk[1][:, lo], In, T.od8[:], True, False, K, "b1")
-        mm(bk[1][:, lo], T.bo32[:], T.pm[:], False, False, ["pm"] + K, "b1")
-        mm(bk[4][:, lo], T.bo32[:], T.pm[:], True, True, ["pm"] + K, "b4")
-        scan(T.scl[:], T.rm[:], bk[2][:, lo], 131072.0, ALU.min, ALU.max, K, ["b2", "scl"])
-        cp(T.cu[:], T.scl[:, 15:256:16], ["scl"], ["cu"])
-        act(T.crs[:], bk[3][:, lo], ACT.Copy, wr=["b3", "crs"])
-        act(T.yk[:], win.indirect(T.cu[:]), ACT.Copy, rd=XK + ["cu"], wr=["yk"])
-        tt(T.tg[:], win.indirect(T.cu[:]), T.z[:, par, :], ALU.min, XK + ["cu", zk], ["tg"])
-        tt(T.eq[:, 15, :], bk[3][:, lo], T.scl[:], ALU.is_equal, ["scl"], ["b3", "eq15"])
+        mm(bk[2][:, hi], In, T.od[:], True, False, K, "b2")
+        tt(T.So[:, 4400:4416], T.So[:, 4368:4384], T.So[:, 3135:4096:64], ALU.min, ["am1", "So03", "So13"], ["am3"], 32)
+        for h in range(2):
+            tt(T.bi[:, h:16:2], T.So[:, 4400 + 8 * h:4408 + 8 * h], T.So[:, 4384 + 8 * h:4392 + 8 * h], ALU.min, ["am3", "am2"], ["bi"], 16)
+        ts(T.it[:, 0:16], T.bi[:], 5, ALU.arith_shift_right, 15, ALU.bitwise_and, rd=["bi"], wr=["ki"], n=16)
+        ts(T.it[:, 16:32], T.bi[:], 31, ALU.bitwise_and, rd=["bi"], wr=["li"], n=16)
+        ts(T.it[:, 32:48], T.bi[:], 16, ALU.bitwise_and, rd=["bi"], wr=["ni"], n=16)
+        tt(T.PT[:, 48:80], T.it[:, 0:32], T.it[:, 0:32], ALU.mult, ["ki", "li"], ["PTs"], 64)
+        cp(T.PT[:, 0:48], T.it[:], ["ki", "li", "ni"], ["PTk"], 48)
+        for h in range(2):
+            mm(bk[7][0:NF, 256 + 128 * h:384 + 128 * h], T.PT[:, h:112:2], I, True, True, ["PTs", "PTk", "PTb", "PT1", "iw"], "b7", 128)
+        cp(FL, bk[7][0:NF, hi], [], ["b7", "FL"])
 
-        def equal_rows(bank, rep, lst, outs, extra):
-            segs, o = [], 0
-            for j in range(15 - NA, 15):
+        def flags(bank, half, w, st=False, sp=False):
+            mm(bk[bank][:, half], w, FL, st, sp, ["FL", "KW0", "KW1", "KN0"] + K, "b%d" % bank)
+
+        flags(4, lo, KP, sp=True)
+        ts(T.pc[:], bk[4][:, lo], -MID, ALU.add, -LOW, ALU.max, wr=["b4", "pc"])
+        flags(5, lo, sh(T.LP, d, NF), sp=True)
+        ts(T.pm[:], bk[5][:, lo], -MID, ALU.add, -LOW, ALU.max, wr=["b5", "pm"])
+        if not gens:
+            aside(act, T.Ls[:, s, :], T.CN[:, s:A:2], ACT.Copy, 0.0, 1.0, ["CN"], ["Ls%d" % s])
+        flags(0, lo, WQ)
+        mm(bk[0][:, lo], T.bo16[:], T.pc[:], False, True, ["pc"] + K, "b0")
+        mm(bk[3][:, lo], T.bo16[:], T.pc[:], True, True, ["pc"] + K, "b3")
+        flags(1, lo, sh(T.WC, d, NF))
+        mm(bk[1][:, lo], T.bo16[:], T.pm[:], False, False, ["pm"] + K, "b1")
+        mm(bk[4][:, lo], T.bo16[:], T.pm[:], True, True, ["pm"] + K, "b4")
+        mm(bk[2][:, hi], T.bo16[:], T.pc[:], False, False, ["pc"] + K, "b2")
+        scan(T.scl[:], T.rm[:], bk[0][:, lo], 131072.0, ALU.min, ALU.max, K, ["b0", "scl"])
+        ts(T.cu[:], T.scl[:, 15:256:16], OFF, ALU.add, rd=["scl"], wr=["cu"], n=16)
+        act(T.yk[:], win.indirect(T.cu[:]), ACT.Copy, rd=XK + ["cu"], wr=["yk"], n=G256)
+
+        def equal_rows(n, bank, lst, b, c0, w, beside):
+            bn, na, e0, a0 = "b%d" % bank, NA[n], 16 * n, 1024 * n
+            rep = (T.crs, T.mrs)[n]
+            if FAST:
+                ts(T.r16[:, n, :], bk[bank][:, lo], OFF, ALU.add, wr=[bn, "r16%d" % n])
+            else:
+                act(rep[:], bk[bank][:, lo], ACT.Copy, wr=[bn, ("crs", "mrs")[n]])
+            tt(T.eq[:, e0 + 15, :], bk[bank][:, lo], T[lst][:], ALU.is_equal, [lst], [bn, "eq%d" % (e0 + 15)])
+            rows, o = [(0, T.eq[:, e0 + 15, :], "eq%d" % (e0 + 15))], a0
+            for j in range(15 - na):
                 c = 16 * j + 16
-                act(T.ad[:, o:o + 256 - c], T[rep][:, c:256], ACT.Abs, T[lst][:, c - 1:c], -1.0, rd=[rep, lst], wr=["ad"])
-                segs.append((c, o))
+                if FAST:
+                    ts(T.eq[:, e0 + j, c:256], T.r16[:, n, c:256], -OFF, ALU.add, T[lst][:, c - 1:c], ALU.is_equal, rd=[lst, "r16%d" % n],
+                       wr=["eq%d" % (e0 + j)], n=(256 - c) / 2)
+                else:
+                    ts(T.eq[:, e0 + j, c:256], rep[:, c:256], T[lst][:, c - 1:c], ALU.is_equal, rd=[lst, ("crs", "mrs")[n]], wr=["eq%d" % (e0 + j)], n=256 - c)
+                rows.append((c, T.eq[:, e0 + j, c:256], "eq%d" % (e0 + j)))
+            for j in range(15 - na, 15):
+                c = 16 * j + 16
+                act(T.ad[:, o:o + 256 - c], bk[bank][:, c:256], ACT.Abs, T[lst][:, c - 1:c], -1.0, rd=[lst], wr=[bn, "ad"], n=256 - c)
+                rows.insert(len(rows) - 2, (c, T.eqa[:, o:o + 256 - c], "eqa%d" % n))
                 o += 256 - c
-            if NA:
-                act(T.eqa[:, 0:o], T.ad[:, 0:o], ACT.Relu, 1.0, -4.0, rd=["ad"], wr=["eqa"])
-            for j in range(15 - NA):
-                c = 16 * j + 16
-                ts(T.eq[:, j, c:256], bk[bank][:, c:256], T[lst][:, c - 1:c], ALU.is_equal, rd=[lst], wr=["b%d" % bank, "eq%d" % j])
-                for b, c0, w in outs:
-                    mm(bk[b][:, c0 + c:c0 + 256], w, T.eq[:, j, c:256], False, False, ["eq%d" % j] + K, "b%d" % b)
-                if j == 12 - NA:
-                    for b, c0, w in outs:
-                        for c, o in segs:
-                            mm(bk[b][:, c0 + c:c0 + 256], w, T.eqa[:, o:o + 256 - c], False, False, ["eqa"] + K, "b%d" % b)
-                if j in extra:
-                    extra[j]()
-            for b, c0, w in outs:
-                last = ops[max(i for i, x in enumerate(ops) if x[0] == "T" and x[3] == ["b%d" % b])]
-                stops.add(last[1])
+            if na:
+                act(T.eqa[:, a0:o], T.ad[:, a0:o], ACT.Relu, 1.0, -4.0, rd=["ad"], wr=["eqa%d" % n], n=o - a0)
+            for fn in beside:
+                fn()
+            for x, (c, src, key) in enumerate(rows):
+                mm(bk[b][:, c0 + c:c0 + 256], w, src, False, x == 15, [key] + K, "b%d" % b, 256 - c)
 
         zn, znk = T.z[:, 1 - par, :], "z%d" % (1 - par)
+        if t < R - 1:
+            mm(bk[7][:, hi], sh(T.iw, dn), z, True, False, [zk] + K, "b7")
+            mm(bk[7][:, hi], sh(T.inw, dn), T.yk[:], False, True, ["yk"] + K, "b7")
+            act(T.zf[:, 1 - par, :], bk[7][:, hi], ACT.Abs, wr=["b7", "zf%d" % (1 - par)])
+            for j in range(16):
+                if j < ZW[t]:
+                    repeat(j, 1 - par, 0, 256, ["zrep0", "zrep1"])
+                else:
+                    repeat(j, 1 - par, 0, 128, ["zrep0"])
+            for j in range(ZW[t], 16):
+                if j < 16 - ZV[t]:
+                    repeat(j, 1 - par, 128, 256, ["zrep1"])
+                else:
+                    aside(cp, T.zrep[:, 2048 + j:4096:16], T.zf[:, 1 - par, H[1]], ["zf%d" % (1 - par)], ["zrepV1"], 64)
 
-        def amounts():
-            act(T.mrs[:], bk[4][:, lo], ACT.Copy, wr=["b4", "mrs"])
-
-        def relist():
-            mm(bk[2][:, hi], In, T.od8[:], True, False, K, "b2")
-            turned(2, 256, T.nfT, "nfT", I8, False)
-            mm(bk[2][:, hi], T.bo32[:], T.pc[:], False, False, ["pc"] + K, "b2")
-
-        def relist2():
-            mm(bk[5][:, hi], In, T.od[:], True, False, K, "b5")
-            mm(bk[5][:, hi], T.bo32[:], T.pm[:], False, False, ["pm"] + K, "b5")
-
-        def newz():
+        def rests():
+            mm(bk[6][:, lo], I, z, True, False, [zk] + K, "b6")
+            mm(bk[6][:, lo], In, T.yk[:], False, True, ["yk"] + K, "b6")
             if t < R - 1:
-                mm(bk[6][:, lo], I, z, True, False, [zk] + K, "b6")
-                mm(bk[6][:, lo], In, T.yk[:], False, True, ["yk"] + K, "b6")
                 act(zn, bk[6][:, lo], ACT.Abs, wr=["b6", znk])
-                mm(bk[7][:, hi], sh(T.iw, dn), z, True, False, [zk] + K, "b7")
-                mm(bk[7][:, hi], sh(T.inw, dn), T.yk[:], False, True, ["yk"] + K, "b7")
-                act(T.zf[:], bk[7][:, hi], ACT.Abs, wr=["b7", "zf", "zf1"])
-                for h in range(2):
-                    for j in range(16 - h * ZA[t]):
-                        op("G", lambda q, j=j, h=h: q.affine_select(T.zrep[:, 2048 * h + j:2048 * h + 2048:16], T.zf[:, H[h]], [[0, 128]],
-                                                                    ALU.is_ge, 0.0, 0, 0), ["zf", "zf1"], ["zrep%d" % h])
+            if HA:
+                act(T.ya[:], bk[6][:, lo], ACT.Relu, 0.0, -1.0, wr=["b6", "ya"])
 
-        mm(bk[1][:, lo], sh(T.bo8, d), T.eq[:, 15, :], False, False, ["eq15"] + K, "b1")
-        equal_rows(3, "crs", "scl", [(1, 0, sh(T.bo8, d))], {JZ: newz, JZ + 1: amounts})
-
-        def second():
-            relist()
-            scan(T.sm2[:], T.rm[:], bk[1][:, lo], 131072.0, ALU.min, ALU.max, K, ["b1", "sm2"])
-            tt(T.c1s[:], bk[1][:, lo], T.nod[:], ALU.is_lt, K, ["b1", "c1s"])
-            cp(T.mu[:], T.sm2[:, 15:256:16], ["sm2"], ["mu"])
-            act(T.hm[:], win.indirect(T.mu[:]), ACT.Copy, rd=XK + ["mu"], wr=["hm"])
-            tt(T.eq[:, 15, :], bk[4][:, lo], T.sm2[:], ALU.is_equal, ["sm2"], ["b4", "eq15"])
-            for _ in range(2):
-                mm(bk[2][:, hi], sh(T.i8w, -d), T.c1s[:], False, False, ["c1s"] + K, "b2")
-            mm(bk[2][:, hi], sh(T.bo8, -d), T.eq[:, 15, :], False, False, ["eq15"] + K, "b2")
-
-        def farbal():
-            mm(bk[0][:, hi], sh(T.iw, -d), T.hm[:], True, True, ["hm"] + K, "b0")
-
-        def amount():
-            tt(T.v0[:], bk[0][:, hi], T.tg[:], ALU.min, ["tg"], ["b0", "v0"])
-            mm(bk[0][:, lo], sh(T.iw, d), T.v0[:], True, True, ["v0"] + K, "b0")
-
-        def weighted():
-            if t < R - 1:
-                c2 = 128 - 16 * (dn % 8)
-                for il in range(16):
-                    mm(bk[6][:, 0:16], T.bow[:, 16 - il + c2:144 - il + c2], T.z[:, 1 - par, il:256:16], il == 0, il == 15, [znk, "bow"] + K, "b6")
-                mm(bk[7][:, lo], I, zn, True, True, [znk] + K, "b7")
-
-        thr = XO + W0 - 0.5
+        def payees():
+            c2 = 128 - 16 * (dn % 8)
+            for il in range(16):
+                mm(bk[6][:, 0:16], T.bow[:, 16 - il + c2:144 - il + c2], T.z[:, 1 - par, il:256:16], il == 0, il == 15, [znk, "bow"], "b6", 16)
+            for h in range(2):
+                mm(bk[6][:, 16 + h:32:2], T.z[:, 1 - par, H[h]], T.bow[:, 16:144:16], True, True, [znk, "bow"], "b6", 8)
+            mm(bk[7][:, lo], I, zn, True, True, [znk] + K, "b7")
+            cp(T.t3[:], bk[6][:, 0:32], [], ["b6", "t3"], 32)
+            ts(T.bl[:], T.t3[:], 511, ALU.bitwise_and, rd=["t3"], wr=["bl0", "bl1"], n=32)
+            cp(T.bu[:], T.bl[:, 0:16], ["bl0"], ["bu"], 16)
+            ts(T.PT[:, 80:96], T.bl[:, 16:32], -256.0, ALU.add, rd=["bl0"], wr=["PTb"], n=16)
 
         def closings():
-            if gens:
-                act(T.sgb[:], T.crs[:], ACT.Sign, thr + P * gens[0] * (len(gens) - 1), -1.0, rd=["crs"], wr=["sgb"])
-                mm(bk[3][:, hi], I, T.yk[:], True, False, ["yk"] + K, "b3")
-                turned(3, 256, T.foT, "foT", I8, False)
-                mm(bk[3][:, hi], I8, T.sgb[:], False, True, ["sgb"] + K, "b3")
+            thr = XO + W0 - 0.5 - OFF
+            act(T.sgb[:], bk[3][:, lo], ACT.Sign, thr + P * gens[0] * (len(gens) - 1), -1.0, wr=["b3", "sgb"])
             if len(gens) > 1:
-                act(T.sga[:], T.crs[:], ACT.Sign, -thr, 1.0, rd=["crs"], wr=["sga"])
-                mm(bk[5][:, hi], I, T.yk[:], True, False, ["yk"] + K, "b5")
-                turned(5, 256, T.foT, "foT", I8, False)
-                mm(bk[5][:, hi], I4, T.sgb[:], False, False, ["sgb"] + K, "b5")
-                mm(bk[5][:, hi], I4, T.sga[:], False, True, ["sga"] + K, "b5")
-
-        def given():
-            for n, u in enumerate(gens):
+                act(T.sga[:], bk[3][:, lo], ACT.Sign, -thr, 1.0, wr=["b3", "sga"])
+            for n in range(len(gens)):
                 b = (3, 5)[n]
-                act(T["wh%d" % n][:], bk[b][:, hi], ACT.Relu, -8192.0, wr=["b%d" % b, "wh%d" % n])
+                mm(bk[b][:, hi], I, T.yk[:], True, False, ["yk"] + K, "b%d" % b)
+                flags(b, hi, WD)
+                if n == 0:
+                    mm(bk[b][:, hi], I8, T.sgb[:], False, True, ["sgb"] + K, "b%d" % b)
+                else:
+                    mm(bk[b][:, hi], I4, T.sgb[:], False, False, ["sgb"] + K, "b%d" % b)
+                    mm(bk[b][:, hi], I4, T.sga[:], False, True, ["sga"] + K, "b%d" % b)
+                act(T.wh[:, n, :], bk[b][:, hi], ACT.Relu, -BIG, wr=["b%d" % b, "wh%d" % n])
 
-        def emptied():
-            for n, u in enumerate(gens):
+        def gifts():
+            for n in range(len(gens)):
                 b = (3, 5)[n]
+                mm(bk[b][:, hi], sh(T.iw, d), T.wh[:, n, :], True, True, ["wh%d" % n] + K, "b%d" % b)
+                act(T.uh[:, n, :], T.wh[:, n, :], ACT.Identity, 63.0, -1.0, rd=["wh%d" % n], wr=["uh%d" % n])
+                act(T.wf[:, n, :], bk[b][:, hi], ACT.Copy, wr=["b%d" % b, "wf%d" % n])
+                act(T.uf[:, n, :], bk[b][:, hi], ACT.Identity, 63.0, -1.0, wr=["b%d" % b, "uf%d" % n])
+
+        def amounts():
+            mm(bk[0][:, hi], I, T.yk[:], True, False, ["yk"] + K, "b0")
+            if HA:
+                mm(bk[0][:, hi], In, T.ya[:], False, False, ["ya"] + K, "b0")
+            mm(bk[0][:, hi], sh(T.inw, -d), T.hm[:], False, True, ["hm"] + K, "b0")
+            if HA:
+                act(T.vf[:], bk[0][:, hi], ACT.Relu, wr=["b0", "vf"])
+                mm(bk[0][:, hi], I, T.ya[:], True, False, ["ya"] + K, "b0")
+                mm(bk[0][:, hi], I, T.vf[:], False, True, ["vf"] + K, "b0")
+            act(T.cn[:], bk[0][:, hi], ACT.Relu, wr=["b0", "cn"])
+            for n, u in enumerate(gens):
+                b = (6, 7)[n]
                 blk = X[:, XO + W0 + P * u:XO + W0 + P * u + P]
-                mm(bk[b][:, lo], I, blk, True, False, XK + K, "b%d" % b)
-                mm(bk[b][:, lo], In, T["wh%d" % n][:], False, True, ["wh%d" % n] + K, "b%d" % b)
-            act(T.nv0[:], T.v0[:], ACT.Identity, 0.0, -1.0, rd=["v0"], wr=["nv0"])
-            for n, u in enumerate(gens):
-                b = (3, 5)[n]
-                act(X[:, XO + W0 + P * u:XO + W0 + P * u + P], bk[b][:, lo], ACT.Copy, wr=["b%d" % b, "X"])
+                mm(bk[b][:, hi], I, blk, True, False, XK + K, "b%d" % b)
+                mm(bk[b][:, hi], In, T.wh[:, n, :], False, True, ["wh%d" % n] + K, "b%d" % b)
+                act(blk, bk[b][:, hi], ACT.Copy, wr=["b%d" % b, "X"])
+            mm(bk[0][:, lo], sh(T.iw, d), T.yk[:], True, False, ["yk"] + K, "b0")
+            mm(bk[0][:, lo], sh(T.inw, d), T.cn[:], False, True, ["cn"] + K, "b0")
+            act(T.vf[:], bk[0][:, lo], ACT.Copy, wr=["b0", "vf"])
+            act(T.nvf[:], bk[0][:, lo], ACT.Identity, 0.0, -1.0, wr=["b0", "nvf"])
 
-        closings()
-        second()
-        if GE:
-            given()
-        equal_rows(4, "mrs", "sm2", [(2, 256, sh(T.bo8, -d))], {JF: farbal if GE else lambda: (farbal(), given()), JV: amount, JE: emptied})
-        relist2()
-        act(T.vf[:], bk[0][:, lo], ACT.Copy, wr=["b0", "vf"])
-        act(T.nvf[:], bk[0][:, lo], ACT.Identity, 0.0, -1.0, wr=["b0", "nvf"])
-        for j in range(16 - ZA[t], 16):
-            act(T.zrep[:, 2048 + j:4096:16], T.zf[:, H[1]], ACT.Copy, rd=["zf", "zf1"], wr=["zrepV"])
-        scan(T.scl[:], T.rm[:], bk[2][:, hi], 131072.0, ALU.min, ALU.max, K, ["b2", "scl"])
-        tt(T.nbs[:], bk[2][:, hi], T.nod[:], ALU.is_lt, K, ["b2", "nbs"])
-        cp(T.cs[:, t, :], T.scl[:, 15:256:16], ["scl"], ["cs%d" % t])
-        mm(bk[5][:, hi], sh(T.i8w, d), T.nbs[:], False, True, ["nbs"] + K, "b5")
-        weighted()
-        mm(bk[4][:, hi], I, T.v0[:], True, False, ["v0"] + K, "b4")
-        mm(bk[4][:, hi], I8, T.nbs[:], False, True, ["nbs"] + K, "b4")
-        for n in range(len(gens)):
-            b = (2, 3)[n]
-            mm(bk[b][:, lo], sh(T.iw, d), T["wh%d" % n][:], True, True, ["wh%d" % n] + K, "b%d" % b)
-            act(T["uh%d" % n][:], T["wh%d" % n][:], ACT.Identity, 63.0, -1.0, rd=["wh%d" % n], wr=["uh%d" % n])
-            act(T["wf%d" % n][:], bk[b][:, lo], ACT.Copy, wr=["b%d" % b, "wf%d" % n])
-            act(T["uf%d" % n][:], bk[b][:, lo], ACT.Identity, 63.0, -1.0, wr=["b%d" % b, "uf%d" % n])
-
-        tt(win.indirect(T.cs[:, t, :]), T.yk[:], T.nv0[:], ALU.add, ["X", "cs%d" % t, "yk", "nv0"], ["X"])
-        act(X[:, wt:wt + P], bk[4][:, hi], ACT.Relu, wr=["b4", "Xnew"])
-        if t == 0:
-            make_selm(1, range(SL, 16))
-        scan(T.sml[:], T.rm[:], bk[5][:, hi], 131072.0, ALU.min, ALU.max, K, ["b5", "sml"])
-        cp(T.ms[:, t, :], T.sml[:, 15:256:16], ["sml"], ["ms%d" % t])
-        if t < R - 1:
-            cp(T.t3[:], bk[6][:, 0:16], [], ["b6", "t3"])
-        tt(T.tg[:], win.indirect(T.ms[:, t, :]), T.vf[:], ALU.max, ["X", "ms%d" % t, "vf"], ["tg"])
-        if t < R - 1:
-            ts(T.bl[:], T.t3[:], 511, ALU.bitwise_and, rd=["t3"], wr=["bl0", "bl1"])
-        tt(win.indirect(T.ms[:, t, :]), T.tg[:], T.nvf[:], ALU.add, ["X", "tg", "nvf"], ["X"])
-        if t < R - 1:
-            cp(T.bu[:], T.bl[:], ["bl0"], ["bu"])
-        for n, u in enumerate(gens):
-            old = X[:, 0:XO + W0 + P * u]
-            for lst, w_, u_ in ((T.cs, "wh%d" % n, "uh%d" % n), (T.ms, "wf%d" % n, "uf%d" % n)):
-                tt(T.tg[:], old.indirect(lst[:, u, :]), T[u_][:], ALU.min, ["X", u_], ["tg"])
-                tt(old.indirect(lst[:, u, :]), T.tg[:], T[w_][:], ALU.add, ["X", "tg", w_], ["X", "XA%d" % n])
-
-        be, bek = T.bexp[:, par, :], "bexp%d" % par
+        equal_rows(0, 3, "scl", 1, 0, sh(T.bo8, d), [rests] * (HA or t < R - 1) + [closings] * (t > 1))
+        scan(T.sm2[:], T.rm[:], bk[1][:, lo], 131072.0, ALU.min, ALU.max, K, ["b1", "sm2"])
+        act(T.tg[:], bk[1][:, lo], ACT.Sign, 32768.5 + OFF, wr=["b1", "tg"])
+        mm(bk[2][:, hi], sh(T.bop, -d), T.tg[:], False, False, ["tg"] + K, "b2")
+        ts(T.mu[:], T.sm2[:, 15:256:16], OFF, ALU.add, rd=["sm2"], wr=["mu"], n=16)
+        if HA:
+            act(T.hm[:], win.indirect(T.mu[:]), ACT.Copy, rd=XK + ["mu"], wr=["hm"], n=G256)
+        else:
+            tt(T.hm[:], win.indirect(T.mu[:]), T.zf[:, par, :], ALU.min, XK + ["mu", "zf%d" % par, "zfa"], ["hm"], G256)
         cn = T.CN[:, s:A:2]
-        mm(bk[0][:, hi], I, T.i256[:], True, False, K, "b0")
-        mm(bk[0][:, hi], T.ones[0:11 + t, 0:128], T.c256[0:11 + t, :], False, False, K, "b0")
-        mm(bk[0][:, hi], sh(T.bof, -d), be, False, False, [bek] + K, "b0")
-        turned(0, 256, T.nek, "nek", I8, False)
-        aside = len(gens) == 2
-        if aside:
-            mm(bk[0][:, hi], T.in32[:], cn, False, False, ["CN"] + K, "b0")
-        mm(bk[0][:, hi], I8, T.nbs[:], False, True, ["nbs"] + K, "b0")
-        if len(gens) == 1:
-            mm(bk[1][:, hi], T.i32[:], T.Ls[:, s, :], True, False, ["Ls%d" % s] + K, "b1")
-            turned(1, 256, T.nek, "nek", I4, False)
-            turned(1, 256, T.foT, "foT", I4, True)
-        if aside:
-            act(T.crs[:], bk[0][:, hi], ACT.Relu, wr=["b0", "crs"])
-            src, key = T.Us, "Us%d" % s
-            mm(bk[1][:, hi], T.i32[:], cn, True, False, ["CN"] + K, "b1")
-            mm(bk[1][:, hi], T.in32[:], src[:, s, :], False, False, [key] + K, "b1")
-            turned(1, 256, T.nek, "nek", I8, False)
-            turned(1, 256, T.foT, "foT", I8, True)
-            act(T.mrs[:], bk[1][:, hi], ACT.Relu, wr=["b1", "mrs"])
-            mm(bk[6][:, hi], T.i32[:], cn, True, False, ["CN"] + K, "b6")
-            mm(bk[6][:, hi], T.i32[:], T.crs[:], False, False, ["crs"] + K, "b6")
-            mm(bk[6][:, hi], T.in32[:], T.mrs[:], False, True, ["mrs"] + K, "b6")
-            act(T.sm2[:], bk[6][:, hi], ACT.Identity, MAGIC, wr=["b6", "sm2"])
-            if t < R - 1:
-                act(T.Cf[:, s:A:2], T.sm2[:], ACT.Identity, -MAGIC, rd=["sm2"], wr=["Cf"])
-                act(cn, bk[6][:, hi], ACT.Copy, wr=["b6", "CN"])
-            else:
-                act(cn, T.sm2[:], ACT.Identity, -MAGIC - 256, rd=["sm2"], wr=["CN"])
-                act(T.CN[:, 1 - s:A:2], T.Cf[:, 1 - s:A:2], ACT.Identity, -256.0, rd=["Cf"], wr=["CN"])
-        if len(gens) == 1:
-            mm(bk[7][:, hi], T.i32[:], cn, True, False, ["CN"] + K, "b7")
-            turned(7, 256, T.nek, "nek", I8, False)
-            mm(bk[7][:, hi], I8, T.nbs[:], False, True, ["nbs"] + K, "b7")
-        if aside and t < R - 1:
-            mm(bk[2][:, hi], T.i32[:], cn, True, False, ["CN"] + K, "b2")
-            mm(bk[2][:, hi], T.in32[:], T.Cf[:, s:A:2], False, True, ["Cf"] + K, "b2")
-        c1 = 128 - 16 * ((-d) % 8)
-        mm(bk[4][:, lo], T.zw[:, 16 + c1:144 + c1], be, True, False, [bek] + K, "b4")
-        mm(bk[4][:, lo], T.zw32[:, 15:143], T.pc[:], False, False, ["pc"] + K, "b4")
-        mm(bk[4][:, lo], T.zw32[:, 14 + c1:142 + c1], T.pm[:], False, False, ["pm"] + K, "b4")
-        mm(bk[4][:, lo], I8, T.nbs[:], False, True, ["nbs"] + K, "b4")
-        def record(t=t):
-            act(T.recb[:, P * t:P * t + P], bk[4][:, lo], ACT.Relu, T.col[:, 6:7], rd=K, wr=["b4", "recb"])
+        src, key = (T.Us, "Us%d" % s) if len(gens) == 2 else (T.Ls, "Ls%d" % s)
 
-        if t == R - 1:
-            record()
-        if t == R - 1:
-            dma("A", T.stf[:, :, 0:128], T.CN[:], ["CN"], ["stf3"])
-            for e in range(3):
-                dma("A", T.stf[:, :, 128 + 24 * e:152 + 24 * e], T.recb[e:128:16, :], ["recb"], ["stf%d" % e])
-            SF = ["stf0", "stf1", "stf2", "stf3"]
-            dma("A", T.lnf[me], T.stf[me], SF, ["lnfo"])
-            for c, (a, b) in enumerate(CH):
-                dma("S", T["sto%d" % c][:], X[:, XO + a:XO + b], XK if c else ["XA0", "Xnew"], ["sto%d" % c])
-            for c in range(NCH):
-                exchange(3 + c, T["sto%d" % c], T["lno%d" % c], ["sto%d" % c], ["lno%d" % c])
-                if c == 0:
-                    exchange(2, T.stf, T.lnf, SF, ["lnf"])
-            dma("A", T.xo[r32, :], X[r32, XO:XO + 4096], XK + ["sto1", "sto2"], [])
-        if not aside:
-            if gens:
-                tt(cn, bk[1][:, hi], cn, ALU.min, ["CN"], ["b1", "CN"])
+        def reopened():
+            if t in ASIDE:
+                flags(5, lo, KD, st=True)
+                mm(bk[5][:, lo], T.i32[:], cn, False, False, ["CN"] + K, "b5", 1024)
+                mm(bk[5][:, lo], T.in32[:], src[:, s, :], False, True, [key] + K, "b5", 1024)
+                act(T.mrs[:], bk[5][:, lo], ACT.Relu, wr=["b5", "mrs"])
+            else:
+                flags(5, lo, KN, st=True)
+                mm(bk[5][:, lo], T.i32[:], src[:, s, :], False, True, [key] + K, "b5", 1024)
+                tt(cn, bk[5][:, lo], cn, ALU.min, ["CN"], ["b5", "CN"])
+            if len(gens) == 1:
+                mm(bk[7][:, hi], T.i32[:], cn, True, False, ["CN"] + K, "b7", 1024)
+
+        def offered():
+            flags(0, hi, KP, st=True)
+            mm(bk[0][:, hi], I, T.i256[:], False, False, K, "b0")
+            mm(bk[0][:, hi], T.ones[0:11 + t, 0:128], T.c256[0:11 + t, :], False, False, K, "b0")
+            flags(0, hi, WB)
+
+        equal_rows(1, 4, "sm2", 2, 256, sh(T.bo8, -d), [payees] * (t < R - 1) + [amounts] + [reopened] * (t > 1))
+        offered()
+        aside(gifts)
+        aside(mm, bk[1][:, lo], In, T.od[:], True, False, K, "b1")
+        aside(mm, bk[1][:, lo], T.bo16[:], T.pm[:], False, False, ["pm"] + K, "b1")
+        scan(T.scl[:], T.rm[:], bk[2][:, hi], 131072.0, ALU.min, ALU.max, K, ["b2", "scl"])
+        act(T.nbs[:], bk[2][:, hi], ACT.Relu, -32768.0 - OFF, -1.0, wr=["b2", "nbs"])
+        NB = T.bon[:, 128:256]
+        if t not in ASIDE:
+            mm(bk[0][:, hi], NB, T.nbs[:], False, True, ["nbs"] + K, "b0")
             tt(cn, bk[0][:, hi], cn, ALU.max, ["CN"], ["b0", "CN"])
             ts(T.Cf[:, s:A:2], cn, MAGIC, ALU.add, -MAGIC, ALU.add, rd=["CN"], wr=["Cf"])
-            mm(bk[2][:, hi], T.i32[:], cn, True, False, ["CN"] + K, "b2")
-            mm(bk[2][:, hi], T.in32[:], T.Cf[:, s:A:2], False, True, ["Cf"] + K, "b2")
-        if t < R - 1:
-            nbs_ = [lambda s=s: act(T.Nb[:, s:A:2], bk[2][:, hi], ACT.Copy, wr=["b2", "Nb"])]
-            recs = [record]
-            cp(T.Mu[:], T.Cf[:].indirect(T.bu[:]), ["Cf", "bu"], ["Mu"])
-            late = [lambda par=par: payee(1 - par, ["bl0", "bl1"], False)]
-            if len(gens) == 1:
-                late.append(lambda s=s: tt(T.Us[:, s, :], bk[7][:, hi], T.Ls[:, s, :], ALU.max, ["Ls%d" % s], ["b7", "Us%d" % s]))
-            if t < R - 2:
-                late.append(lambda s=s: cp(T.Lu[:, s, :], T.Cf[:, s:A:2], ["Cf"], ["Lu%d" % s]))
+        ts(T.cs[:, t, :], T.scl[:, 15:256:16], OFF, ALU.add, rd=["scl"], wr=["cs%d" % t], n=16)
+        mm(bk[1][:, lo], sh(T.bon, d), T.nbs[:], False, True, ["nbs"] + K, "b1")
 
+        def supports():
+            flags(7, hi, KP)
+            mm(bk[7][:, hi], NB, T.nbs[:], False, True, ["nbs"] + K, "b7")
+            tt(T.Us[:, s, :], bk[7][:, hi], T.Ls[:, s, :], ALU.max, ["Ls%d" % s], ["b7", "Us%d" % s])
+
+        def built():
+            mm(bk[4][:, hi], I, T.yk[:], True, False, ["yk"] + K, "b4")
+            mm(bk[4][:, hi], In, T.cn[:], False, False, ["cn"] + K, "b4")
+            mm(bk[4][:, hi], NB, T.nbs[:], False, True, ["nbs"] + K, "b4")
+            act(X[:, wt:wt + P], bk[4][:, hi], ACT.Relu, wr=["b4", "Xnew"])
+
+        def record():
+            c1 = 128 - 16 * ((-d) % 8)
+            flags(3, lo, WR, st=True)
+            mm(bk[3][:, lo], T.zw16[:, 15:143], T.pc[:], False, False, ["pc"] + K, "b3")
+            mm(bk[3][:, lo], T.zw16[:, 14 + c1:142 + c1], T.pm[:], False, False, ["pm"] + K, "b3")
+            mm(bk[3][:, lo], NB, T.nbs[:], False, True, ["nbs"] + K, "b3")
+            act(T.recb[:, P * t:P * t + P], bk[3][:, lo], ACT.Relu, T.col[:, 6:7], rd=K, wr=["b3", "recb"])
+
+        def moves():
+            cp(win.indirect(T.cs[:, t, :]), T.cn[:], ["X", "cs%d" % t, "cn"], ["X"], S256)
+            scan(T.sml[:], T.rm[:], bk[1][:, lo], 131072.0, ALU.min, ALU.max, K, ["b1", "sml"])
+            ts(T.ms[:, t, :], T.sml[:, 15:256:16], OFF, ALU.add, rd=["sml"], wr=["ms%d" % t], n=16)
+            tt(T.tg[:], win.indirect(T.ms[:, t, :]), T.vf[:], ALU.max, ["X", "ms%d" % t, "vf"], ["tg"], G256)
+            tt(win.indirect(T.ms[:, t, :]), T.tg[:], T.nvf[:], ALU.add, ["X", "tg", "nvf"], ["X"], S256)
+            for n, u in enumerate(gens):
+                old = X[:, 0:XO + W0 + P * u]
+                for lst, w_, u_ in ((T.cs, "wh", "uh"), (T.ms, "wf", "uf")):
+                    tt(T.tg[:], old.indirect(lst[:, u, :]), T[u_][:, n, :], ALU.min, ["X", "%s%d" % (u_, n)], ["tg"], G256)
+                    tt(old.indirect(lst[:, u, :]), T.tg[:], T[w_][:, n, :], ALU.add, ["X", "tg", "%s%d" % (w_, n)], ["X", "XA%d" % n], S256)
+
+        if t in ASIDE:
+            moves()
+        if len(gens) == 1:
+            aside(supports)
+        if t in ASIDE:
+            mm(bk[0][:, hi], T.in32[:], cn, False, False, ["CN"] + K, "b0", 1024)
+            mm(bk[6][:, hi], T.i32[:], cn, True, False, ["CN"] + K, "b6", 1024)
+            if gens:
+                mm(bk[6][:, hi], T.in32[:], T.mrs[:], False, False, ["mrs"] + K, "b6", 1024)
+            mm(bk[0][:, hi], NB, T.nbs[:], False, True, ["nbs"] + K, "b0")
+            act(T.crs[:], bk[0][:, hi], ACT.Relu, wr=["b0", "crs"])
+            mm(bk[6][:, hi], T.i32[:], T.crs[:], False, True, ["crs"] + K, "b6", 1024)
+            act(T.mrs[:], bk[6][:, hi], ACT.Identity, MAGIC, wr=["b6", "mrs"])
+            if t < R - 1:
+                act(cn, bk[6][:, hi], ACT.Copy, wr=["b6", "CN"])
+                act(T.Cf[:, s:A:2], T.mrs[:], ACT.Identity, -MAGIC, rd=["mrs"], wr=["Cf"])
+            else:
+                act(cn, T.mrs[:], ACT.Identity, -MAGIC - 256, rd=["mrs"], wr=["CN"])
+                act(T.CN[:, 1 - s:A:2], T.Cf[:, 1 - s:A:2], ACT.Identity, -256.0, rd=["Cf"], wr=["CN"])
+        if t < R - 1:
+            mm(bk[2][:, hi], T.i32[:], cn, True, False, ["CN"] + K, "b2", 1024)
+            mm(bk[2][:, hi], T.in32[:], T.Cf[:, s:A:2], False, True, ["Cf"] + K, "b2", 1024)
+            act(T.Nb[:, s:A:2], bk[2][:, hi], ACT.Copy, wr=["b2", "Nb"])
+            aside(cp, T.Mu[:], T.Cf[:].indirect(T.bu[:]), ["Cf", "bu"], ["Mu"], G256)
+            if t < R - 2:
+                aside(cp, T.Lu[:, s, :], T.Cf[:, s:A:2], ["Cf"], ["Lu%d" % s])
+        if t not in ASIDE:
+            moves()
+        aside(built)
+        aside(record)
+
+    dma("A", T.stf[:, :, 0:128], T.CN[:], ["CN"], ["stf3"], 256)
+    for e in range(3):
+        dma("A", T.stf[:, :, 128 + 24 * e:152 + 24 * e], T.recb[e:128:16, :], ["recb"], ["stf%d" % e], 48)
+    SF = ["stf0", "stf1", "stf2", "stf3"]
+    dma("A", T.lnf[me], T.stf[me], SF, ["lnfo"], 100)
+    for c, (a, b) in enumerate(CH):
+        dma("S", T["sto%d" % c][:], X[:, XO + a:XO + b], XK if c else ["XA0", "Xnew"], ["sto%d" % c], 340)
+    for c in range(NCH):
+        exchange(3 + c, T["sto%d" % c], T["lno%d" % c], ["sto%d" % c], ["lno%d" % c], 88)
+        if c == 0:
+            exchange(2, T.stf, T.lnf, SF, ["lnf"], 100)
+    dma("A", T.xo[r32, :], X[r32, XO:XO + 4096], XK + ["sto1", "sto2"], [], 256)
     for c in range(NCH):
         for a, b in ((0, me), (me + 1, N)):
             if b > a:
-                dma("S", T.xo[32 * a:32 * b, CH[c][0]:CH[c][1]], T["lno%d" % c][a:b], ["lno%d" % c], [])
-    dma("A", T.co[:], T.lnf[:, :, 0:128], ["lnf", "lnfo"], [])
+                dma("S", T.xo[32 * a:32 * b, CH[c][0]:CH[c][1]], T["lno%d" % c][a:b], ["lno%d" % c], [], 170)
+    dma("A", T.co[:], T.lnf[:, :, 0:128], ["lnf", "lnfo"], [], 256)
     for e in range(3):
-        dma("A", T.rec[8 * e:8 * e + 8, :], T.lnf[:, :, 128 + 24 * e:152 + 24 * e], ["lnf", "lnfo"], [])
-    emit(g, T, ops)
+        dma("A", T.rec[8 * e:8 * e + 8, :], T.lnf[:, :, 128 + 24 * e:152 + 24 * e], ["lnf", "lnfo"], [], 48)
+    emit(g, T, ops, lazy)

@@ -7,16 +7,19 @@ ALU, ACT = AluOpType, ActivationFunctionType
 N = 4
 W0, P, R, A = 2560, 256, 6, 512
 WT = [1, 64, 5, 83, 17, 131, 29, 211, 43, 157, 61, 239, 71, 113, 97, 199]
-KRS = [(8, 8)] * 6
-ORDER = ["y0 h0 n0 r0 y1 m0 h1 s0 p0 r1 b0 m1 s1 l0 p1 b1"] + ["y0 h0 r0 y1 m0 h1 n0 s0 r1 p0 b0 m1 s1 l0 p1 b1"] * 5
+KRS = [(8, 8)] + [(6, 6)] * 5
+ORDER = ["y0 h0 n0 r0 y1 m0 h1 s0 p0 r1 b0 m1 s1 l0 p1 b1"] + ["y0 h0 y1 m0 h1 n0 p0 r0 s0 r1 m1 b0 s1 l0 p1 b1"] * 5
 FAST = True
 HA = False
 PASSES = 1
-WAKE = 150
-GAP = 100
-OVER = 200
-ZW = [8, 8, 4, 4, 0, 0]
-ZV = [2, 2, 0, 0, 0, 0]
+WAKE = 220
+GAP = 120
+OVER = 250
+NEK = True
+GX = 1.2
+MSL = True
+ZW = [0, 0, 0, 0, 0, 0]
+ZA = [8, 8, 4, 4, 2, 0]
 ASIDE = (5,)
 NP = 3
 NA = (4, 4)
@@ -51,7 +54,7 @@ SCRATCH = {
     "bi": ("sbuf", [128, 16], I32), "it": ("sbuf", [128, 48], I32), "PT": ("sbuf", [128, 112], B), "lf": ("sbuf", [128, 16], F),
     "t3": ("sbuf", [128, 32], I32), "bl": ("sbuf", [128, 32], I32),
     "bc": ("sbuf", [128, 16], F), "bu": ("sbuf", [128, 16], U16), "cu": ("sbuf", [128, 16], U16), "mu": ("sbuf", [128, 16], U16),
-    "cs": ("sbuf", [128, R, 16], U16), "ms": ("sbuf", [128, R, 16], U16), "ex": ("sbuf", [128, 16], U16),
+    "cs": ("sbuf", [128, R, 16], U16), "ms": ("sbuf", [128, R, 16], U16), "ex": ("sbuf", [128, 32], U16),
     "i4": ("sbuf", [128, 128], B), "i32": ("sbuf", [128, 128], F), "bow": ("sbuf", [128, 272], B),
     "zw": ("sbuf", [128, 272], B), "zw32": ("sbuf", [128, 272], F), "zw16": ("sbuf", [128, 272], H16), "bo16": ("sbuf", [128, 128], H16),
     "pc": ("sbuf", [128, 256], H16), "pm": ("sbuf", [128, 256], H16),
@@ -91,7 +94,7 @@ def engine_split(core, peers, topo):
 
 def apart(k):
     return (len(k) == 2 and k[0] == "b" and k[1].isdigit()) or k.rstrip("01") in (
-        "K", "KA", "KB", "KF", "So", "zrep", "zrepV", "ad", "mym", "myr", "wrow", "selm", "recb", "bi")
+        "K", "KA", "KB", "KF", "So", "zrep", "zrepV", "zrepA", "ad", "mym", "myr", "wrow", "selm", "recb", "bi")
 
 
 def arrange(ops, lazy):
@@ -228,7 +231,7 @@ def rank_program(g, core, T, topo):
         lazy.update(range(n, len(ops)))
 
     def op(e, fn, rd, wr, n):
-        busy = {"V": 55 + 0.87 * n, "A": 70 + 0.87 * n, "T": 10 + 0.44 * n, "G": 170 + 0.87 * n}[e]
+        busy = {"V": 40 + 0.87 * n, "A": 50 + 0.87 * n, "T": 8 + 0.44 * n, "G": GX * (170 + 0.87 * n)}[e]
         ops.append((e, fn, list(rd), list(wr), None, busy, 0))
 
     def dma(e, out, in_, rd, wr, kb):
@@ -374,7 +377,9 @@ def rank_program(g, core, T, topo):
     ts(T.col[:, 6:7], T.col[:, 8:9], OFF - 256.0, ALU.add, rd=["col8"], wr=["K"], n=1)
     iota(T.rm[:], [[0, 256]], 131072, 0, ["rm"])
     ts(T.rm[:, 0:256:16], T.lf[:], ce, ALU.subtract, rd=["rm", "lf", "colg"], wr=["rm"], n=16)
-    cp(T.ex[:], T.i16[:, 0:16], ["i16"], ["K"], 16)
+    cp(T.ex[:, 0:16], T.i16[:, 0:16], ["i16"], ["K"], 16)
+    for h in range(2):
+        cp(T.ex[:, 16 + 8 * h:24 + 8 * h], T.i16[:, h:16:2], ["i16"], ["K"], 8)
     iota(T.c256[:], [[0, 256]], 256, 0, ["KG"])
     iota(T.ones[:, 0:128], [[0, 128]], 1, 0, ["KG"])
     ms(T.ones[0:2, 128:256], 496.0, ["c496"], 64)
@@ -455,7 +460,7 @@ def rank_program(g, core, T, topo):
     act(T.bow[:], T.zw[:], ACT.Identity, 0.0, T.col[:, 9:10], rd=["col9", "zw"], wr=["bow"])
     ts(T.bc[:], T.bl[:, 0:16], -256.0, ALU.add, rd=["bl0", "bl1"], wr=["bc"], n=16)
     ts(T.Lu[:, 1, :], T.pli[:, 1:A:2], 256.0, ALU.add, rd=["pli"], wr=["Lu1"])
-    tt(T.nbs[:], T.bc[:].indirect(T.ex[:]), T.dm[:], ALU.mult, ["bc", "dm", "K"], ["nbs"], G256)
+    tt(T.nbs[:], T.bc[:].indirect(T.ex[:, 0:16]), T.dm[:], ALU.mult, ["bc", "dm", "K"], ["nbs"], G256)
 
     for t in range(R):
         s, par = t % 2, t % 2
@@ -478,7 +483,7 @@ def rank_program(g, core, T, topo):
 
         def far(h):
             tt(T.mh[:, 2048 * h:2048 * h + 2048], win.indirect(T.Mu[:, H[h]]), T.zrep[:, 2048 * h:2048 * h + 2048], ALU.min,
-               XK + ["Mu", "zrep%d" % h, "zrepV%d" % h], ["mh%d" % h], 8 * G256)
+               XK + ["Mu", "zrep%d" % h, "zrepV%d" % h, "zrepA%d" % h], ["mh%d" % h], 8 * G256)
 
         def relus(h):
             for n, k0 in enumerate(range(16 - KRS[t][h], 16, 4)):
@@ -526,8 +531,7 @@ def rank_program(g, core, T, topo):
                     tt(T.So[:, 4352:4368], T.So[:, 4111:4352:16], T.lf[:], ALU.add, ["Sol", "lf"], ["am0"], 32)
                 if (h, b) == (1, 2):
                     tt(T.So[:, 4368:4384], T.So[:, 63:1024:64], T.So[:, 1087:2048:64], ALU.min, ["So00", "So01", "So10", "So11"], ["am1"], 32)
-            if h:
-                tt(T.So[:, 4384:4400], T.So[:, 4352:4368], T.So[:, 2111:3072:64], ALU.min, ["am0", "So02", "So12"], ["am2"], 32)
+                    tt(T.So[:, 4384:4400], T.So[:, 4352:4368], T.So[:, 2111:3072:64], ALU.min, ["am0", "So02", "So12"], ["am2"], 32)
 
         def least(h):
             scan(T.So[:, 4096:4352], T.d0[:, 1024:1280], bk[6][:, lo], 0.0, ALU.add, ALU.min, ["d0l"], ["b6", "Sol"])
@@ -551,22 +555,31 @@ def rank_program(g, core, T, topo):
         mm(bk[0][:, lo], In, T.od[:], True, False, K, "b0")
         mm(bk[1][:, lo], In, T.od8[:], True, False, K, "b1")
         mm(bk[2][:, hi], In, T.od[:], True, False, K, "b2")
-        tt(T.So[:, 4400:4416], T.So[:, 4368:4384], T.So[:, 3135:4096:64], ALU.min, ["am1", "So03", "So13"], ["am3"], 32)
+        tt(T.So[:, 4400:4416], T.So[:, 4368:4384], T.So[:, 4384:4400], ALU.min, ["am1", "am2"], ["am3"], 32)
         for h in range(2):
-            tt(T.bi[:, h:16:2], T.So[:, 4400 + 8 * h:4408 + 8 * h], T.So[:, 4384 + 8 * h:4392 + 8 * h], ALU.min, ["am3", "am2"], ["bi"], 16)
+            tt(T.bi[:, h:16:2], T.So[:, 4400 + 8 * h:4408 + 8 * h], T.So[:, 3135 + 512 * h:3584 + 512 * h:64], ALU.min, ["am3", "So%d3" % h], ["bi"], 16)
         ts(T.it[:, 0:16], T.bi[:], 5, ALU.arith_shift_right, 15, ALU.bitwise_and, rd=["bi"], wr=["ki"], n=16)
         ts(T.it[:, 16:32], T.bi[:], 31, ALU.bitwise_and, rd=["bi"], wr=["li"], n=16)
         ts(T.it[:, 32:48], T.bi[:], 16, ALU.bitwise_and, rd=["bi"], wr=["ni"], n=16)
         tt(T.PT[:, 48:80], T.it[:, 0:32], T.it[:, 0:32], ALU.mult, ["ki", "li"], ["PTs"], 64)
         cp(T.PT[:, 0:48], T.it[:], ["ki", "li", "ni"], ["PTk"], 48)
+        if NEK:
+            tt(T.tg[:], T.it[:, 0:16].indirect(T.ex[:, 16:32]), T.i16[:], ALU.not_equal, ["ki"] + K, ["tg"], G256)
         for h in range(2):
             mm(bk[7][0:NF, 256 + 128 * h:384 + 128 * h], T.PT[:, h:112:2], I, True, True, ["PTs", "PTk", "PTb", "PT1", "iw"], "b7", 128)
-        cp(FL, bk[7][0:NF, hi], [], ["b7", "FL"])
+        if NEK:
+            act(FL, bk[7][0:NF, hi], ACT.Copy, wr=["b7", "FL"])
+        else:
+            cp(FL, bk[7][0:NF, hi], [], ["b7", "FL"])
 
         def flags(bank, half, w, st=False, sp=False):
             mm(bk[bank][:, half], w, FL, st, sp, ["FL", "KW0", "KW1", "KN0"] + K, "b%d" % bank)
 
-        flags(4, lo, KP, sp=True)
+        if NEK:
+            for h in range(2):
+                mm(bk[4][:, H[h]], T.tg[:, H[h]], I8, False, h == 1, ["tg"] + K, "b4", 128)
+        else:
+            flags(4, lo, KP, sp=True)
         ts(T.pc[:], bk[4][:, lo], -MID, ALU.add, -LOW, ALU.max, wr=["b4", "pc"])
         flags(5, lo, sh(T.LP, d, NF), sp=True)
         ts(T.pm[:], bk[5][:, lo], -MID, ALU.add, -LOW, ALU.max, wr=["b5", "pm"])
@@ -617,16 +630,15 @@ def rank_program(g, core, T, topo):
             mm(bk[7][:, hi], sh(T.iw, dn), z, True, False, [zk] + K, "b7")
             mm(bk[7][:, hi], sh(T.inw, dn), T.yk[:], False, True, ["yk"] + K, "b7")
             act(T.zf[:, 1 - par, :], bk[7][:, hi], ACT.Abs, wr=["b7", "zf%d" % (1 - par)])
-            for j in range(16):
+            for j in range(16 - ZA[t]):
                 if j < ZW[t]:
                     repeat(j, 1 - par, 0, 256, ["zrep0", "zrep1"])
                 else:
                     repeat(j, 1 - par, 0, 128, ["zrep0"])
-            for j in range(ZW[t], 16):
-                if j < 16 - ZV[t]:
-                    repeat(j, 1 - par, 128, 256, ["zrep1"])
-                else:
-                    aside(cp, T.zrep[:, 2048 + j:4096:16], T.zf[:, 1 - par, H[1]], ["zf%d" % (1 - par)], ["zrepV1"], 64)
+            for j in range(ZW[t], 16 - ZA[t]):
+                repeat(j, 1 - par, 128, 256, ["zrep1"])
+            for j in range(16 - ZA[t], 16):
+                aside(act, T.zrep[:, j:4096:16], T.zf[:, 1 - par, :], ACT.Copy, 0.0, 1.0, ["zf%d" % (1 - par)], ["zrepA0", "zrepA1"])
 
         def rests():
             mm(bk[6][:, lo], I, z, True, False, [zk] + K, "b6")

import math
from concourse.bass import DstId, RemoteDMATransfer
from concourse.mybir import AluOpType, ActivationFunctionType, AxisListType

ALU, ACT = AluOpType, ActivationFunctionType

N = 4
W0, P, R, A = 2560, 256, 6, 512
WT = [1, 64, 5, 83, 17, 131, 29, 211, 43, 157, 61, 239, 71, 113, 97, 199]
KRS = [(8, 8)] + [(6, 6)] * 5
ORDER = ["y0 h0 n0 r0 y1 m0 h1 s0 p0 r1 b0 m1 s1 l0 p1 b1"] + ["y0 h0 y1 m0 h1 n0 p0 r0 s0 r1 m1 b0 s1 l0 p1 b1"] * 5
FAST = True
HA = False
PASSES = 1
WAKE = 220
GAP = 120
OVER = 250
NEK = True
GX = 1.2
MSL = True
ZW = [0, 0, 0, 0, 0, 0]
ZA = [8, 8, 4, 4, 2, 0]
ASIDE = (5,)
NP = 3
NA = (4, 4)
MAGIC = 1.5 * 2 ** 23
XO = 256
BIG = 8192.0
LOW, MID = 2048.0, 2303.0
OFF = MID + 15 * LOW
CH = [(2816, 4096), (0, 1408), (1408, 2816)]
NCH = len(CH)
XH = W0 // 2
NF = 56

F, B, I32, U16, H16 = "float32", "bfloat16", "int32", "uint16", "float16"
SCRATCH = {
    "sti": ("dram", [N, 128, 132], I32), "lni": ("dram", [N, 128, 132], I32),
    "stn": ("dram", [N, 128, 128], B), "lnn": ("dram", [N, 128, 128], B), "plh": ("sbuf", [128, A + 160], I32),
    "stb": ("dram", [N, 128, 384], B), "lnb": ("dram", [N, 128, 384], B),
    "stc": ("dram", [N, 128, 320], B), "lnc": ("dram", [N, 128, 320], B),
    "stf": ("dram", [N, 128, 200], F), "lnf": ("dram", [N, 128, 200], F),
    "X": ("sbuf", [128, XO + 4096], B), "y": ("sbuf", [128, 4096], B), "mh": ("sbuf", [128, 4096], B),
    "my": ("sbuf", [128, 4096], B), "zrep": ("sbuf", [128, 4096], B), "zf": ("sbuf", [128, 2, 256], B),
    "Eb": ("sbuf", [128, 4096], F), "ad": ("sbuf", [128, 2048], B), "eqa": ("sbuf", [128, 2048], B),
    "in32": ("sbuf", [128, 128], F), "w2": ("sbuf", [128, 272], F), "d0": ("sbuf", [128, 1280], F), "So": ("sbuf", [128, 4416], F),
    "selm": ("sbuf", [128, 4096], B), "nil": ("sbuf", [128, 512], B), "eq": ("sbuf", [128, 32, 256], B),
    "nmb": ("sbuf", [128, W0], B), "pli": ("sbuf", [128, A], I32), "plu": ("sbuf", [128, A], U16),
    "CN": ("sbuf", [128, A], F), "Cf": ("sbuf", [128, A], F), "Nb": ("sbuf", [128, A], B),
    "Lu": ("sbuf", [128, 2, 256], U16), "Mu": ("sbuf", [128, 256], U16), "NM": ("sbuf", [128, 256], B),
    "Ls": ("sbuf", [128, 2, 256], F), "Us": ("sbuf", [128, 2, 256], F), "recb": ("sbuf", [128, 1536], F),
    "wh": ("sbuf", [128, 2, 256], B), "wf": ("sbuf", [128, 2, 256], B), "uh": ("sbuf", [128, 2, 256], B), "uf": ("sbuf", [128, 2, 256], B),
    "z": ("sbuf", [128, 2, 256], B), "r16": ("sbuf", [128, 2, 256], U16),
    "bi": ("sbuf", [128, 16], I32), "it": ("sbuf", [128, 48], I32), "PT": ("sbuf", [128, 112], B), "lf": ("sbuf", [128, 16], F),
    "t3": ("sbuf", [128, 32], I32), "bl": ("sbuf", [128, 32], I32),
    "bc": ("sbuf", [128, 16], F), "bu": ("sbuf", [128, 16], U16), "cu": ("sbuf", [128, 16], U16), "mu": ("sbuf", [128, 16], U16),
    "cs": ("sbuf", [128, R, 16], U16), "ms": ("sbuf", [128, R, 16], U16), "ex": ("sbuf", [128, 32], U16),
    "i4": ("sbuf", [128, 128], B), "i32": ("sbuf", [128, 128], F), "bow": ("sbuf", [128, 272], B),
    "zw": ("sbuf", [128, 272], B), "zw32": ("sbuf", [128, 272], F), "zw16": ("sbuf", [128, 272], H16), "bo16": ("sbuf", [128, 128], H16),
    "pc": ("sbuf", [128, 256], H16), "pm": ("sbuf", [128, 256], H16),
    "w1": ("sbuf", [128, 272], F), "col": ("sbuf", [128, 16], F), "oh": ("sbuf", [128, 32], F),
    "coli": ("sbuf", [128, 8], I32), "wrow": ("sbuf", [128, 32], F),
}
for _n in ["FL", "ya", "yk", "hm", "cn", "vf", "nvf", "nbs", "sga", "sgb", "tg",
           "iw", "inw", "i8w", "bo", "bo8", "bop", "bon", "od", "od8", "dm", "i256", "c256", "ones",
           "Sel", "SG", "LP", "WC", "KW", "KN", "WQ", "WR"]:
    SCRATCH[_n] = ("sbuf", [128, 256], B)
for _n in ["scl", "sml", "sm2", "crs", "mrs", "Gs", "Mf", "rm", "i16"]:
    SCRATCH[_n] = ("sbuf", [128, 256], F)
for _c in range(NCH):
    SCRATCH["sto%d" % _c] = ("dram", [N, 128, (CH[_c][1] - CH[_c][0]) // 4], B)
    SCRATCH["lno%d" % _c] = ("dram", [N, 128, (CH[_c][1] - CH[_c][0]) // 4], B)
for _b in range(8):
    SCRATCH["pb%d" % _b] = ("psum", [128, 512], F)
SEMAPHORES = ["sV", "sA", "sT", "sG"] + ["d%d" % _i for _i in range(56)] + ["ar%d" % _i for _i in range(5 + NCH)] + ["ls%d" % _i for _i in range(5 + NCH)]


def engine_split(core, peers, topo):
    far = [p for p in peers if topo.chip(p) != topo.chip(core)]
    near = [p for p in peers if p not in far]
    out, used = {}, []
    for grp in (far, near):
        if not grp:
            continue
        free = [e for e in topo.engines(core, grp[0]) if e not in used]
        n = 1
        while 2 * n * len(grp) <= len(free):
            n *= 2
        for i, p in enumerate(grp):
            out[p] = free[i * n:(i + 1) * n]
            used += out[p]
    return out


def apart(k):
    return (len(k) == 2 and k[0] == "b" and k[1].isdigit()) or k.rstrip("01") in (
        "K", "KA", "KB", "KF", "So", "zrep", "zrepV", "zrepA", "ad", "mym", "myr", "wrow", "selm", "recb", "bi")


def arrange(ops, lazy):
    lastw, readers, sure, after = {}, {}, [], []
    for i, (e, fn, rd, wr, sig, busy, lat) in enumerate(ops):
        s, a = set(lastw[k] for k in rd if k in lastw), set()
        for k in wr:
            j = lastw.get(k)
            if j is not None:
                weak = k[:2] == "o:" or (ops[j][0] == e and ops[j][4] is None and sig is None and apart(k))
                (a if weak else s).add(j)
            s.update(readers.get(k, []))
        sure.append(s)
        after.append(a - s)
        for k in rd:
            readers.setdefault(k, []).append(i)
        for k in wr:
            lastw[k] = i
            readers[k] = []

    def gap(j, i, strong):
        return ops[j][5] + (ops[j][6] + WAKE if strong else 0)

    rank = [len(ops) if i in lazy else i for i in range(len(ops))]
    for i in range(len(ops) - 1, -1, -1):
        for j in sure[i] | after[i]:
            rank[j] = min(rank[j], rank[i])
    ahead, behind = [[] for _ in ops], [[] for _ in ops]
    for i in range(len(ops)):
        for js, strong in ((sure[i], True), (after[i], False)):
            for j in js:
                ahead[i].append((j, gap(j, i, strong)))
                behind[j].append((i, gap(j, i, strong) + ops[i][5] - ops[j][5]))

    def place(turn, edges, first):
        start, slots = [0.0] * len(ops), {}
        for i in turn:
            t = max([first[i]] + [start[j] + w for j, w in edges[i]])
            if ops[i][0] is not None:
                sl = slots.setdefault(ops[i][0], [])
                n = bisect(sl, t)
                while n < len(sl) and sl[n][0] < t + min(ops[i][5], max(GAP, ops[i][5] - OVER)):
                    t = max(t, sl[n][1])
                    n += 1
                sl.insert(n, (t, min([t + ops[i][5]] + [x[0] for x in sl[n:n + 1]])))
            start[i] = t
        return start

    every, zero = range(len(ops)), [0.0] * len(ops)
    start = place(sorted(every, key=lambda i: (rank[i], i)), ahead, zero)
    for _ in range(PASSES):
        back = place(sorted(every, key=lambda i: (-start[i] - ops[i][5], -i)), behind, [o[6] for o in ops])
        start = place(sorted(every, key=lambda i: (-back[i] - ops[i][5], i)), ahead, zero)
    return sure, sorted(every, key=lambda i: (start[i], i))


def bisect(slots, t):
    a, b = 0, len(slots)
    while a < b:
        m = (a + b) // 2
        if slots[m][1] > t:
            b = m
        else:
            a = m + 1
    return a


def emit(g, T, ops, lazy):
    Q = {"V": g.vector, "A": g.scalar, "T": g.tensor, "G": g, "S": g.sync}
    sure, order = arrange(ops, lazy)
    place = {i: n for n, i in enumerate(order)}
    clock, pos, need, waits, done, last = {k: {} for k in Q}, {k: 0 for k in Q}, set(), {}, {}, {}
    for i in order:
        e, sig = ops[i][0], ops[i][4]
        waits[i] = []
        if e is not None:
            ck = clock[e]
            for j in sorted(sure[i], key=lambda j: -place[j]):
                src, val, know = done[j]
                if ck.get(src, -1) >= val:
                    continue
                waits[i].append(j)
                need.add(j)
                for a, b in know.items():
                    ck[a] = max(ck.get(a, -1), b)
                ck[src] = val
            pos[e] += 1
            if sig is None:
                last[e] = i
        done[i] = (e if sig is None else sig[0], pos[e] if sig is None else 0, dict(clock[e]) if e is not None else {})
    need |= set(last.values())
    cnt, at = {k: 0 for k in Q}, {}
    for i in order:
        e, sig = ops[i][0], ops[i][4]
        if sig is not None:
            at[i] = sig
        elif i in need:
            cnt[e] += 1
            at[i] = ("s" + e, cnt[e])
    for i in order:
        e, fn, sig = ops[i][0], ops[i][1], ops[i][4]
        if e is None:
            continue
        for j in waits[i]:
            Q[e].wait_ge(T.sem[at[j][0]], at[j][1])
        ins = fn(Q[e])
        if sig is not None:
            if sig[0][0] == "d":
                ins.then_inc(T.sem[sig[0]], 16)
        elif i in need:
            ins.then_inc(T.sem[at[i][0]], 1)
    for o in ops:
        if o[4] is not None:
            g.wait_ge(T.sem[o[4][0]], o[4][1])
    for k in cnt:
        if cnt[k]:
            g.wait_ge(T.sem["s" + k], cnt[k])


def rank_program(g, core, T, topo):
    me = T.rank_of(core)
    if me is None:
        return
    cores = list(T.cores)
    peers = [c for c in cores if c != core]
    mine = engine_split(core, peers, topo)
    arrive = sum(len(engine_split(c, [x for x in cores if x != c], topo)[core]) for c in peers)
    ops, nd, stops, lazy = [], [0], set(), set()
    GATHER, SCATTER = 1.4, 3.0

    def aside(fn, *args):
        n = len(ops)
        fn(*args)
        lazy.update(range(n, len(ops)))

    def op(e, fn, rd, wr, n):
        busy = {"V": 40 + 0.87 * n, "A": 50 + 0.87 * n, "T": 8 + 0.44 * n, "G": GX * (170 + 0.87 * n)}[e]
        ops.append((e, fn, list(rd), list(wr), None, busy, 0))

    def dma(e, out, in_, rd, wr, kb):
        ops.append((e, lambda q: q.dma_start(out, in_), list(rd), list(wr) + ["o:" + e], ("d%d" % nd[0], 16), 60, 2000 + 8 * kb))
        nd[0] += 1

    def exchange(n, st, ln, rd, wr, kb):
        def fn(q):
            tr = []
            for c in peers:
                rid, pid, _ = topo.addr(c)
                tr.append(RemoteDMATransfer(dst_ids=[DstId(rid=rid, pnc=pid)], dma_engine_mask=sum(1 << e for e in mine[c]),
                                            remote_sem=T.sem["ar%d" % n], src=st[T.rank_of(c)], dst=ln[me]))
            return q.remote_dma_fused(tr, local_sem=T.sem["ls%d" % n])
        ops.append(("G", fn, list(rd), ["o:G", "o:x%d" % n], ("ls%d" % n, sum(len(v) for v in mine.values())), 600, 3000 + 30 * kb))
        ops.append((None, None, [], list(wr) + ["o:x%d" % n], ("ar%d" % n, arrive), 1, 3000 + 30 * kb))

    def ts(out, in0, s1, o0, s2=None, o1=None, rd=(), wr=(), n=256):
        if o1 is None:
            op("V", lambda q: q.tensor_scalar(out, in0, s1, None, o0), rd, wr, n)
        else:
            op("V", lambda q: q.tensor_scalar(out, in0, s1, s2, o0, o1), rd, wr, n)

    def tt(out, in0, in1, o, rd=(), wr=(), n=256):
        op("V", lambda q: q.tensor_tensor(out, in0, in1, o), rd, wr, n)

    def cp(out, in_, rd=(), wr=(), n=256):
        op("V", lambda q: q.tensor_copy(out, in_), rd, wr, n)

    def ms(ap, v, wr, n=16):
        op("V", lambda q: q.memset(ap, v), [], wr, n)

    def scan(out, a, b, init, o0, o1, rd=(), wr=(), n=256):
        op("V", lambda q: q.tensor_tensor_scan(out, a, b, init, o0, o1), rd, wr, n)

    def act(out, in_, func, bias=0.0, scale=1.0, rd=(), wr=(), n=256):
        if func == ACT.Copy:
            op("A", lambda q: q.activation(out, in_, func), rd, wr, n)
        else:
            op("A", lambda q: q.activation(out, in_, func, bias=bias, scale=scale), rd, wr, n)

    def mm(out, lhsT, rhs, st, sp, rd, bank, n=256):
        def fn(q):
            return q.matmul(out, lhsT, rhs, st, sp or fn in stops)
        op("T", fn, rd, [bank], max(64, n))

    def iota(out, pat, base, cm, wr, flt=True, rd=()):
        n = 2 * math.prod(p[1] for p in pat)
        if flt:
            op("G", lambda q: q.iota(out, pat, base, cm, allow_small_or_imprecise_dtypes=True), rd, wr, n)
        else:
            op("G", lambda q: q.iota(out, pat, base, cm), rd, wr, n)

    def sh(w, d, p=128):
        c = 128 - 16 * (d % 8)
        return w[0:p, c:c + 128]

    bk = [T["pb%d" % i] for i in range(8)]
    X, I, In, I8, I4 = T.X, T.iw[:, 128:256], T.inw[:, 128:256], T.i8w[:, 128:256], T.i4[:]
    lo, hi = slice(0, 256), slice(256, 512)
    H = [slice(0, 128), slice(128, 256)]
    r32 = slice(32 * me, 32 * me + 32)
    G256, S256 = 256 * GATHER, 256 * SCATTER

    ms(T.nmb[:], 0.0, ["nm0"], 1280)
    dma("S", T.plh[:, A:A + 160], T.fr0[:], [], ["nm"], 80)
    dma("A", T.stb[:, :, 0:320], T.x0[:, 0:XH], [], ["stb0"], 320)
    dma("S", T.stb[:, :, 320:384], T.z0[:], [], ["stb1"], 64)
    dma("A", T.plh[:, 0:A], T.pl[:], [], ["plh"], 256)
    dma("S", T.sti[:, :, 0:128], T.pl[:], [], ["sti0"], 256)
    dma("S", T.sti[:, :, 128:132], T.b0[:], [], ["sti2"], 64)
    dma("A", T.stc[:], T.x0[:, XH:W0], [], ["stc"], 500)
    dma("A", T.lni[me, :, 0:128], T.pl[r32, :], [], ["lni0"], 64)
    dma("A", T.lni[me, :, 128:132], T.b0[r32, :], [], ["lni2"], 16)
    dma("S", T.lnb[me, :, 320:384], T.z0[r32, :], [], ["lnb1"], 16)

    iota(T.coli[:, 0:1], [[0, 1]], 0, 1, ["coli0"], False)
    iota(T.w1[:, 0:256], [[0, 2], [1, 128]], 0, 0, ["w1"])
    iota(T.w2[:, 0:256], [[0, 2], [1, 8], [0, 16]], 0, 0, ["w2"])
    iota(T.i16[:], [[0, 16], [1, 16]], 0, 0, ["i16"])
    iota(T.So[:, 0:272], [[1, 272]], -16, 0, ["w3"])
    exchange(1, T.stb, T.lnb, ["stb0", "stb1"], ["lnb"], 96)
    exchange(0, T.sti, T.lni, ["sti0", "sti2"], ["lni"], 66)
    exchange(4 + NCH, T.stc, T.lnc, ["stc"], ["lnc"], 80)
    iota(T.lf[:], [[-16, 16]], 255 - int(OFF), 0, ["lf"])
    iota(T.i256[:], [[1, 256]], 0, 0, ["KG"])
    cp(T.col[:, 0:1], T.coli[:, 0:1], ["coli0"], ["colp"], 1)
    for c, (v, o) in enumerate(((4, ALU.arith_shift_right), (15, ALU.bitwise_and), (3, ALU.arith_shift_right), (7, ALU.bitwise_and))):
        ts(T.coli[:, 1 + c:2 + c], T.coli[:, 0:1], v, o, rd=["coli0"], wr=["coli%d" % (1 + c)], n=1)
    cp(T.col[:, 1:5], T.coli[:, 1:5], ["coli1", "coli2", "coli3", "coli4"], ["colg"], 4)
    cp_, cg, ce = T.col[:, 0:1], T.col[:, 1:2], T.col[:, 2:3]
    ts(T.iw[:], T.w1[:, 0:256], cp_, ALU.is_equal, rd=["w1", "colp"], wr=["iw"])
    ts(T.bo[:], T.w2[:, 0:256], cg, ALU.is_equal, rd=["w2", "colg"], wr=["bo"])
    ts(T.Sel[:], T.w2[:, 0:256], T.col[:, 4:5], ALU.is_equal, rd=["w2", "colg"], wr=["Sel"])
    ts(T.hm[:, 0:160], T.plh[:, A:A + 160], -256.0, ALU.add, 1.0 / 1024, ALU.mult, rd=["nm"], wr=["hm"], n=160)
    dma("S", T.nmb[0:128:16, :], T.hm[:, 0:160], ["nm0", "hm"], ["nmb"], 40)
    dma("S", X[r32, XO:XO + W0], T.x0[r32, :], ["stc"], ["Xown"], 160)
    ts(T.wrow[:, 16:32], T.i16[:, 0:16], ce, ALU.is_equal, 2.0 ** 32, ALU.mult, rd=["i16", "colg"], wr=["rowm"], n=16)
    act(T.inw[:], T.iw[:], ACT.Identity, 0.0, -1.0, rd=["iw"], wr=["KA"])
    act(X[:, 0:XO], T.iw[:], ACT.Identity, 0.0, 0.0, rd=["iw"], wr=["X"])
    for j in range(4):
        act(T.nil[:, j:512:4], T.iw[:, 0:128], ACT.Identity, 0.0, -2.0 ** 32, rd=["iw"], wr=["KA"], n=128)
    for out, v in ((T.bop, 512.0), (T.bon, -512.0)):
        act(out[:], T.bo[:], ACT.Identity, 0.0, v, rd=["bo"], wr=["KA"])

    def make_selm(s):
        for l in range(16):
            c = 2048 * s + 512 * (l // 4)
            act(T.selm[:, c + l % 4:c + 512:4], sh(T.bo, -2 * (1 + s)), ACT.Identity, 0.0, T.wrow[:, 16 + l:17 + l], rd=["rowm", "bo"], wr=["selm%d" % s], n=128)
    ts(T.od[:], T.i16[:], ce, ALU.not_equal, 32768.0, ALU.mult, rd=["i16", "colg"], wr=["od"])

    cp(T.plu[:], T.plh[:, 0:A], ["plh"], ["plu"], 512)
    for h in range(2):
        act(T.mh[:, 2048 * h:2048 * h + 2048], T.nmb[:].indirect(T.plu[:, 256 + 128 * h:384 + 128 * h]), ACT.Copy, rd=["nmb", "plu"], wr=["mh%d" % h], n=8 * G256)
    ts(T.col[:, 5:6], cg, 16.0, ALU.mult, rd=["colg"], wr=["col5"], n=1)
    ts(T.w1[:], T.So[:, 0:272], T.col[:, 5:6], ALU.subtract, rd=["w3", "col5"], wr=["w1"])
    ts(T.w2[:], T.w1[:], 0.0, ALU.is_equal, rd=["w1"], wr=["w2"])
    ts(T.So[:, 0:272], T.w1[:], 128.0, ALU.is_equal, rd=["w1"], wr=["w3"])
    tt(T.zw32[:], T.w2[:], T.So[:, 0:272], ALU.add, ["w2", "w3"], ["zw32"], 544)
    cp(T.zw[:], T.zw32[:], ["zw32"], ["zw"])
    for h in range(2):
        cp(T.my[:, 2048 * h:2048 * h + 2048], T.nmb[:].indirect(T.plu[:, H[h]]), ["nmb", "plu"], ["myn%d" % h], 8 * G256)
    for h in range(2):
        for c, buf, keys in ((1, T.mh, ["mh%d" % h]), (0, T.my, ["myn%d" % h, "mym%d" % h] + ["myr%d%d" % (h, n) for n in range(4)])):
            b = 2 * h + c
            for k in range(16):
                mm(bk[b][:, 0:128], T.zw[:, 16 - k:144 - k], buf[:, 2048 * h + k:2048 * h + 2048:16], k == 0, k == 15, keys + ["zw"], "b%d" % b, 128)
    for b in (1, 0, 3, 2):
        c = 256 * (b % 2) + 128 * (b // 2)
        act(T.ad[:, c:c + 128], bk[b][:, 0:128], ACT.Copy, wr=["b%d" % b, "ad"], n=128)
    dma("A", T.stn[:], T.ad[:, 0:512], ["ad"], ["stn"], 128)
    dma("A", T.Nb[r32, :], T.ad[r32, 0:512], ["ad"], ["Nbo"], 32)
    make_selm(0)
    make_selm(1)
    act(T.bo8[:], T.bo[:], ACT.Identity, 0.0, -BIG, rd=["bo"], wr=["KB"])
    for out, v, n in ((T.i8w, -BIG, 256), (T.i4, BIG / 2, 128), (T.i32, 1.0, 128), (T.in32, -1.0, 128)):
        act(out[:, 0:n], T.iw[:, 0:n], ACT.Identity, 0.0, v, rd=["iw"], wr=["KB"], n=n)
    cp(T.bo16[:], T.bo[:, 0:128], ["bo"], ["K"], 64)
    cp(T.zw16[:], T.zw[:], ["zw"], ["K"], 136)
    ts(T.od8[:], T.od[:], -BIG, ALU.add, rd=["od"], wr=["K"], n=128)
    ts(T.dm[:], T.i16[:], ce, ALU.is_equal, rd=["i16", "colg"], wr=["dm"])
    ts(T.col[:, 8:9], ce, 0.0, ALU.is_equal, 512.0 - OFF, ALU.mult, rd=["colg"], wr=["col8"], n=1)
    ts(T.col[:, 6:7], T.col[:, 8:9], OFF - 256.0, ALU.add, rd=["col8"], wr=["K"], n=1)
    iota(T.rm[:], [[0, 256]], 131072, 0, ["rm"])
    ts(T.rm[:, 0:256:16], T.lf[:], ce, ALU.subtract, rd=["rm", "lf", "colg"], wr=["rm"], n=16)
    cp(T.ex[:, 0:16], T.i16[:, 0:16], ["i16"], ["K"], 16)
    for h in range(2):
        cp(T.ex[:, 16 + 8 * h:24 + 8 * h], T.i16[:, h:16:2], ["i16"], ["K"], 8)
    iota(T.c256[:], [[0, 256]], 256, 0, ["KG"])
    iota(T.ones[:, 0:128], [[0, 128]], 1, 0, ["KG"])
    ms(T.ones[0:2, 128:256], 496.0, ["c496"], 64)
    ms(T.ones[0:1, 128:256], 2.0 ** 20, ["c496"], 64)
    ms(T.PT[:, 96:112], 1.0, ["PT1"])

    oh = [T.oh[:, j:j + 1] for j in range(32)]
    ts(T.oh[:, 0:8], T.i16[:, 0:8], T.col[:, 3:4], ALU.is_equal, rd=["i16", "colg"], wr=["oh"], n=8)
    ts(T.oh[:, 8:16], T.oh[:, 0:8], -BIG, ALU.mult, rd=["oh"], wr=["ohb"], n=8)
    tt(T.oh[:, 16:20:3], T.oh[:, 0:4:3], T.oh[:, 1:5:3], ALU.add, ["oh"], ["oh1"], 4)
    ts(T.oh[:, 20:22], T.oh[:, 11:13], oh[14], ALU.add, rd=["ohb"], wr=["oh2"], n=2)
    ts(oh[22], oh[8], -2.0, ALU.mult, oh[20], ALU.add, rd=["ohb", "oh2"], wr=["KF"], n=1)
    ts(oh[23], oh[9], -2.0, ALU.mult, oh[21], ALU.add, rd=["ohb", "oh2"], wr=["KF"], n=1)
    ts(oh[24], oh[10], -1.0 / 16, ALU.mult, oh[14], ALU.add, rd=["ohb"], wr=["KF"], n=1)
    ts(oh[25], oh[2], -2048.0, ALU.mult, rd=["oh"], wr=["KF"], n=1)
    ts(oh[26], oh[2], 1.0 / 64, ALU.mult, rd=["oh"], wr=["KF"], n=1)
    ts(oh[27], oh[5], 1.0 / 1024, ALU.mult, rd=["oh"], wr=["KF"], n=1)
    ts(T.crs[:], T.i16[:], oh[6], ALU.mult, oh[16], ALU.add, rd=["i16", "oh", "oh1"], wr=["crs"])
    tt(T.mrs[:], T.crs[:], T.i16[:], ALU.mult, ["crs", "i16"], ["mrs"], 512)
    ts(T.tg[:], T.mrs[:], oh[19], ALU.add, rd=["mrs", "oh1"], wr=["tg"])
    tt(T.SG[:], T.tg[:], T.Sel[:], ALU.mult, ["tg", "Sel"], ["SG"], 512)
    ts(T.cn[:, 0:128], T.i16[:, 0:128], 0.0, ALU.is_equal, oh[5], ALU.mult, rd=["i16", "oh"], wr=["cn"], n=128)
    tt(T.WR[:, 0:128], T.cn[:, 0:128], T.Sel[:, 0:128], ALU.mult, ["cn", "Sel"], ["K"])
    act(T.KW[:, 0:128], T.SG[:, 0:128], ACT.Identity, 0.0, oh[22], rd=["SG", "KF"], wr=["KW0"], n=128)
    act(T.KW[:, 128:256], T.Sel[:, 0:128], ACT.Identity, 0.0, oh[24], rd=["Sel", "KF"], wr=["KW1"], n=128)
    act(T.LP[:], T.SG[:], ACT.Identity, 0.0, oh[23], rd=["SG", "KF"], wr=["KB"])
    act(T.WC[:], T.Sel[:], ACT.Identity, 0.0, oh[25], rd=["Sel", "KF"], wr=["KB"])
    act(T.WQ[:, 0:128], T.Sel[:, 0:128], ACT.Identity, 0.0, oh[26], rd=["Sel", "KF"], wr=["KB"], n=128)
    act(T.WQ[:, 128:256], T.Sel[:, 0:128], ACT.Identity, 0.0, oh[27], rd=["Sel", "KF"], wr=["KB"], n=128)
    tt(T.KN[:, 0:128], T.KW[:, 0:128], T.KW[:, 128:256], ALU.add, ["KW0", "KW1"], ["KN0"])
    ts(T.KN[:, 128:256], T.KN[:, 0:128], -1.0, ALU.mult, rd=["KN0"], wr=["K"], n=64)
    KP, WD, KD, KN = T.KW[0:NF, 0:128], T.KW[0:NF, 128:256], T.KN[0:NF, 0:128], T.KN[0:NF, 128:256]
    WQ, WB, WR, FL = T.WQ[0:NF, 0:128], T.WQ[0:NF, 128:256], T.WR[0:NF, 0:128], T.FL[0:NF, :]
    ts(T.col[:, 7:8], T.col[:, 0:1], 1.0, ALU.mult, rd=["colp", "rm", "od", "dm", "zw32", "i16", "c496", "K"], wr=["K"], n=1)
    K1 = ["iw", "KA", "KG", "c496"]
    K = ["K", "KA", "KB", "KG"]

    dma("S", T.zf[32:128, 0, :], T.lnb[0:3, :, 320:384], ["lnb", "lnb1"], ["zfa"], 48)
    dma("S", T.zf[0:32, 0, :], T.lnb[3, :, 320:384], ["lnb", "lnb1"], ["zf0"], 16)
    for n, (a, b) in enumerate(((0, me), (me + 1, N))):
        if b > a:
            dma("S", X[32 * a:32 * b, XO:XO + XH], T.lnb[a:b, :, 0:320], ["lnb"], ["Xin%d" % n], 160)
    dma("S", T.z[:, 0, :], T.lnb[:, :, 320:384], ["lnb", "lnb1"], ["z0"], 64)
    dma("S", T.pli[:], T.lni[:, :, 0:128], ["lni", "lni0"], ["pli"], 256)
    dma("S", T.bl[32:128, 0:16], T.lni[0:3, :, 128:132], ["lni", "lni2"], ["bl0"], 16)
    dma("S", T.bl[0:32, 0:16], T.lni[3, :, 128:132], ["lni", "lni2"], ["bl1"], 16)
    for n, (a, b) in enumerate(((0, me), (me + 1, N))):
        if b > a:
            dma("S", X[32 * a:32 * b, XO + XH:XO + W0], T.lnc[a:b], ["lnc"], ["Xin%d" % (2 + n)], 160)

    ts(T.Lu[:, 0, :], T.pli[:, 0:A:2], 256.0, ALU.add, rd=["pli"], wr=["Lu0"])
    ts(T.Cf[:], T.pli[:], 256.0, ALU.add, rd=["pli"], wr=["Cf"], n=512)
    cp(T.bu[:], T.bl[:, 0:16], ["bl0", "bl1"], ["bu"], 16)
    cp(T.Mu[:], T.Cf[:].indirect(T.bu[:]), ["Cf", "bu"], ["Mu"], G256)

    def repeat(j, par, a, b, keys):
        op("G", lambda q: q.affine_select(T.zrep[:, 16 * a + j:16 * b:16], T.zf[:, par, a:b], [[0, b - a]], ALU.is_ge, 0.0, 0, 0),
           ["zf%d" % par, "zfa"], keys, 2 * (b - a))

    for j in range(NP):
        repeat(j, 0, 0, 256, ["zrep0", "zrep1"])
    exchange(3 + NCH, T.stn, T.lnn, ["stn"], ["lnn"], 32)
    iota(T.d0[:, 0:1024], [[0, 1024]], -1, 0, ["d00", "d01"])
    iota(T.d0[:, 1024:1280], [[0, 256]], -32, 0, ["d0l"])
    iota(T.d0[:, 0:1024:512], [[0, 2]], 2 ** 23, 0, ["d00", "d01"])
    iota(T.d0[:, 1024:1280:16], [[0, 16]], 2 ** 23, 0, ["d0l"])
    for j in range(16):
        iota(T.wrow[:, j:j + 1], [[0, 1]], WT[j], 0, ["wrow"])
    for n, (a, b) in enumerate(((0, me), (me + 1, N))):
        if b > a:
            dma("S", T.Nb[32 * a:32 * b, :], T.lnn[a:b], ["lnn"], ["Nbi%d" % n], 64)
    for j in range(NP, 16):
        cp(T.zrep[:, j:4096:16], T.zf[:, 0, :], ["zf0", "zfa"], ["zrepV0", "zrepV1"], 128)
    mm(bk[7][:, lo], I, T.z[:, 0, :], True, True, ["z0", "iw"], "b7")
    act(T.col[:, 10:11], T.col[:, 0:1], ACT.Copy, rd=["Nbo", "Nbi0", "Nbi1", "colp"], wr=["Nb"], n=1)
    tt(T.wrow[:, 0:16], T.wrow[:, 0:16], T.dm[:, 0:16], ALU.mult, ["wrow", "dm"], ["wrow2"], 32)
    op("V", lambda q: q.tensor_reduce(T.col[:, 9:10], T.wrow[:, 0:16], AxisListType.X, ALU.add), ["wrow2"], ["col9"], 16)
    act(T.bow[:], T.zw[:], ACT.Identity, 0.0, T.col[:, 9:10], rd=["col9", "zw"], wr=["bow"])
    ts(T.bc[:], T.bl[:, 0:16], -256.0, ALU.add, rd=["bl0", "bl1"], wr=["bc"], n=16)
    ts(T.Lu[:, 1, :], T.pli[:, 1:A:2], 256.0, ALU.add, rd=["pli"], wr=["Lu1"])
    tt(T.nbs[:], T.bc[:].indirect(T.ex[:, 0:16]), T.dm[:], ALU.mult, ["bc", "dm", "K"], ["nbs"], G256)

    for t in range(R):
        s, par = t % 2, t % 2
        d = 2 * (1 + s)
        dn = 2 * (1 + (1 - s))
        zk, z = "z%d" % par, T.z[:, par, :]
        wt = XO + W0 + P * t
        win = X[:, 0:wt]
        XK = ["X", "Xnew", "Xown", "Xin0", "Xin1", "Xin2", "Xin3"]
        gens = [u for u in (t - 2, t - 4) if u >= 0]

        def ycol(h, k):
            return T.y[:, 2048 * h + k:2048 * h + 2048:16]

        def myk(h, k, n=1):
            return T.my[:, 2048 * h + 128 * k:2048 * h + 128 * (k + n)]

        def home(h):
            act(T.y[:, 2048 * h:2048 * h + 2048], win.indirect(T.Lu[:, s, H[h]]), ACT.Copy, rd=XK + ["Lu%d" % s], wr=["y%d" % h], n=8 * G256)

        def far(h):
            tt(T.mh[:, 2048 * h:2048 * h + 2048], win.indirect(T.Mu[:, H[h]]), T.zrep[:, 2048 * h:2048 * h + 2048], ALU.min,
               XK + ["Mu", "zrep%d" % h, "zrepV%d" % h, "zrepA%d" % h], ["mh%d" % h], 8 * G256)

        def relus(h):
            for n, k0 in enumerate(range(16 - KRS[t][h], 16, 4)):
                b, w = 4 + n % 2, min(4, 16 - k0)
                for j in range(w):
                    o = bk[b][:, 128 * j:128 * j + 128]
                    mm(o, I, T.z[:, par, H[h]], True, False, [zk] + K1, "b%d" % b, 128)
                    mm(o, In, ycol(h, k0 + j), False, True, ["y%d" % h] + K1, "b%d" % b, 128)
                act(myk(h, k0, w), bk[b][:, 0:128 * w], ACT.Relu, wr=["b%d" % b, "myr%d%d" % (h, n)], n=128 * w)

        def mins(h):
            for k in range(16 - KRS[t][h]):
                tt(myk(h, k), bk[7][:, H[h]], ycol(h, k), ALU.min, ["y%d" % h], ["b7", "mym%d" % h], 128)

        def sums(h):
            kr, a = KRS[t][h], 128 * h
            mm(bk[6][:, H[h]], T.ones[0:2, 0:128], T.ones[0:2, 128:256], True, False, K1, "b6", 128)
            for k in range(16 - kr, 16 if kr < 16 else 0):
                mm(bk[6][:, a + k:a + 128:16], T.z[:, par, H[h]], T.bop[:, 128:256:16], False, False, [zk] + K1, "b6", 8)
            for k in range(16):
                w, key = (T.bon, "myr%d%d" % (h, (k - 16 + kr) // 4)) if k >= 16 - kr else (T.bop, "mym%d" % h)
                mm(bk[6][:, a + k:a + 128:16], myk(h, k), w[:, 128:256:16], False, k == 15, [key] + K1, "b6", 8)
            act(T.Gs[:, H[h]], bk[6][:, H[h]], ACT.Identity, -29.0, wr=["b6", "Gs%d" % h], n=128)
            act(T.Gs[:, a:a + 128:16], bk[6][:, a:a + 128:16], ACT.Identity, 2.0 ** 23, rd=["Gs%d" % h], wr=["b6", "Gs%d" % h], n=8)
            tt(T.d0[:, 4 * a + 4:4 * a + 512:4], T.Gs[:, a + 1:a + 128], bk[6][:, a:a + 127], ALU.subtract, ["Gs%d" % h], ["b6", "d0%d" % h], 128)

        def names(h):
            act(T.NM[:], T.Nb[:].indirect(T.bu[:]), ACT.Copy, rd=["Nb", "bu"], wr=["NM"], n=G256)

        def pairs(h):
            for b in range(4):
                c = 2048 * h + 512 * b
                mm(bk[b][:], T.NM[:, H[h]], T.selm[:, 2048 * s + 512 * b:2048 * s + 512 * b + 512], True, False, ["NM", "selm%d" % s], "b%d" % b, 512)
                mm(bk[b][:], T.Nb[:, 256 * h + s:256 * h + 256:2], T.nil[:], False, False, ["Nb", "KA"], "b%d" % b, 512)
                for j in range(4):
                    mm(bk[b][:, j:512:4], T.mh[:, 2048 * h + 4 * b + j:2048 * h + 2048:16], sh(T.bon, -d), False, j == 3, ["mh%d" % h] + K1, "b%d" % b, 128)
                act(T.Eb[:, c:c + 512], bk[b][:], ACT.Abs, 512.0 * 1008 + 483 + 4 * b, wr=["b%d" % b, "E%d%d" % (h, b)], n=512)

        def bests(h):
            for b in range(4):
                c = 1024 * b + 512 * h
                scan(T.So[:, c:c + 512], T.d0[:, 512 * h:512 * h + 512], T.Eb[:, 2048 * h + 512 * b:2048 * h + 512 * b + 512], 0.0, ALU.add, ALU.min,
                     ["d0%d" % h, "w3", "E%d%d" % (h, b)], ["So%d%d" % (h, b)], 512)
                if (h, b) == (1, 0):
                    tt(T.So[:, 4352:4368], T.So[:, 4111:4352:16], T.lf[:], ALU.add, ["Sol", "lf"], ["am0"], 32)
                if (h, b) == (1, 2):
                    tt(T.So[:, 4368:4384], T.So[:, 63:1024:64], T.So[:, 1087:2048:64], ALU.min, ["So00", "So01", "So10", "So11"], ["am1"], 32)
                    tt(T.So[:, 4384:4400], T.So[:, 4352:4368], T.So[:, 2111:3072:64], ALU.min, ["am0", "So02", "So12"], ["am2"], 32)

        def least(h):
            scan(T.So[:, 4096:4352], T.d0[:, 1024:1280], bk[6][:, lo], 0.0, ALU.add, ALU.min, ["d0l"], ["b6", "Sol"])
            act(T.lf[:], bk[6][:, 15:256:16], ACT.Identity, -496.0, wr=["b6", "lf"], n=16)

        steps = {"y": home, "h": far, "r": relus, "m": mins, "s": sums, "n": names, "p": pairs, "b": bests, "l": least}
        for w in ORDER[t].split():
            steps[w[0]](int(w[1]))
        aside(act, T.Mf[:], T.Cf[:].indirect(T.bu[:]), ACT.Copy, 0.0, 1.0, ["Cf", "bu"], ["Mf"], G256)
        if t == 0:
            mm(bk[4][:], T.i32[:], T.Cf[:], True, False, ["Cf", "KB"], "b4", 2048)
            mm(bk[4][:], I, T.Nb[:], False, True, ["Nb", "iw"], "b4", 512)
            act(T.CN[:], bk[4][:], ACT.Copy, wr=["b4", "CN"], n=512)
            c0 = 128 - 16 * ((-d) % 8)
            for h in range(2):
                mm(bk[5][:, h:16:2], T.nbs[:, H[h]], T.bo[:, c0:c0 + 128:16], True, True, ["nbs", "bo"], "b5", 8)
            cp(T.PT[:, 80:96], bk[5][:, 0:16], [], ["b5", "PTb"], 16)

        mm(bk[4][:, lo], T.i32[:], T.Cf[:, s:A:2], True, False, ["Cf"] + K, "b4", 1024)
        mm(bk[5][:, lo], T.i32[:], T.Mf[:], True, False, ["Mf"] + K, "b5", 1024)
        mm(bk[0][:, lo], In, T.od[:], True, False, K, "b0")
        mm(bk[1][:, lo], In, T.od8[:], True, False, K, "b1")
        mm(bk[2][:, hi], In, T.od[:], True, False, K, "b2")
        tt(T.So[:, 4400:4416], T.So[:, 4368:4384], T.So[:, 4384:4400], ALU.min, ["am1", "am2"], ["am3"], 32)
        for h in range(2):
            tt(T.bi[:, h:16:2], T.So[:, 4400 + 8 * h:4408 + 8 * h], T.So[:, 3135 + 512 * h:3584 + 512 * h:64], ALU.min, ["am3", "So%d3" % h], ["bi"], 16)
        ts(T.it[:, 0:16], T.bi[:], 5, ALU.arith_shift_right, 15, ALU.bitwise_and, rd=["bi"], wr=["ki"], n=16)
        ts(T.it[:, 16:32], T.bi[:], 31, ALU.bitwise_and, rd=["bi"], wr=["li"], n=16)
        ts(T.it[:, 32:48], T.bi[:], 16, ALU.bitwise_and, rd=["bi"], wr=["ni"], n=16)
        tt(T.PT[:, 48:80], T.it[:, 0:32], T.it[:, 0:32], ALU.mult, ["ki", "li"], ["PTs"], 64)
        cp(T.PT[:, 0:48], T.it[:], ["ki", "li", "ni"], ["PTk"], 48)
        if NEK:
            tt(T.tg[:], T.it[:, 0:16].indirect(T.ex[:, 16:32]), T.i16[:], ALU.not_equal, ["ki"] + K, ["tg"], G256)
        for h in range(2):
            mm(bk[7][0:NF, 256 + 128 * h:384 + 128 * h], T.PT[:, h:112:2], I, True, True, ["PTs", "PTk", "PTb", "PT1", "iw"], "b7", 128)
        if NEK:
            act(FL, bk[7][0:NF, hi], ACT.Copy, wr=["b7", "FL"])
        else:
            cp(FL, bk[7][0:NF, hi], [], ["b7", "FL"])

        def flags(bank, half, w, st=False, sp=False):
            mm(bk[bank][:, half], w, FL, st, sp, ["FL", "KW0", "KW1", "KN0"] + K, "b%d" % bank)

        if NEK:
            for h in range(2):
                mm(bk[4][:, H[h]], T.tg[:, H[h]], I8, False, h == 1, ["tg"] + K, "b4", 128)
        else:
            flags(4, lo, KP, sp=True)
        ts(T.pc[:], bk[4][:, lo], -MID, ALU.add, -LOW, ALU.max, wr=["b4", "pc"])
        flags(5, lo, sh(T.LP, d, NF), sp=True)
        ts(T.pm[:], bk[5][:, lo], -MID, ALU.add, -LOW, ALU.max, wr=["b5", "pm"])
        if not gens:
            aside(act, T.Ls[:, s, :], T.CN[:, s:A:2], ACT.Copy, 0.0, 1.0, ["CN"], ["Ls%d" % s])
        flags(0, lo, WQ)
        mm(bk[0][:, lo], T.bo16[:], T.pc[:], False, True, ["pc"] + K, "b0")
        mm(bk[3][:, lo], T.bo16[:], T.pc[:], True, True, ["pc"] + K, "b3")
        flags(1, lo, sh(T.WC, d, NF))
        mm(bk[1][:, lo], T.bo16[:], T.pm[:], False, False, ["pm"] + K, "b1")
        mm(bk[4][:, lo], T.bo16[:], T.pm[:], True, True, ["pm"] + K, "b4")
        mm(bk[2][:, hi], T.bo16[:], T.pc[:], False, False, ["pc"] + K, "b2")
        scan(T.scl[:], T.rm[:], bk[0][:, lo], 131072.0, ALU.min, ALU.max, K, ["b0", "scl"])
        ts(T.cu[:], T.scl[:, 15:256:16], OFF, ALU.add, rd=["scl"], wr=["cu"], n=16)
        act(T.yk[:], win.indirect(T.cu[:]), ACT.Copy, rd=XK + ["cu"], wr=["yk"], n=G256)

        def equal_rows(n, bank, lst, b, c0, w, beside):
            bn, na, e0, a0 = "b%d" % bank, NA[n], 16 * n, 1024 * n
            rep = (T.crs, T.mrs)[n]
            if FAST:
                ts(T.r16[:, n, :], bk[bank][:, lo], OFF, ALU.add, wr=[bn, "r16%d" % n])
            else:
                act(rep[:], bk[bank][:, lo], ACT.Copy, wr=[bn, ("crs", "mrs")[n]])
            tt(T.eq[:, e0 + 15, :], bk[bank][:, lo], T[lst][:], ALU.is_equal, [lst], [bn, "eq%d" % (e0 + 15)])
            rows, o = [(0, T.eq[:, e0 + 15, :], "eq%d" % (e0 + 15))], a0
            for j in range(15 - na):
                c = 16 * j + 16
                if FAST:
                    ts(T.eq[:, e0 + j, c:256], T.r16[:, n, c:256], -OFF, ALU.add, T[lst][:, c - 1:c], ALU.is_equal, rd=[lst, "r16%d" % n],
                       wr=["eq%d" % (e0 + j)], n=(256 - c) / 2)
                else:
                    ts(T.eq[:, e0 + j, c:256], rep[:, c:256], T[lst][:, c - 1:c], ALU.is_equal, rd=[lst, ("crs", "mrs")[n]], wr=["eq%d" % (e0 + j)], n=256 - c)
                rows.append((c, T.eq[:, e0 + j, c:256], "eq%d" % (e0 + j)))
            for j in range(15 - na, 15):
                c = 16 * j + 16
                act(T.ad[:, o:o + 256 - c], bk[bank][:, c:256], ACT.Abs, T[lst][:, c - 1:c], -1.0, rd=[lst], wr=[bn, "ad"], n=256 - c)
                rows.insert(len(rows) - 2, (c, T.eqa[:, o:o + 256 - c], "eqa%d" % n))
                o += 256 - c
            if na:
                act(T.eqa[:, a0:o], T.ad[:, a0:o], ACT.Relu, 1.0, -4.0, rd=["ad"], wr=["eqa%d" % n], n=o - a0)
            for fn in beside:
                fn()
            for x, (c, src, key) in enumerate(rows):
                mm(bk[b][:, c0 + c:c0 + 256], w, src, False, x == 15, [key] + K, "b%d" % b, 256 - c)

        zn, znk = T.z[:, 1 - par, :], "z%d" % (1 - par)
        if t < R - 1:
            mm(bk[7][:, hi], sh(T.iw, dn), z, True, False, [zk] + K, "b7")
            mm(bk[7][:, hi], sh(T.inw, dn), T.yk[:], False, True, ["yk"] + K, "b7")
            act(T.zf[:, 1 - par, :], bk[7][:, hi], ACT.Abs, wr=["b7", "zf%d" % (1 - par)])
            for j in range(16 - ZA[t]):
                if j < ZW[t]:
                    repeat(j, 1 - par, 0, 256, ["zrep0", "zrep1"])
                else:
                    repeat(j, 1 - par, 0, 128, ["zrep0"])
            for j in range(ZW[t], 16 - ZA[t]):
                repeat(j, 1 - par, 128, 256, ["zrep1"])
            for j in range(16 - ZA[t], 16):
                aside(act, T.zrep[:, j:4096:16], T.zf[:, 1 - par, :], ACT.Copy, 0.0, 1.0, ["zf%d" % (1 - par)], ["zrepA0", "zrepA1"])

        def rests():
            mm(bk[6][:, lo], I, z, True, False, [zk] + K, "b6")
            mm(bk[6][:, lo], In, T.yk[:], False, True, ["yk"] + K, "b6")
            if t < R - 1:
                act(zn, bk[6][:, lo], ACT.Abs, wr=["b6", znk])
            if HA:
                act(T.ya[:], bk[6][:, lo], ACT.Relu, 0.0, -1.0, wr=["b6", "ya"])

        def payees():
            c2 = 128 - 16 * (dn % 8)
            for il in range(16):
                mm(bk[6][:, 0:16], T.bow[:, 16 - il + c2:144 - il + c2], T.z[:, 1 - par, il:256:16], il == 0, il == 15, [znk, "bow"], "b6", 16)
            for h in range(2):
                mm(bk[6][:, 16 + h:32:2], T.z[:, 1 - par, H[h]], T.bow[:, 16:144:16], True, True, [znk, "bow"], "b6", 8)
            mm(bk[7][:, lo], I, zn, True, True, [znk] + K, "b7")
            cp(T.t3[:], bk[6][:, 0:32], [], ["b6", "t3"], 32)
            ts(T.bl[:], T.t3[:], 511, ALU.bitwise_and, rd=["t3"], wr=["bl0", "bl1"], n=32)
            cp(T.bu[:], T.bl[:, 0:16], ["bl0"], ["bu"], 16)
            ts(T.PT[:, 80:96], T.bl[:, 16:32], -256.0, ALU.add, rd=["bl0"], wr=["PTb"], n=16)

        def closings():
            thr = XO + W0 - 0.5 - OFF
            act(T.sgb[:], bk[3][:, lo], ACT.Sign, thr + P * gens[0] * (len(gens) - 1), -1.0, wr=["b3", "sgb"])
            if len(gens) > 1:
                act(T.sga[:], bk[3][:, lo], ACT.Sign, -thr, 1.0, wr=["b3", "sga"])
            for n in range(len(gens)):
                b = (3, 5)[n]
                mm(bk[b][:, hi], I, T.yk[:], True, False, ["yk"] + K, "b%d" % b)
                flags(b, hi, WD)
                if n == 0:
                    mm(bk[b][:, hi], I8, T.sgb[:], False, True, ["sgb"] + K, "b%d" % b)
                else:
                    mm(bk[b][:, hi], I4, T.sgb[:], False, False, ["sgb"] + K, "b%d" % b)
                    mm(bk[b][:, hi], I4, T.sga[:], False, True, ["sga"] + K, "b%d" % b)
                act(T.wh[:, n, :], bk[b][:, hi], ACT.Relu, -BIG, wr=["b%d" % b, "wh%d" % n])

        def gifts():
            for n in range(len(gens)):
                b = (3, 5)[n]
                mm(bk[b][:, hi], sh(T.iw, d), T.wh[:, n, :], True, True, ["wh%d" % n] + K, "b%d" % b)
                act(T.uh[:, n, :], T.wh[:, n, :], ACT.Identity, 63.0, -1.0, rd=["wh%d" % n], wr=["uh%d" % n])
                act(T.wf[:, n, :], bk[b][:, hi], ACT.Copy, wr=["b%d" % b, "wf%d" % n])
                act(T.uf[:, n, :], bk[b][:, hi], ACT.Identity, 63.0, -1.0, wr=["b%d" % b, "uf%d" % n])

        def amounts():
            mm(bk[0][:, hi], I, T.yk[:], True, False, ["yk"] + K, "b0")
            if HA:
                mm(bk[0][:, hi], In, T.ya[:], False, False, ["ya"] + K, "b0")
            mm(bk[0][:, hi], sh(T.inw, -d), T.hm[:], False, True, ["hm"] + K, "b0")
            if HA:
                act(T.vf[:], bk[0][:, hi], ACT.Relu, wr=["b0", "vf"])
                mm(bk[0][:, hi], I, T.ya[:], True, False, ["ya"] + K, "b0")
                mm(bk[0][:, hi], I, T.vf[:], False, True, ["vf"] + K, "b0")
            act(T.cn[:], bk[0][:, hi], ACT.Relu, wr=["b0", "cn"])
            for n, u in enumerate(gens):
                b = (6, 7)[n]
                blk = X[:, XO + W0 + P * u:XO + W0 + P * u + P]
                mm(bk[b][:, hi], I, blk, True, False, XK + K, "b%d" % b)
                mm(bk[b][:, hi], In, T.wh[:, n, :], False, True, ["wh%d" % n] + K, "b%d" % b)
                act(blk, bk[b][:, hi], ACT.Copy, wr=["b%d" % b, "X"])
            mm(bk[0][:, lo], sh(T.iw, d), T.yk[:], True, False, ["yk"] + K, "b0")
            mm(bk[0][:, lo], sh(T.inw, d), T.cn[:], False, True, ["cn"] + K, "b0")
            act(T.vf[:], bk[0][:, lo], ACT.Copy, wr=["b0", "vf"])
            act(T.nvf[:], bk[0][:, lo], ACT.Identity, 0.0, -1.0, wr=["b0", "nvf"])

        equal_rows(0, 3, "scl", 1, 0, sh(T.bo8, d), [rests] * (HA or t < R - 1) + [closings] * (t > 1))
        scan(T.sm2[:], T.rm[:], bk[1][:, lo], 131072.0, ALU.min, ALU.max, K, ["b1", "sm2"])
        act(T.tg[:], bk[1][:, lo], ACT.Sign, 32768.5 + OFF, wr=["b1", "tg"])
        mm(bk[2][:, hi], sh(T.bop, -d), T.tg[:], False, False, ["tg"] + K, "b2")
        ts(T.mu[:], T.sm2[:, 15:256:16], OFF, ALU.add, rd=["sm2"], wr=["mu"], n=16)
        if HA:
            act(T.hm[:], win.indirect(T.mu[:]), ACT.Copy, rd=XK + ["mu"], wr=["hm"], n=G256)
        else:
            tt(T.hm[:], win.indirect(T.mu[:]), T.zf[:, par, :], ALU.min, XK + ["mu", "zf%d" % par, "zfa"], ["hm"], G256)
        cn = T.CN[:, s:A:2]
        src, key = (T.Us, "Us%d" % s) if len(gens) == 2 else (T.Ls, "Ls%d" % s)

        def reopened():
            if t in ASIDE:
                flags(5, lo, KD, st=True)
                mm(bk[5][:, lo], T.i32[:], cn, False, False, ["CN"] + K, "b5", 1024)
                mm(bk[5][:, lo], T.in32[:], src[:, s, :], False, True, [key] + K, "b5", 1024)
                act(T.mrs[:], bk[5][:, lo], ACT.Relu, wr=["b5", "mrs"])
            else:
                flags(5, lo, KN, st=True)
                mm(bk[5][:, lo], T.i32[:], src[:, s, :], False, True, [key] + K, "b5", 1024)
                tt(cn, bk[5][:, lo], cn, ALU.min, ["CN"], ["b5", "CN"])
            if len(gens) == 1:
                mm(bk[7][:, hi], T.i32[:], cn, True, False, ["CN"] + K, "b7", 1024)

        def offered():
            flags(0, hi, KP, st=True)
            mm(bk[0][:, hi], I, T.i256[:], False, False, K, "b0")
            mm(bk[0][:, hi], T.ones[0:11 + t, 0:128], T.c256[0:11 + t, :], False, False, K, "b0")
            flags(0, hi, WB)

        equal_rows(1, 4, "sm2", 2, 256, sh(T.bo8, -d), [payees] * (t < R - 1) + [amounts] + [reopened] * (t > 1))
        offered()
        aside(gifts)
        aside(mm, bk[1][:, lo], In, T.od[:], True, False, K, "b1")
        aside(mm, bk[1][:, lo], T.bo16[:], T.pm[:], False, False, ["pm"] + K, "b1")
        scan(T.scl[:], T.rm[:], bk[2][:, hi], 131072.0, ALU.min, ALU.max, K, ["b2", "scl"])
        act(T.nbs[:], bk[2][:, hi], ACT.Relu, -32768.0 - OFF, -1.0, wr=["b2", "nbs"])
        NB = T.bon[:, 128:256]
        if t not in ASIDE:
            mm(bk[0][:, hi], NB, T.nbs[:], False, True, ["nbs"] + K, "b0")
            tt(cn, bk[0][:, hi], cn, ALU.max, ["CN"], ["b0", "CN"])
            ts(T.Cf[:, s:A:2], cn, MAGIC, ALU.add, -MAGIC, ALU.add, rd=["CN"], wr=["Cf"])
        ts(T.cs[:, t, :], T.scl[:, 15:256:16], OFF, ALU.add, rd=["scl"], wr=["cs%d" % t], n=16)
        mm(bk[1][:, lo], sh(T.bon, d), T.nbs[:], False, True, ["nbs"] + K, "b1")

        def supports():
            flags(7, hi, KP)
            mm(bk[7][:, hi], NB, T.nbs[:], False, True, ["nbs"] + K, "b7")
            tt(T.Us[:, s, :], bk[7][:, hi], T.Ls[:, s, :], ALU.max, ["Ls%d" % s], ["b7", "Us%d" % s])

        def built():
            mm(bk[4][:, hi], I, T.yk[:], True, False, ["yk"] + K, "b4")
            mm(bk[4][:, hi], In, T.cn[:], False, False, ["cn"] + K, "b4")
            mm(bk[4][:, hi], NB, T.nbs[:], False, True, ["nbs"] + K, "b4")
            act(X[:, wt:wt + P], bk[4][:, hi], ACT.Relu, wr=["b4", "Xnew"])

        def record():
            c1 = 128 - 16 * ((-d) % 8)
            flags(3, lo, WR, st=True)
            mm(bk[3][:, lo], T.zw16[:, 15:143], T.pc[:], False, False, ["pc"] + K, "b3")
            mm(bk[3][:, lo], T.zw16[:, 14 + c1:142 + c1], T.pm[:], False, False, ["pm"] + K, "b3")
            mm(bk[3][:, lo], NB, T.nbs[:], False, True, ["nbs"] + K, "b3")
            act(T.recb[:, P * t:P * t + P], bk[3][:, lo], ACT.Relu, T.col[:, 6:7], rd=K, wr=["b3", "recb"])

        def moves():
            cp(win.indirect(T.cs[:, t, :]), T.cn[:], ["X", "cs%d" % t, "cn"], ["X"], S256)
            scan(T.sml[:], T.rm[:], bk[1][:, lo], 131072.0, ALU.min, ALU.max, K, ["b1", "sml"])
            ts(T.ms[:, t, :], T.sml[:, 15:256:16], OFF, ALU.add, rd=["sml"], wr=["ms%d" % t], n=16)
            tt(T.tg[:], win.indirect(T.ms[:, t, :]), T.vf[:], ALU.max, ["X", "ms%d" % t, "vf"], ["tg"], G256)
            tt(win.indirect(T.ms[:, t, :]), T.tg[:], T.nvf[:], ALU.add, ["X", "tg", "nvf"], ["X"], S256)
            for n, u in enumerate(gens):
                old = X[:, 0:XO + W0 + P * u]
                for lst, w_, u_ in ((T.cs, "wh", "uh"), (T.ms, "wf", "uf")):
                    tt(T.tg[:], old.indirect(lst[:, u, :]), T[u_][:, n, :], ALU.min, ["X", "%s%d" % (u_, n)], ["tg"], G256)
                    tt(old.indirect(lst[:, u, :]), T.tg[:], T[w_][:, n, :], ALU.add, ["X", "tg", "%s%d" % (w_, n)], ["X", "XA%d" % n], S256)

        if t in ASIDE:
            moves()
        if len(gens) == 1:
            aside(supports)
        if t in ASIDE:
            mm(bk[0][:, hi], T.in32[:], cn, False, False, ["CN"] + K, "b0", 1024)
            mm(bk[6][:, hi], T.i32[:], cn, True, False, ["CN"] + K, "b6", 1024)
            if gens:
                mm(bk[6][:, hi], T.in32[:], T.mrs[:], False, False, ["mrs"] + K, "b6", 1024)
            mm(bk[0][:, hi], NB, T.nbs[:], False, True, ["nbs"] + K, "b0")
            act(T.crs[:], bk[0][:, hi], ACT.Relu, wr=["b0", "crs"])
            mm(bk[6][:, hi], T.i32[:], T.crs[:], False, True, ["crs"] + K, "b6", 1024)
            act(T.mrs[:], bk[6][:, hi], ACT.Identity, MAGIC, wr=["b6", "mrs"])
            if t < R - 1:
                act(cn, bk[6][:, hi], ACT.Copy, wr=["b6", "CN"])
                act(T.Cf[:, s:A:2], T.mrs[:], ACT.Identity, -MAGIC, rd=["mrs"], wr=["Cf"])
            else:
                act(cn, T.mrs[:], ACT.Identity, -MAGIC - 256, rd=["mrs"], wr=["CN"])
                act(T.CN[:, 1 - s:A:2], T.Cf[:, 1 - s:A:2], ACT.Identity, -256.0, rd=["Cf"], wr=["CN"])
        if t < R - 1:
            mm(bk[2][:, hi], T.i32[:], cn, True, False, ["CN"] + K, "b2", 1024)
            mm(bk[2][:, hi], T.in32[:], T.Cf[:, s:A:2], False, True, ["Cf"] + K, "b2", 1024)
            act(T.Nb[:, s:A:2], bk[2][:, hi], ACT.Copy, wr=["b2", "Nb"])
            aside(cp, T.Mu[:], T.Cf[:].indirect(T.bu[:]), ["Cf", "bu"], ["Mu"], G256)
            if t < R - 2:
                aside(cp, T.Lu[:, s, :], T.Cf[:, s:A:2], ["Cf"], ["Lu%d" % s])
        if t not in ASIDE:
            moves()
        aside(built)
        aside(record)

    dma("A", T.stf[:, :, 0:128], T.CN[:], ["CN"], ["stf3"], 256)
    for e in range(3):
        dma("A", T.stf[:, :, 128 + 24 * e:152 + 24 * e], T.recb[e:128:16, :], ["recb"], ["stf%d" % e], 48)
    SF = ["stf0", "stf1", "stf2", "stf3"]
    dma("A", T.lnf[me], T.stf[me], SF, ["lnfo"], 100)
    for c, (a, b) in enumerate(CH):
        dma("S", T["sto%d" % c][:], X[:, XO + a:XO + b], XK if c else ["XA0", "Xnew"], ["sto%d" % c], 340)
    for c in range(NCH):
        exchange(3 + c, T["sto%d" % c], T["lno%d" % c], ["sto%d" % c], ["lno%d" % c], 88)
        if c == 0:
            exchange(2, T.stf, T.lnf, SF, ["lnf"], 100)
    dma("A", T.xo[r32, :], X[r32, XO:XO + 4096], XK + ["sto1", "sto2"], [], 256)
    for c in range(NCH):
        for a, b in ((0, me), (me + 1, N)):
            if b > a:
                dma("S", T.xo[32 * a:32 * b, CH[c][0]:CH[c][1]], T["lno%d" % c][a:b], ["lno%d" % c], [], 170)
    dma("A", T.co[:], T.lnf[:, :, 0:128], ["lnf", "lnfo"], [], 256)
    for e in range(3):
        dma("A", T.rec[8 * e:8 * e + 8, :], T.lnf[:, :, 128 + 24 * e:152 + 24 * e], ["lnf", "lnfo"], [], 48)
    emit(g, T, ops, lazy)
